import numpy as np, ml_dtypes
CORES = [23,119,17,113]
N = 4
BF = ml_dtypes.bfloat16
W, T, K, R = 4096, 1024, 256, 8
SR, SG = (1,), (0, 1)
def pack(x, ix, q, c):
    return {"rec": np.ascontiguousarray(x.reshape(N, 128, W)).astype(np.float32).astype(BF), "idx": np.ascontiguousarray(ix.reshape(N, 128, T)).astype(np.int32),
            "que": np.ascontiguousarray(q).astype(np.int32), "cur": np.ascontiguousarray(c.reshape(N, 8, 1)).astype(np.int32)}
def setup_inputs(rng):
    x = rng.integers(0, 16, (N, 8, 16, W)); ix = rng.integers(0, W, (N, 8, 16, T))
    q = np.ascontiguousarray(np.argsort(rng.random((N, 8, T)), axis=-1)[..., :K]); q[..., 17::32] = q[..., 2::32]
    return pack(x, ix, q, rng.integers(0, T, (N, 8)))
def regions(rng):
    o = 1 + rng.permutation(W - 2)
    return o[:816], o[816:820], np.concatenate([np.array([0, W - 1]), o[820:1330]]), o[1330:]
def give(rng, x, at, k, v):
    v = np.asarray(v)
    x[k, at] = (v >> 8) + (W >> 8) * rng.integers(0, 4096 // W, v.shape); x[(k + 1) % 16, at] = (v >> 4) & 15; x[(k + 2) % 16, at] = v & 15
def twin(rng, rd, w, bits, on):
    return int(rng.choice(rd[np.isin(rd ^ w, rd) & ((rd & bits) == on)]))
def group(rng, reg, edge):
    ixr, sp, dat, rdp = reg
    x = rng.integers(0, 16, (16, W)); x[:, rdp] = rng.integers(1, 16, (16, len(rdp))); o = rng.permutation(ixr); d0 = rng.permutation(dat)
    c0 = int(rng.choice(np.array([0, T - K, T - K - 1, T - 5, int(rng.integers(0, T))]))); q = (c0 + np.arange(K)) & (T - 1); c = (c0 + K) & (T - 1)
    i, j = c & 511, int(np.argmax(d0 == edge)); d0[[i, j]] = d0[[j, i]]
    give(rng, x, o[:512], 0, d0)
    at = o[512:752].reshape(15, 16); give(rng, x, at, np.arange(1, 16)[:, None], rng.choice(rdp, (15, 16)))
    ix = np.zeros((16, T), np.int64); ix[0] = o[np.arange(T) & 511]; ix[1:] = at[np.arange(15)[:, None], rng.integers(0, 16, (15, T))]
    return x, ix, q, c, d0, o[752:]
def blank():
    return np.zeros((N, 8, 16, W), np.int64), np.zeros((N, 8, 16, T), np.int64), np.zeros((N, 8, K), np.int64), np.zeros((N, 8), np.int64)
def setup_inputs_calm(rng):
    reg = regions(rng); s, s2, s3, e = [int(v) for v in reg[1]]; rd = reg[3]; x, ix, q, c = blank(); m = R + 2
    for r in range(N):
        for g in range(8):
            xa, ia, qa, ca, d0, sp = group(rng, reg, (0, W - 1)[(r + g) & 1]); n = (r + g) % 4
            give(rng, xa, sp[:3], 0, np.array([s, s2, s3])); give(rng, xa, sp[3:18], np.arange(1, 16), np.full(15, e))
            ia[0, qa[0]] = sp[0]; ia[0, qa[3:m + 2]] = sp[0]; ia[0, qa[1]] = sp[1]; ia[0, qa[2]] = sp[2]; ia[1:, qa[1:3]] = sp[3:18][:, None]
            kk = int(rng.integers(1, 16)); give(rng, xa, np.array([s]), kk, np.array([s]))
            vic = qa[m + 2 + rng.permutation(K - m - 2)[:n + 1]]; ia[kk, vic[:n]] = s
            j = int(vic[n]); ed = np.zeros(16, np.int64); k2, k3, k4 = [int(v) for v in 1 + rng.permutation(15)[:3]]; a2, a3 = np.array([s2]), np.array([s3])
            if g == 1:
                w = 2184 & (W - 1); v = twin(rng, rd, w, 0, 0); ed[:] = 8
                give(rng, xa, a2, k2, np.array([v])); give(rng, xa, a3, k3, np.array([v ^ w])); ia[k2, j] = s2; ia[k3, j] = s3
            elif g == 3:
                k2 = int(rng.integers(2, 8)); k3 = 2 * k2 + 1; k4 = 1; ed[k2 + 2] = 8; ed[(k3 + 2) & 15] = 12
                give(rng, xa, a2, k2, np.array([twin(rng, rd, 8, 8, 0)])); give(rng, xa, a3, k3, np.array([twin(rng, rd, 4, 4, 4)])); ia[k2, j] = s2; ia[k3, j] = s3
            elif g == 5:
                ed[(k2 + 1) & 15] = 8; give(rng, xa, a2, k2, np.array([twin(rng, rd, 128, 0, 0)])); ia[k2, j] = s2
            elif g == 7:
                k2 = 2 * int(rng.integers(1, 8)); k3 = k2 + 1; k4 = 1; ed[(k3 + 2) & 15] = 1
                give(rng, xa, a2, k3, np.array([twin(rng, rd, 1, 3, 2)])); give(rng, xa, sp[19:20], k2, np.array([W - 1])); ia[k2, j] = sp[19]; ia[k3, j] = s2
            else:
                ed[(k2 + 3 + int(rng.integers(0, 13))) & 15] = 8; give(rng, xa, a2, k2, rng.choice(rd, 1)); ia[k2, j] = s2
            give(rng, xa, sp[18:19], k4, np.array([s2])); ia[k4, j] = sp[18]; xa[:, e] = ed
            x[r, g] = xa; ix[r, g] = ia; q[r, g] = qa; c[r, g] = ca
    return pack(x, ix, q, c)
def setup_inputs_corners(rng):
    reg = regions(rng); s, s2, e = int(reg[1][0]), int(reg[1][1]), int(reg[1][3]); x, ix, q, c = blank(); par = int(rng.integers(0, 2))
    for r in range(N):
        for g in range(8):
            xa, ia, qa, ca, d0, sp = group(rng, reg, (0, W - 1)[(r + g) & 1]); xa[:, e] = 8
            if r % 2 == par:
                z = s2 if g == 4 else s
                kk = int(rng.integers(1, 16)); give(rng, xa, np.array([z]), kk, rng.choice(reg[3], 1)); was = ia[kk].copy(); ia[kk] = z
                if g == 6: ia[0] = int(ia[0, qa[0]])
                if g % 4 == 1: j = np.array([(ca + K - 1) & (T - 1)])
                elif g % 4 == 2: j = np.array([ca])
                elif g % 4 == 3: j = np.nonzero(rng.random(T) < 0.5)[0]
                else: j = np.zeros(0, np.int64)
                ia[kk, j] = was[j]
            else:
                give(rng, xa, sp[:1], 0, np.array([s])); give(rng, xa, sp[33:48], np.arange(1, 16), np.full(15, e)); give(rng, xa, sp[48:49], 0, np.array([s2]))
                two = qa[1:3] if g % 2 == 0 else qa[R + 34:R + 36]
                if g % 2 == 0:
                    ia[0] = sp[0]
                    if g == 2: qa = np.full(K, qa[0])
                else:
                    ia[0, qa[:R + 2]] = sp[0]; j = qa[R + 2:R + 34]
                    give(rng, xa, sp[1:33], 7, d0[j & 511]); ia[7, j] = sp[1:33]
                if g != 2:
                    ia[0, two] = sp[48]; ia[1:, two] = sp[33:48][:, None]
            x[r, g] = xa; ix[r, g] = ia; q[r, g] = qa; c[r, g] = ca
    return pack(x, ix, q, c)
def setup_inputs_crowd(rng):
    reg = regions(rng); x, ix, q, c = blank(); al = np.arange(T)
    for r in range(N):
        kinds = rng.permutation(8)
        for g in range(8):
            xa, ia, qa, ca, d0, sp = group(rng, reg, (0, W - 1)[(r + g) & 1]); h = int(kinds[g])
            if h == 1:
                give(rng, xa, sp[:1], 15, d0[qa[:1] & 511]); ia[15, qa[K - 1]] = sp[0]
            if h == 2: ia[0] = int(ia[0, ca])
            if h == 3:
                j = int(qa[int(rng.choice(np.array([0, K >> 1, K - 1])))]); was = int(ia[0, j]); ia[0] = int(ia[0, ca]); ia[0, j] = was
            if h == 4: ia[0] = ia[0, (ca + rng.integers(0, 2, T)) & (T - 1)]
            if h == 5: ia[0] = ia[0, (ca + rng.integers(0, 3, T)) & (T - 1)]
            if h == 6:
                give(rng, xa, sp[:15], np.arange(1, 16), np.full(15, d0[qa[0] & 511])); kk = rng.integers(1, 16, T); m = al != qa[0]
                ia[kk[m], al[m]] = sp[kk[m] - 1]
            if h == 7:
                give(rng, xa, sp[:15], np.arange(1, 16), np.full(15, d0[ca & 511])); ia[0] = int(ia[0, ca]); ia[1:] = sp[:15][:, None]
            x[r, g] = xa; ix[r, g] = ia; q[r, g] = qa; c[r, g] = ca
    return pack(x, ix, q, c)
def setup_inputs_ends(rng):
    x = 15 * rng.integers(0, 2, (N, 8, 16, W)); x = np.where(rng.random((N, 8, 1, W)) < 0.5, x[:, :, :1], x)
    fr = rng.random((N, 8, W)) < 0.33; fr[..., 0] = False; fr[..., W - 1] = False
    x = np.where(fr[:, :, None], rng.integers(0, 16, x.shape), x)
    z = 15 * (rng.random((N, 8, 1)) < 0.25).astype(np.int64); x[..., 0] = z; x[..., W - 1] = 15 - z
    d, ix, q, c = blank(); c = (T - 1) * rng.integers(0, 2, (N, 8)); c[:, 0] = 0; c[:, 7] = T - 1
    for r in range(N):
        for g in range(8):
            end = rng.random(T) < 0.65; end[0] = True; end[T - 1] = True
            e = rng.integers(0, 2, (16, T)); e = np.where(rng.random(T) < 0.5, e[:1], e)
            if g % 2 == 0: e[:, 0] = 0
            e[:, T - 1] = rng.integers(0, 2, 16); e[0, T - 1] = 1; e[8, T - 1] = 0; e[15, T - 1] = 1
            ix[r, g] = np.where(end, e * (W - 1), rng.choice(np.nonzero(fr[r, g])[0], (16, T)))
            qa = rng.choice(np.nonzero(~end)[0], K); at = rng.permutation(K)[:2 * K // 3]
            qa[at] = (T - 1) * rng.integers(0, 2, len(at)); qa[K - 1] = T - 1; q[r, g] = qa
    return pack(x, ix, q, c)
def setup_inputs_spread(rng):
    e = rng.choice(np.array([0.5, 1.0, 1.0, 2.0, 3.0]), (N, 8, 1, 1)); i = rng.choice(np.array([1.0, 1.0, 2.0, 3.0]), (N, 8, 1, 1)); j = rng.choice(np.array([1.0, 2.0]), (N, 8, 1))
    x = np.minimum((16 * rng.random((N, 8, 16, W)) ** e).astype(np.int64), 15); ix = np.minimum((W * rng.random((N, 8, 16, T)) ** i).astype(np.int64), W - 1)
    q = np.minimum((T * rng.random((N, 8, K)) ** j).astype(np.int64), T - 1)
    return pack(x, ix, q, rng.integers(0, T, (N, 8)))
def check_inputs(d):
    bad = []
    for k, hi in (("rec", 15), ("idx", W - 1), ("que", T - 1), ("cur", T - 1)):
        v = np.asarray(d[k]).astype(np.float64)
        if not np.all((v >= 0) & (v <= hi)): bad.append("range of " + k)
        elif np.any(v != np.floor(v)): bad.append("whole numbers of " + k)
    return bad
def reference(rec, idx, que, cur):
    x = rec.astype(np.float32).astype(np.int64).reshape(N, 8, 16, W); ix = idx.astype(np.int64).reshape(N, 8, 16, T)
    q = que.astype(np.int64); c = cur.astype(np.int64).reshape(N, 8); kept = np.full((N, 8, 16, K), -1, np.int64); pl = np.arange(K)
    ra = np.arange(N)[:, None, None, None]; ga = np.arange(8)[None, :, None, None]; ka = np.arange(16)[None, None, :, None]
    for t in range(R):
        sr, sg = SR[t % len(SR)], SG[t % len(SG)]
        at = ix[ra, ga, ka, q[:, :, None, :]]
        d = (256 * x[ra, ga, ka, at] + 16 * x[ra, ga, (ka + 1) % 16, at] + x[ra, ga, (ka + 2) % 16, at]) & (W - 1)
        fresh = kept[:, :, 0] < 0; redo = ~fresh & np.any(d != kept, axis=2); sent = ~fresh & ~redo
        lock = np.full((N, 8, W), K, np.int64); np.minimum.at(lock, (ra[..., 0], ga[..., 0], d[:, :, 0]), np.where(sent, pl, K))
        low = np.min(np.take_along_axis(lock, d.reshape(N, 8, 16 * K), 2).reshape(N, 8, 16, K), axis=2)
        go = sent & (low >= pl)
        rr, gg, ii = np.nonzero(go); nm = d[rr, gg, :, ii]; ro, go_ = (rr + sr) % N, (gg + sg) % 8
        v = x[ro[:, None], go_[:, None], :, nm]
        x[ro, go_, :, nm[:, 0]] = (v[:, 0] + np.max(v[:, 1:], axis=1)) & 15
        o = np.argsort(np.where(go, 2, np.where(redo, 1, 0)), axis=2, kind="stable"); n = np.sum(go, axis=2)[..., None]
        tail = pl >= K - n
        q = np.where(tail, (c[..., None] + pl - (K - n)) & (T - 1), np.take_along_axis(q, o, 2))
        kept = np.where(tail[:, :, None], -1, np.take_along_axis(d, o[:, :, None, :], 3)); c = (c + n[..., 0]) & (T - 1)
    return {"yx": x.reshape(N, 128, W).astype(np.float32).astype(BF), "yq": q.astype(np.float32), "yd": kept.reshape(N, 128, K).astype(np.float32)}

@@ -1,0 +1,519 @@
+from concourse.mybir import AluOpType as ALU, ActivationFunctionType as ACT
+
+W = 16384.0
+NR = 7
+LOW = 32
+
+SCRATCH = {
+    "xs": ("sbuf", [128, 4096 + 256], "bfloat16"),
+    "ixi": ("sbuf", [128, 1024], "int32"),
+    "qi": ("sbuf", [128, 272], "int32"),
+    "qf": ("sbuf", [128, 272], "float32"),
+    "wa0": ("sbuf", [128, 1536], "float32"), "wa1": ("sbuf", [128, 1536], "float32"),
+    "wq0": ("sbuf", [128, 1536], "float32"), "wq1": ("sbuf", [128, 1536], "float32"),
+    "ws": ("sbuf", [128, 1536], "float32"),
+    "lt": ("sbuf", [128, LOW + 4096 + 256], "float32"),
+    "g1": ("sbuf", [128, 4096], "bfloat16"), "g2": ("sbuf", [128, 4096], "bfloat16"),
+    "lg": ("sbuf", [128, 4096], "bfloat16"), "mx": ("sbuf", [128, 4096], "bfloat16"),
+    "d1": ("sbuf", [128, 4096], "bfloat16"),
+    "wn": ("sbuf", [128, 2048], "bfloat16"),
+    "at": ("sbuf", [128, 256], "uint16"),
+    "su": ("sbuf", [128, 2048], "uint16"), "sin": ("sbuf", [128, 2048], "uint16"),
+    "osn": ("sbuf", [128, 128], "uint16"), "oin": ("sbuf", [128, 128], "uint16"),
+    "s32": ("sbuf", [128, 272], "float32"),
+    "df": ("sbuf", [128, 256], "bfloat16"), "ne": ("sbuf", [128, 256], "bfloat16"),
+    "wv": ("sbuf", [128, 256], "bfloat16"),
+    "hh": ("sbuf", [128, 272], "float32"),
+    "m1": ("sbuf", [128, 256], "float32"), "m3": ("sbuf", [128, 256], "float32"), "m4": ("sbuf", [128, 256], "float32"),
+    "mo": ("sbuf", [128, 256], "float32"), "orow": ("sbuf", [128, 256], "float32"),
+    "lo": ("sbuf", [128, 32], "uint16"), "du": ("sbuf", [128, 16], "uint16"), "ou": ("sbuf", [128, 16], "uint16"),
+    "ff": ("sbuf", [128, 64], "bfloat16"), "uu": ("sbuf", [128, 64], "bfloat16"), "tt": ("sbuf", [128, 48], "bfloat16"),
+    "old": ("sbuf", [128, 16], "float32"), "oldr": ("sbuf", [128, 16], "float32"), "kth": ("sbuf", [128, 16], "float32"),
+    "tl": ("sbuf", [128, 16], "float32"), "tl2": ("sbuf", [128, 16], "float32"), "om": ("sbuf", [128, 16], "float32"),
+    "c1": ("sbuf", [128, 4], "float32"), "cw": ("sbuf", [128, 4], "float32"), "nx": ("sbuf", [128, 4], "float32"),
+    "ci": ("sbuf", [128, 32], "int32"), "cj": ("sbuf", [128, 32], "int32"), "cf": ("sbuf", [128, 32], "float32"),
+    "col": ("sbuf", [128, 16], "float32"),
+    "wk": ("sbuf", [128, 64], "float32"), "bi": ("sbuf", [128, 128], "float32"),
+    "irow": ("sbuf", [128, 256], "float32"), "arow": ("sbuf", [128, 256], "float32"), "grow": ("sbuf", [128, 128], "float32"),
+    "e8": ("sbuf", [128, 128], "float32"), "b8": ("sbuf", [128, 8], "float32"),
+    "one1": ("sbuf", [128, 128], "bfloat16"), "onew": ("sbuf", [128, 128], "bfloat16"), "oner": ("sbuf", [128, 128], "bfloat16"),
+    "oneb": ("sbuf", [128, 128], "bfloat16"), "onef": ("sbuf", [128, 128], "bfloat16"), "rotb": ("sbuf", [128, 128], "bfloat16"),
+    "idn": ("sbuf", [128, 128], "bfloat16"), "idw": ("sbuf", [128, 128], "bfloat16"),
+    "sel": ("sbuf", [128, 128], "float32"), "selr": ("sbuf", [128, 128], "float32"), "rot": ("sbuf", [128, 128], "float32"),
+    "tle": ("sbuf", [128, 128], "bfloat16"), "tgt": ("sbuf", [128, 128], "bfloat16"), "tmp": ("sbuf", [128, 128], "bfloat16"),
+    "sgn": ("sbuf", [128, 256], "bfloat16"), "sgh": ("sbuf", [128, 256], "bfloat16"),
+    "dgm": ("sbuf", [128, 272], "bfloat16"), "nd": ("sbuf", [128, 272], "bfloat16"),
+    "ko": ("sbuf", [128, 256], "bfloat16"), "ko1": ("sbuf", [128, 256], "bfloat16"), "ko2": ("sbuf", [128, 256], "bfloat16"),
+    "rs": ("sbuf", [128, 256], "float32"),
+    "iw": ("sbuf", [128, 16], "float32"), "iwo": ("sbuf", [128, 16], "float32"),
+    "pn": ("psum", [128, 512], "float32"), "z1": ("psum", [128, 512], "float32"),
+    "z3": ("psum", [128, 512], "float32"), "z4": ("psum", [128, 512], "float32"), "ph": ("psum", [128, 512], "float32"),
+    "pr": ("psum", [128, 512], "float32"), "pp": ("psum", [128, 512], "float32"), "pd": ("psum", [128, 512], "float32"),
+}
+PSUM = [k for k, v in SCRATCH.items() if v[0] == "psum"]
+SEMAPHORES = (["ev", "es", "et", "eg", "sent", "dq", "dc", "di", "dx", "dyx", "dyq", "dyd"]
+              + ["rs%d" % t for t in range(1, NR + 1)] + ["ro%d" % t for t in range(1, NR + 1)])
+ESEM = {"v": "ev", "s": "es", "t": "et", "g": "eg"}
+
+NAME_PLAN = "svsvsvsv"
+LOCK_PLAN = "vsvsvsvsvsvsvsvs"
+EARLY_VALUES = 5
+PRE_VALUES = 1
+FIRST_VALUES = 3
+FIRST_MAX = {"l15": 6, "o": 12, "c": 16}
+S_FIRST = 15
+MAX_PLAN = {"s9": 1, "s8": 2, "s5": 3, "s4": 4, "s1": 5, "l15": 10, "b": 12, "o": 14, "c": 16}
+SEND_AT = 0
+CARRY_LATE = False
+
+
+def rank_program(g, core, T, topo):
+    rank = T.rank_of(core)
+    if rank is None:
+        return
+    nxt = T.cores[(rank + 1) % len(T.cores)]
+    rid, pid = topo.addr(nxt)[0], topo.addr(nxt)[1]
+    mask = topo.mask(core, nxt)
+    neng = len(topo.engines(core, nxt))
+    Q = {"v": g.vector, "s": g.scalar, "t": g.tensor, "g": g, "y": g.sync}
+    ops = []
+
+    def R(name, lo=None, hi=None, step=1, parts=128):
+        if lo is None:
+            lo, hi = 0, SCRATCH[name][1][1]
+        return (name, lo, hi, step, parts)
+
+    def A(r):
+        if not isinstance(r, tuple):
+            return r
+        if len(r) == 3:
+            return A(r[1]).indirect(A(r[2]))
+        name, lo, hi, step, parts = r
+        if step == 1:
+            return T[name][0:parts, lo:hi]
+        return T[name][0:parts, lo:hi:step]
+
+    def ind(win, off):
+        return ("ind", win, off)
+
+    def add(q, fn, outs, ins, dma=None, ext=None):
+        rd, wr = [], []
+        for r in ins:
+            if isinstance(r, tuple):
+                rd += [r[1], r[2]] if len(r) == 3 else [r]
+        for r in outs:
+            if isinstance(r, tuple):
+                if len(r) == 3:
+                    wr.append(r[1]); rd.append(r[2])
+                else:
+                    wr.append(r)
+        ops.append({"q": q, "fn": fn, "rd": rd, "wr": wr, "dma": dma, "ext": ext or []})
+
+    def copy(o, i, q="v", ext=None):
+        if q == "v":
+            add("v", lambda e: e.tensor_copy(A(o), A(i)), [o], [i], ext=ext)
+        else:
+            add("s", lambda e: e.activation(A(o), A(i), ACT.Copy), [o], [i], ext=ext)
+
+    def ts(o, i, s1, op0, s2=None, op1=None):
+        if op1 is None:
+            add("v", lambda e: e.tensor_scalar(A(o), A(i), A(s1), None, op0), [o], [i, s1])
+        else:
+            add("v", lambda e: e.tensor_scalar(A(o), A(i), A(s1), A(s2), op0, op1), [o], [i, s1, s2])
+
+    def tt(o, a, b, op, ext=None):
+        add("v", lambda e: e.tensor_tensor(A(o), A(a), A(b), op), [o], [a, b], ext=ext)
+
+    def scan(o, d0, d1, init, op0, op1):
+        add("v", lambda e: e.tensor_tensor_scan(A(o), A(d0), A(d1), init, op0, op1), [o], [d0, d1])
+
+    def act(o, i, func, bias=0.0, scale=1.0):
+        add("s", lambda e: e.activation(A(o), A(i), func, bias=A(bias), scale=A(scale)), [o], [i, bias, scale])
+
+    def mset(o, c):
+        add("v", lambda e: e.memset(A(o), c), [o], [])
+
+    def mm(o, l, r, start, stop):
+        add("t", lambda e: e.matmul(A(o), A(l), A(r), start, stop), [o], [l, r])
+
+    def iota(o, pat, base, cm):
+        if SCRATCH[o[0]][2] == "int32":
+            add("g", lambda e: e.iota(A(o), pat, base, cm), [o], [])
+        else:
+            add("g", lambda e: e.iota(A(o), pat, base, cm, allow_small_or_imprecise_dtypes=True), [o], [])
+
+    def send(dst, src, sem):
+        add("g", lambda e: e.remote_dma(A(dst), A(src), T.sem[sem], T.sem["sent"], pid, rid, mask), [], [src], dma="remote")
+
+    def col(j):
+        return R("col", j, j + 1)
+
+    add("s", lambda e: e.dma_start(T.qi[0:8, 0:256], T.que[:]), [R("qi", 0, 256)], [], dma="dq")
+    add("y", lambda e: e.dma_start(T.ixi[:, :], T.idx[:]), [R("ixi")], [], dma="di")
+    add("y", lambda e: e.dma_start(T.xs[:, 0:4096], T.rec[:]), [R("xs", 0, 4096)], [], dma="dx")
+
+    iota(R("ci", 0, 16), [[-1, 16]], 16, 1)
+    iota(R("ci", 16, 19), [[16, 3]], 0, 1)
+    iota(R("arow"), [[0, 16], [1, 16]], 0, 0)
+    iota(R("e8", 0, 128, 1, 8), [[1, 8], [0, 16]], 0, -1)
+    iota(R("grow"), [[16, 8], [0, 16]], 0, 0)
+    iota(R("irow"), [[1, 256]], 0, 0)
+    iota(R("bi"), [[-256, 8], [16, 16]], -255, 0)
+    add("g", lambda e: e.dma_start(T.qi[0:8, 256:257], T.cur[:], allow_slow_non_contiguous=True), [R("qi", 256, 257)], [], dma="dc")
+    iota(R("lt"), [[0, LOW + 4096 + 256]], 0, 0)
+
+    mset(R("wn"), 0.0)
+    copy(R("d1", 0, 2048), R("wn"), "s")
+    copy(R("d1", 2048, 4096), R("wn"), "s")
+    ts(R("ci", 18, 19), R("ci", 18, 19), 80.0, ALU.add)
+    ts(R("cj", 0, 17), R("ci", 0, 17), 15, ALU.bitwise_and)
+    copy(col(0), R("ci", 16, 17))
+    ts(R("cj", 17, 19), R("ci", 17, 19), 127, ALU.bitwise_and)
+    ts(R("cj", 19, 22), R("ci", 16, 19), 112, ALU.bitwise_and)
+    mset(R("rs"), -1.0e6)
+    copy(R("cf", 0, 22), R("cj", 0, 22))
+    mset(R("dgm", 256, 272), 0.0)
+    mset(R("s32", 256, 272), 0.0)
+    ca, cp, cpr, cpb = R("cf", 16, 17), col(0), R("cf", 17, 18), R("cf", 18, 19)
+    cg, cgr, cgb = R("cf", 19, 20), R("cf", 20, 21), R("cf", 21, 22)
+    ts(col(9), ca, 0.0, ALU.is_equal, -8192.0, ALU.mult)
+    ts(col(5), ca, -1.0, ALU.mult)
+    ts(R("wk", 0, 16), R("cf", 0, 16), 0.0, ALU.is_equal, 256.0, ALU.mult)
+    ts(R("wk", 16, 32), R("cf", 0, 16), 1.0, ALU.is_equal, 16.0, ALU.mult)
+    ts(R("wk", 32, 48), R("cf", 0, 16), 2.0, ALU.is_equal)
+    ts(R("ko1"), R("arow"), ca, ALU.is_equal, 4096.0, ALU.mult)
+    ts(R("ko2"), R("arow"), ca, ALU.is_lt, -8192.0, ALU.mult)
+    tt(R("wk", 48, 64), R("wk", 0, 16), R("wk", 16, 32), ALU.add)
+    ts(R("e8", 0, 128, 1, 8), R("e8", 0, 128, 1, 8), 0.0, ALU.is_equal)
+    copy(R("qf", 0, 256, 1, 8), R("qi", 0, 256, 1, 8))
+    mm(R("pp", 0, 256), R("e8", 0, 128, 1, 8), R("qf", 0, 256, 1, 8), True, True)
+    tt(R("ko"), R("ko1"), R("ko2"), ALU.add)
+    tt(R("wk", 0, 16), R("wk", 48, 64), R("wk", 32, 48), ALU.add)
+    ts(R("b8"), R("grow", 0, 128, 16), cg, ALU.is_equal)
+    ts(col(8), col(9), -1.0, ALU.mult, -4096.0, ALU.add)
+    ts(R("ko", 15, 256, 16), R("ko", 15, 256, 16), col(9), ALU.add)
+    ts(col(7), col(9), 4096.0, ALU.add)
+    act(R("sgn"), R("arow"), ACT.Sign, col(5), 1.0)
+    for k in range(16):
+        act(R("wn", 129 * k, 128 * k + 128, 16), R("b8"), ACT.Identity, 0.0, R("wk", k, k + 1))
+    act(R("sgh"), R("sgn"), ACT.Identity, 0.0, 0.5)
+    ts(R("dgm", 0, 256), R("arow"), ca, ALU.is_equal, -2.0, ALU.mult)
+    scan(R("mo"), R("pp", 0, 256), R("ko"), -1.0, ALU.max, ALU.add)
+    act(R("nd"), R("dgm"), ACT.Identity, 1.0, 0.5)
+    copy(R("wq0", 0, 256), R("pp", 0, 256), "s")
+    ts(R("rot"), R("irow", 0, 128), cpr, ALU.is_equal)
+    ts(R("ou"), R("mo", 15, 256, 16), col(8), ALU.add)
+    ts(R("selr"), R("grow"), cpr, ALU.is_equal)
+    ts(R("idw"), R("irow", 0, 128), cp, ALU.is_equal, W, ALU.mult)
+    ts(R("onew"), R("grow"), cg, ALU.is_equal, W, ALU.mult)
+    ts(R("iw"), R("irow", 0, 256, 16), ca, ALU.add)
+    ts(R("bi"), R("bi"), ca, ALU.add)
+    ts(R("rs", 0, 256, 16), R("iw"), 4096.0 - 2 * W, ALU.add)
+    copy(R("at"), ind(R("ixi"), R("ou")))
+    ts(R("idn"), R("irow", 0, 128), cp, ALU.is_equal)
+    ts(R("sel"), R("grow"), cp, ALU.is_equal)
+    ts(R("rotb"), R("irow", 0, 128), cpb, ALU.is_equal)
+    ts(R("one1"), R("grow"), cg, ALU.is_equal)
+    ts(R("oner"), R("grow"), cgr, ALU.is_equal, W, ALU.mult)
+    ts(R("onef"), R("grow"), cgr, ALU.is_equal)
+    ts(R("oneb"), R("grow"), cgb, ALU.is_equal)
+    ts(R("tmp"), R("irow", 0, 128), cp, ALU.is_ge)
+    ts(R("iwo"), R("iw"), col(7), ALU.add)
+    tt(R("tle"), R("tmp"), R("one1"), ALU.mult)
+    mset(R("ff", 0, 33), 0.0)
+    mset(R("kth"), 4096.0 - 2 * W)
+    tt(R("tgt"), R("one1"), R("tle"), ALU.subtract)
+    mset(R("d1", 0, 4096, 16), -64.0)
+    copy(R("wa0", 1280, 1536), R("ixi", 0, 256))
+    copy(R("qf", 256, 257, 1, 8), R("qi", 256, 257, 1, 8))
+    mm(R("pp", 256, 257), R("e8", 0, 128, 1, 8), R("qf", 256, 257, 1, 8), True, True)
+
+    def names(t, between):
+        for c in range(8):
+            copy(R("g1", 512 * c, 512 * c + 512), ind(R("xs", 0, 4096), R("at", 32 * c, 32 * c + 32)), NAME_PLAN[c])
+            if c % 2:
+                b = c // 2
+                for k in range(16):
+                    mm(R("pn", 64 * b, 64 * b + 64), R("wn", 128 * k, 128 * k + 128),
+                       R("g1", 1024 * b + k, 1024 * b + 1024, 16), k == 0, k == 15)
+            for f in between.get(c, []):
+                f(t)
+
+    def turn_stored(t):
+        if t % 2:
+            mm(R("pr", 0, 256), R("rot"), R("s32", 0, 256), True, True)
+
+    def send_stored(t):
+        su = R("su", 256 * t, 256 * t + 256)
+        copy(su, R("pr", 0, 256) if t % 2 else R("s32", 0, 256))
+        send(R("sin", 256 * t, 256 * t + 256), su, "rs%d" % t)
+
+    def twins_pe(t):
+        sel = R("selr") if t % 2 else R("sel")
+        mm(R("ph", 0, 272), sel, R("s32"), True, False)
+        mm(R("ph", 0, 272), R("idw"), R("dgm"), False, True)
+        mm(R("pd", 256, 512), sel, R("s32", 0, 256), True, False)
+        mm(R("pd", 256, 512), R("onew"), R("dgm", 0, 256), False, True)
+
+    def twins_v(t):
+        scan(R("hh"), R("nd"), R("ph", 0, 272), 0.0, ALU.mult, ALU.min)
+        tt(R("ne"), R("hh", 15, 271), R("pd", 256, 512), ALU.not_equal)
+        mm(R("z1", 0, 256), R("idw"), R("ne"), False, t == 1)
+
+    def lock_base(t):
+        mm(R("z1", 0, 256), R("selr") if t % 2 else R("sel"), R("s32", 0, 256), True, False)
+        mm(R("z1", 0, 256), R("onew"), R("dgm", 0, 256), False, False)
+        mm(R("z1", 0, 256), R("idw"), R("sgh"), False, False)
+
+    def list_base(t):
+        mm(R("z3", 0, 256), R("selr") if t % 2 else R("sel"), R("s32", 0, 256), True, False)
+        mm(R("z3", 0, 256), R("idw"), R("dgm", 0, 256), False, False)
+        if t > 1:
+            mm(R("z4", 0, 256), R("idw"), R("dgm", 0, 256), True, False)
+
+    def kinds(t):
+        one = R("oner") if t % 2 else R("onew")
+        tt(R("df"), R("s32", 0, 256), R("pn", 0, 256), ALU.not_equal)
+        mm(R("z1", 0, 256), one, R("df"), False, True)
+        mm(R("z4", 0, 256), one, R("df"), False, True)
+        mm(R("z3", 0, 256), one, R("df"), False, False)
+
+    def locks(t):
+        scan(R("m1"), R("rs"), R("z1", 0, 256), -1.0e6, ALU.max, ALU.min)
+        ts(R("lo", 0, 32, 2), R("m1", 15, 256, 16), 2 * W + LOW, ALU.add, ca, ALU.max)
+        for c in range(15, -1, -1):
+            ts(ind(R("lt"), R("lo", 2 * c, 2 * c + 1)), R("irow", 16 * c, 16 * c + 16), -1.0, ALU.mult, 256.0 * t + 255.0, ALU.add)
+            if t > 1 and c == 15:
+                scan(R("m4"), R("rs"), R("z4", 0, 256), -1.0e6, ALU.max, ALU.min)
+            if t > 1 and c == 13:
+                tt(R("ff", 17, 33), R("m4", 15, 256, 16), R("oldr") if t % 2 else R("old"), ALU.is_ge)
+            if t > 1 and c == 12:
+                ts(R("kth"), R("ff", 17, 33), 1.0e6, ALU.mult, 4096.0 - 2 * W, ALU.add)
+            if c == S_FIRST:
+                for b in range(PRE_VALUES if t > 1 else 0, early(t)):
+                    values(t, b)
+            if t > 1:
+                maxima(t, "s%d" % c)
+
+    def heads(b):
+        copy(R("d1", 512 * b + 15, 512 * b + 512, 16), R("g2", 512 * b, 512 * b + 512, 16), "s")
+
+    def values(t, b):
+        copy(R("g2", 512 * b, 512 * b + 512), ind(R("xs", 0, 4096), R("sin", 256 * t + 32 * b, 256 * t + 32 * b + 32)), "s",
+             ext=[("rs%d" % t, neng)])
+        if b > 0 and b != early(t):
+            heads(b - 1)
+        if b == 7 or b == early(t) - 1:
+            heads(b)
+
+    def early(t):
+        return EARLY_VALUES if t > 1 else FIRST_VALUES
+
+    done = [0]
+
+    def maxima(t, slot):
+        upto = 16 * t + (MAX_PLAN if t > 1 else FIRST_MAX).get(slot, 0)
+        done[0] = max(done[0], 16 * t)
+        if upto > done[0]:
+            lo, hi = 256 * (done[0] - 16 * t), 256 * (upto - 16 * t)
+            scan(R("mx", lo, hi), R("g2", lo, hi), R("d1", lo, hi), 0.0, ALU.max, ALU.add)
+            done[0] = upto
+
+    def lookups(t):
+        for c in range(16):
+            o = R("lg", 256 * c, 256 * c + 256)
+            src = ind(R("lt", LOW, LOW + 4096), R("su", 256 * t + 16 * c, 256 * t + 16 * c + 16))
+            bias = R("bi", 16 * t + c, 16 * t + c + 1)
+            if LOCK_PLAN[c] == "v":
+                ts(o, src, bias, ALU.add, 0.0, ALU.max)
+            else:
+                act(o, src, ACT.Relu, bias, 1.0)
+            if c % 4 == 3:
+                b = c // 4
+                for k in range(16):
+                    mm(R("z3", 64 * b, 64 * b + 64), R("idw"), R("lg", 1024 * b + k, 1024 * b + 1024, 16), False, c == 15 and k == 15)
+            maxima(t, "l%d" % c)
+
+    def decide(t):
+        scan(R("m3"), R("rs"), R("z3", 0, 256), -1.0e6, ALU.max, ALU.min)
+        ts(R("osn", 16 * t, 16 * t + 16), R("m3", 15, 256, 16), 2 * W, ALU.add)
+        send(R("oin", 16 * t, 16 * t + 16), R("osn", 16 * t, 16 * t + 16), "ro%d" % t)
+
+    def order_a(t):
+        m = R("m3", 15, 256, 16)
+        ts(R("ff", 33, 49), m, 4096.0 - 2 * W, ALU.is_lt)
+        tt(R("ff", 1, 17), m, R("kth"), ALU.is_ge)
+        scan(R("uu", 0, 49), R("ff", 0, 49), R("ff", 0, 49), 0.0, ALU.add, ALU.max)
+        mm(R("pp", 0, 48), R("tle"), R("uu", 1, 49), True, False)
+        mm(R("pp", 0, 48), R("tgt"), R("uu", 0, 48), False, True)
+        mm(R("pp", 64, 65), R("oneb") if t % 2 else R("one1"), R("uu", 32, 33), True, True)
+        if t % 2 == 0:
+            mm(R("pp", 72, 73), R("onef"), R("uu", 32, 33), True, True)
+
+    def order_b(t):
+        tt(R("tt"), R("ff", 1, 49), R("pp", 0, 48), ALU.mult)
+        for j in range(3):
+            mm(R("pd", 0, 16), R("rotb") if t % 2 else R("idn"), R("tt", 16 * j, 16 * j + 16), j == 0, j == 2)
+        ts(R("c1", 0, 1), R("pp", 64, 65), -1.0, ALU.mult, R("nx", 0, 1), ALU.add)
+        ts(R("old"), R("iw"), R("pp", 64, 65), ALU.is_lt, 4096.0 - 2 * W, ALU.mult)
+        if t % 2 == 0:
+            ts(R("oldr"), R("iw"), R("pp", 72, 73), ALU.is_lt, 4096.0 - 2 * W, ALU.mult)
+
+    def order_c(t):
+        ts(R("du"), R("pd", 0, 16), -1.0, ALU.add)
+        ts(R("tl"), R("iwo"), R("c1", 0, 1), ALU.add)
+        copy(ind(R("orow"), R("du")), R("irow"))
+        tt(R("tl2"), R("tl"), R("old"), ALU.add)
+        maxima(t, "o")
+        scan(R("mo"), R("orow"), R("ko"), -1.0, ALU.max, ALU.add)
+        if t < NR:
+            ts(R("cw", 0, 1), R("c1", 0, 1), 1024.0, ALU.is_ge, -1024.0, ALU.mult)
+        tt(R("om"), R("mo", 15, 256, 16), R("tl2"), ALU.max)
+        if t < NR:
+            ts(R("nx", 0, 1), R("c1", 0, 1), R("cw", 0, 1), ALU.add, 256.0, ALU.add)
+        ts(R("ou"), R("om"), col(8), ALU.add)
+
+    def wrap(t):
+        ts(R("wv"), R("mx", 15, 4096, 16), 16.0, ALU.is_ge, -16.0, ALU.mult)
+
+    def write(t):
+        tt(ind(R("xs"), R("oin", 16 * t, 16 * t + 16)), R("mx", 15, 4096, 16), R("wv"), ALU.add, ext=[("ro%d" % t, neng)])
+
+    def carry(t):
+        if t < NR - 1:
+            copy(R("wa%d" % (t % 2), 0, 256), ind(R("wa%d" % ((t - 1) % 2)), R("ou")), "s")
+        copy(R("wq%d" % (t % 2), 0, 256), ind(R("wq%d" % ((t - 1) % 2)), R("ou")), "s")
+
+    for t in range(1, NR + 1):
+        if t == 1:
+            names(t, {})
+            copy(R("s32", 0, 256), R("pn", 0, 256), "s")
+            turn_stored(t)
+            twins_pe(t)
+            copy(R("ws", 0, 256), R("pn", 0, 256), "s")
+            ts(R("nx", 0, 1), R("pp", 256, 257), 256.0, ALU.add)
+            copy(R("wa0", 256, 1280), R("ixi"))
+            send_stored(t)
+            iota(R("ws", 256, 1536), [[0, 1280]], -1, 0)
+            iota(R("wq0", 256, 1280), [[1, 1024]], 0, 0)
+            iota(R("wq0", 1280, 1536), [[1, 256]], 0, 0)
+            lock_base(t)
+            twins_v(t)
+            list_base(t)
+            copy(R("wa1", 256, 1536), R("wa0", 256, 1536), "s")
+            copy(R("wa0", 0, 256), ind(R("wa0", 256, 1536), R("ou")), "s")
+        else:
+            names(t, {SEND_AT: [send_stored], 7: [twins_v]} if SEND_AT >= 0 else {7: [twins_v]})
+            kinds(t)
+            for b in range(PRE_VALUES):
+                values(t, b)
+            copy(R("ws", 0, 256), R("pn", 0, 256), "s")
+            if CARRY_LATE:
+                carry(t - 1)
+        locks(t)
+        lookups(t)
+        for b in range(early(t), 8):
+            values(t, b)
+        decide(t)
+        if t == 1:
+            iota(R("wq1", 256, 1280), [[1, 1024]], 0, 0)
+            iota(R("wq1", 1280, 1536), [[1, 256]], 0, 0)
+        order_a(t)
+        maxima(t, "a")
+        order_b(t)
+        maxima(t, "b")
+        order_c(t)
+        copy(R("s32", 0, 256), ind(R("ws"), R("ou")), "s")
+        if t == NR:
+            add("y", lambda e: e.dma_start(T.yd[:], T.s32[:, 0:256]), [], [R("s32", 0, 256)], dma="dyd")
+            maxima(t, "c")
+            wrap(t)
+            write(t)
+            add("y", lambda e: e.dma_start(T.yx[:], T.xs[:, 0:4096]), [], [R("xs", 0, 4096)], dma="dyx")
+        if t < NR:
+            turn_stored(t + 1)
+            twins_pe(t + 1)
+            lock_base(t + 1)
+            list_base(t + 1)
+            maxima(t, "c")
+            copy(R("at"), ind(R("wa%d" % ((t - 1) % 2)), R("ou")))
+            wrap(t)
+            if SEND_AT < 0:
+                send_stored(t + 1)
+            write(t)
+        if t == NR or not CARRY_LATE:
+            carry(t)
+    ql = "wq%d" % (NR % 2)
+    add("s", lambda e: e.dma_start(T.yq[:], T[ql][0:128:16, 0:256]), [], [R(ql, 0, 256)], dma="dyq")
+
+    def meet(a, b):
+        if a[0] != b[0] or a[1] >= b[2] or b[1] >= a[2]:
+            return False
+        return a[3] != b[3] or a[3] == 1 or (a[1] - b[1]) % a[3] == 0
+
+    def banks(o):
+        return set(r[0] for r in o["rd"] + o["wr"] if r[0] in PSUM)
+
+    known = {q: {} for q in Q}
+    byname = {}
+    for n, o in enumerate(ops):
+        q = o["q"]
+        cand = set()
+        for r in o["rd"] + o["wr"]:
+            cand.update(byname.get(r[0], []))
+        need = {}
+        bk = banks(o)
+        for m in cand:
+            p = ops[m]
+            same = p["q"] == q and p["dma"] is None and o["dma"] is None
+            hit = any(meet(a, b) for a in o["rd"] for b in p["wr"]) or any(meet(a, b) for a in o["wr"] for b in p["wr"] + p["rd"])
+            if same:
+                hit = hit and q != "t"
+            else:
+                hit = hit or bool(bk & banks(p))
+            if hit:
+                if p["dma"] == "remote":
+                    raise ValueError("a buffer that a remote write reads is written again")
+                key = p["dma"] or p["q"]
+                need[key] = max(need.get(key, -1), m)
+        o["wait"] = []
+        for key, m in sorted(need.items(), key=lambda kv: -kv[1]):
+            if known[q].get(key, -1) < m:
+                o["wait"].append(m)
+                ops[m]["sig"] = True
+                for k2, v2 in ops[m]["clock"].items():
+                    known[q][k2] = max(known[q].get(k2, -1), v2)
+        o["xw"] = []
+        for name, val in o["ext"]:
+            if name not in known[q]:
+                known[q][name] = 0
+                o["xw"].append((name, val))
+        o["clock"] = dict(known[q])
+        o["clock"][o["dma"] or q] = n
+        for r in o["rd"] + o["wr"]:
+            byname.setdefault(r[0], []).append(n)
+    count = {q: 0 for q in ESEM}
+    nsent = 0
+    for o in ops:
+        e = Q[o["q"]]
+        for m in o["wait"]:
+            p = ops[m]
+            if p["dma"]:
+                e.wait_ge(T.sem[p["dma"]], 16)
+            else:
+                e.wait_ge(T.sem[ESEM[p["q"]]], p["count"])
+        for name, val in o["xw"]:
+            e.wait_ge(T.sem[name], val)
+        ins = o["fn"](e)
+        if o["dma"] == "remote":
+            nsent += neng
+        elif o["dma"]:
+            ins.then_inc(T.sem[o["dma"]], 16)
+        elif o.get("sig"):
+            count[o["q"]] += 1
+            o["count"] = count[o["q"]]
+            ins.then_inc(T.sem[ESEM[o["q"]]], 1)
+    g.wait_ge(T.sem["sent"], nsent)
+    g.sync.wait_ge(T.sem["dyd"], 16)
+    g.sync.wait_ge(T.sem["dyx"], 16)
+    g.scalar.wait_ge(T.sem["dyq"], 16)

@@ -20,7 +20,7 @@ SCRATCH = {
     "at": ("sbuf", [128, 256], "uint16"),
     "su": ("sbuf", [128, 2048], "uint16"), "sin": ("sbuf", [128, 2048], "uint16"),
     "osn": ("sbuf", [128, 128], "uint16"), "oin": ("sbuf", [128, 128], "uint16"),
-    "s32": ("sbuf", [128, 272], "float32"),
+    "s32": ("sbuf", [128, 272], "float32"), "s16": ("sbuf", [128, 272], "float16"),
     "df": ("sbuf", [128, 256], "bfloat16"), "ne": ("sbuf", [128, 256], "bfloat16"),
     "wv": ("sbuf", [128, 256], "bfloat16"),
     "hh": ("sbuf", [128, 272], "float32"),
@@ -40,11 +40,12 @@ SCRATCH = {
     "oneb": ("sbuf", [128, 128], "bfloat16"), "onef": ("sbuf", [128, 128], "bfloat16"), "rotb": ("sbuf", [128, 128], "bfloat16"),
     "idn": ("sbuf", [128, 128], "bfloat16"), "idw": ("sbuf", [128, 128], "bfloat16"),
     "sel": ("sbuf", [128, 128], "float32"), "selr": ("sbuf", [128, 128], "float32"), "rot": ("sbuf", [128, 128], "float32"),
+    "selh": ("sbuf", [128, 128], "float16"), "roth": ("sbuf", [128, 128], "float16"),
     "tle": ("sbuf", [128, 128], "bfloat16"), "tgt": ("sbuf", [128, 128], "bfloat16"), "tmp": ("sbuf", [128, 128], "bfloat16"),
     "sgn": ("sbuf", [128, 256], "bfloat16"), "sgh": ("sbuf", [128, 256], "bfloat16"),
     "dgm": ("sbuf", [128, 272], "bfloat16"), "nd": ("sbuf", [128, 272], "bfloat16"),
     "ko": ("sbuf", [128, 256], "bfloat16"), "ko1": ("sbuf", [128, 256], "bfloat16"), "ko2": ("sbuf", [128, 256], "bfloat16"),
-    "rs": ("sbuf", [128, 256], "float32"),
+    "rs": ("sbuf", [128, 256], "float32"), "off": ("sbuf", [128, 64], "bfloat16"),
     "iw": ("sbuf", [128, 16], "float32"), "iwo": ("sbuf", [128, 16], "float32"),
     "pn": ("psum", [128, 512], "float32"), "z1": ("psum", [128, 512], "float32"),
     "z3": ("psum", [128, 512], "float32"), "z4": ("psum", [128, 512], "float32"), "ph": ("psum", [128, 512], "float32"),
@@ -52,19 +53,21 @@ SCRATCH = {
 }
 PSUM = [k for k, v in SCRATCH.items() if v[0] == "psum"]
 SEMAPHORES = (["ev", "es", "et", "eg", "sent", "dq", "dc", "di", "dx", "dyx", "dyq", "dyd"]
-              + ["rs%d" % t for t in range(1, NR + 1)] + ["ro%d" % t for t in range(1, NR + 1)])
+              + ["rs%d" % t for t in range(NR + 1)] + ["ro%d" % t for t in range(1, NR + 1)])
 ESEM = {"v": "ev", "s": "es", "t": "et", "g": "eg"}
 
-NAME_PLAN = "svsvsvsv"
 LOCK_PLAN = "vsvsvsvsvsvsvsvs"
-EARLY_VALUES = 5
-PRE_VALUES = 1
+EARLY_VALUES = 4
+HEADS = {2: [(0, 2)], 3: [(2, 4)], 4: [(4, 5)], 5: [(5, 6)], 6: [(6, 7)], 7: [(7, 8)]}
+FIRST_HEADS = {2: [(0, 3)], 4: [(3, 4)], 6: [(4, 6)], 7: [(6, 8)]}
 FIRST_VALUES = 3
-FIRST_MAX = {"l15": 6, "o": 12, "c": 16}
-S_FIRST = 15
-MAX_PLAN = {"s9": 1, "s8": 2, "s5": 3, "s4": 4, "s1": 5, "l15": 10, "b": 12, "o": 14, "c": 16}
-SEND_AT = 0
-CARRY_LATE = False
+FIRST_MAX = {"l15": 6, "b": 8, "o": 12, "c": 16}
+KEEP_AT = 8
+CUT = 120
+PIECES = {16: (120, 128)}
+LOW_AT = (12, 10, 9, 6, 5, 4)
+MAX_PLAN = {"s3": 1, "s2": 2, "s1": 3, "l15": 8, "a": 10, "o": 12, "c": 16}
+SPARE = 2048.0 - 2 * W
 
 
 def rank_program(g, core, T, topo):
@@ -173,7 +176,7 @@ def rank_program(g, core, T, topo):
     mset(R("rs"), -1.0e6)
     copy(R("cf", 0, 22), R("cj", 0, 22))
     mset(R("dgm", 256, 272), 0.0)
-    mset(R("s32", 256, 272), 0.0)
+    copy(R("s16", 256, 272), R("cf", 0, 16))
     ca, cp, cpr, cpb = R("cf", 16, 17), col(0), R("cf", 17, 18), R("cf", 18, 19)
     cg, cgr, cgb = R("cf", 19, 20), R("cf", 20, 21), R("cf", 21, 22)
     ts(col(9), ca, 0.0, ALU.is_equal, -8192.0, ALU.mult)
@@ -196,7 +199,7 @@ def rank_program(g, core, T, topo):
     act(R("sgn"), R("arow"), ACT.Sign, col(5), 1.0)
     for k in range(16):
         act(R("wn", 129 * k, 128 * k + 128, 16), R("b8"), ACT.Identity, 0.0, R("wk", k, k + 1))
-    act(R("sgh"), R("sgn"), ACT.Identity, 0.0, 0.5)
+    act(R("sgh"), R("sgn"), ACT.Identity, -2.0, 0.5)
     ts(R("dgm", 0, 256), R("arow"), ca, ALU.is_equal, -2.0, ALU.mult)
     scan(R("mo"), R("pp", 0, 256), R("ko"), -1.0, ALU.max, ALU.add)
     act(R("nd"), R("dgm"), ACT.Identity, 1.0, 0.5)
@@ -208,7 +211,7 @@ def rank_program(g, core, T, topo):
     ts(R("onew"), R("grow"), cg, ALU.is_equal, W, ALU.mult)
     ts(R("iw"), R("irow", 0, 256, 16), ca, ALU.add)
     ts(R("bi"), R("bi"), ca, ALU.add)
-    ts(R("rs", 0, 256, 16), R("iw"), 4096.0 - 2 * W, ALU.add)
+    ts(R("rs", 0, 256, 16), R("iw"), SPARE, ALU.add)
     copy(R("at"), ind(R("ixi"), R("ou")))
     ts(R("idn"), R("irow", 0, 128), cp, ALU.is_equal)
     ts(R("sel"), R("grow"), cp, ALU.is_equal)
@@ -221,90 +224,133 @@ def rank_program(g, core, T, topo):
     ts(R("iwo"), R("iw"), col(7), ALU.add)
     tt(R("tle"), R("tmp"), R("one1"), ALU.mult)
     mset(R("ff", 0, 33), 0.0)
-    mset(R("kth"), 4096.0 - 2 * W)
+    mset(R("kth"), SPARE)
     tt(R("tgt"), R("one1"), R("tle"), ALU.subtract)
     mset(R("d1", 0, 4096, 16), -64.0)
     copy(R("wa0", 1280, 1536), R("ixi", 0, 256))
+    copy(R("wa1", 1280, 1536), R("wa0", 1280, 1536), "s")
+    mset(R("off"), -2048.0 / W)
+    copy(R("wa0", 0, 256), R("at"))
+    copy(R("s32", 256, 272), R("cf", 0, 16), "s")
+    ts(R("roth"), R("irow", 0, 128), cpr, ALU.is_equal)
+    ts(R("selh"), R("grow"), cpr, ALU.is_equal)
     copy(R("qf", 256, 257, 1, 8), R("qi", 256, 257, 1, 8))
     mm(R("pp", 256, 257), R("e8", 0, 128, 1, 8), R("qf", 256, 257, 1, 8), True, True)
 
-    def names(t, between):
-        for c in range(8):
-            copy(R("g1", 512 * c, 512 * c + 512), ind(R("xs", 0, 4096), R("at", 32 * c, 32 * c + 32)), NAME_PLAN[c])
-            if c % 2:
-                b = c // 2
-                for k in range(16):
-                    mm(R("pn", 64 * b, 64 * b + 64), R("wn", 128 * k, 128 * k + 128),
-                       R("g1", 1024 * b + k, 1024 * b + 1024, 16), k == 0, k == 15)
-            for f in between.get(c, []):
-                f(t)
+    def pn(lo, hi):
+        return R("pn", lo, hi) if lo < 128 else R("pr", 128 + lo, 128 + hi)
+
+    def z1(h):
+        return R("pp", 256, 384) if h else R("z1", 0, 128)
+
+    def half(name, h):
+        return R(name, 128 * h, 128 * h + 128)
+
+    def digits(lo, hi, q):
+        copy(R("g1", 16 * lo, 16 * hi), ind(R("xs", 0, 4096), R("at", lo, hi)), q)
+
+    def names(b):
+        mm(pn(64 * b, 64 * b + 64), R("idw"), R("off"), True, False)
+        for k in range(16):
+            mm(pn(64 * b, 64 * b + 64), R("wn", 128 * k, 128 * k + 128), R("g1", 1024 * b + k, 1024 * b + 1024, 16), False, k == 15)
+
+    def rest_names(slot):
+        if slot in PIECES:
+            digits(PIECES[slot][0], PIECES[slot][1], "v")
+            if PIECES[slot][1] == 128:
+                names(1)
+
+    def keep_names(dst, q):
+        for h in (1, 0):
+            copy(half(dst, h), pn(128 * h, 128 * h + 128), q)
 
     def turn_stored(t):
         if t % 2:
-            mm(R("pr", 0, 256), R("rot"), R("s32", 0, 256), True, True)
+            mm(R("pr", 0, 256), R("rot"), stored(t, 256), True, True)
+
+    def stored(t, n):
+        return R("s32" if t > 1 else "s16", 0, n)
+
+    def first_rows(t):
+        return R("selh" if t == 1 else "selr" if t % 2 else "sel")
 
     def send_stored(t):
         su = R("su", 256 * t, 256 * t + 256)
-        copy(su, R("pr", 0, 256) if t % 2 else R("s32", 0, 256))
+        ts(su, R("pr", 0, 256) if t % 2 else R("s32", 0, 256), 2048.0, ALU.add)
         send(R("sin", 256 * t, 256 * t + 256), su, "rs%d" % t)
 
     def twins_pe(t):
-        sel = R("selr") if t % 2 else R("sel")
-        mm(R("ph", 0, 272), sel, R("s32"), True, False)
+        mm(R("ph", 0, 272), first_rows(t), stored(t, 272), True, False)
         mm(R("ph", 0, 272), R("idw"), R("dgm"), False, True)
-        mm(R("pd", 256, 512), sel, R("s32", 0, 256), True, False)
+        mm(R("pd", 256, 512), first_rows(t), stored(t, 256), True, False)
         mm(R("pd", 256, 512), R("onew"), R("dgm", 0, 256), False, True)
 
     def twins_v(t):
         scan(R("hh"), R("nd"), R("ph", 0, 272), 0.0, ALU.mult, ALU.min)
         tt(R("ne"), R("hh", 15, 271), R("pd", 256, 512), ALU.not_equal)
-        mm(R("z1", 0, 256), R("idw"), R("ne"), False, t == 1)
 
-    def lock_base(t):
-        mm(R("z1", 0, 256), R("selr") if t % 2 else R("sel"), R("s32", 0, 256), True, False)
-        mm(R("z1", 0, 256), R("onew"), R("dgm", 0, 256), False, False)
-        mm(R("z1", 0, 256), R("idw"), R("sgh"), False, False)
+    def lock_base(t, h):
+        mm(z1(h), first_rows(t), half("s32" if t > 1 else "s16", h), True, False)
+        mm(z1(h), R("idw"), half("sgh", h), False, False)
+
+    def lock_twins(t, h):
+        mm(z1(h), R("idw"), half("ne", h), False, t == 1)
 
     def list_base(t):
-        mm(R("z3", 0, 256), R("selr") if t % 2 else R("sel"), R("s32", 0, 256), True, False)
+        mm(R("z3", 0, 256), first_rows(t), stored(t, 256), True, False)
         mm(R("z3", 0, 256), R("idw"), R("dgm", 0, 256), False, False)
         if t > 1:
             mm(R("z4", 0, 256), R("idw"), R("dgm", 0, 256), True, False)
 
-    def kinds(t):
+    def kinds(t, h):
         one = R("oner") if t % 2 else R("onew")
-        tt(R("df"), R("s32", 0, 256), R("pn", 0, 256), ALU.not_equal)
-        mm(R("z1", 0, 256), one, R("df"), False, True)
-        mm(R("z4", 0, 256), one, R("df"), False, True)
-        mm(R("z3", 0, 256), one, R("df"), False, False)
+        tt(half("df", h), half("s32", h), pn(128 * h, 128 * h + 128), ALU.not_equal)
+        mm(z1(h), one, half("df", h), False, True)
+        if h == 0:
+            list_base(t)
+            mm(R("z4", 0, 256), one, R("df"), False, True)
+            mm(R("z3", 0, 256), one, R("df"), False, False)
+
+    def firsts(h):
+        scan(half("m1", h), half("rs", h), z1(h), -1.0e6, ALU.max, ALU.min)
+
+    def lock_list(h):
+        ts(R("lo", 16 * h, 16 * h + 16, 2), R("m1", 128 * h + 15, 128 * h + 128, 16), 4096.0 - SPARE + LOW, ALU.add, ca, ALU.max)
 
     def locks(t):
-        scan(R("m1"), R("rs"), R("z1", 0, 256), -1.0e6, ALU.max, ALU.min)
-        ts(R("lo", 0, 32, 2), R("m1", 15, 256, 16), 2 * W + LOW, ALU.add, ca, ALU.max)
         for c in range(15, -1, -1):
             ts(ind(R("lt"), R("lo", 2 * c, 2 * c + 1)), R("irow", 16 * c, 16 * c + 16), -1.0, ALU.mult, 256.0 * t + 255.0, ALU.add)
-            if t > 1 and c == 15:
+            if t > 1:
+                rest_names(c)
+            if t > 1 and c == LOW_AT[0]:
+                kinds(t, 0)
+            if t > 1 and c == LOW_AT[1]:
+                firsts(0)
+            if t > 1 and c == LOW_AT[2]:
+                lock_list(0)
+            if t > 1 and c == LOW_AT[3]:
                 scan(R("m4"), R("rs"), R("z4", 0, 256), -1.0e6, ALU.max, ALU.min)
-            if t > 1 and c == 13:
+            if t > 1 and c == LOW_AT[4]:
                 tt(R("ff", 17, 33), R("m4", 15, 256, 16), R("oldr") if t % 2 else R("old"), ALU.is_ge)
-            if t > 1 and c == 12:
-                ts(R("kth"), R("ff", 17, 33), 1.0e6, ALU.mult, 4096.0 - 2 * W, ALU.add)
-            if c == S_FIRST:
-                for b in range(PRE_VALUES if t > 1 else 0, early(t)):
+            if t > 1 and c == LOW_AT[5]:
+                ts(R("kth"), R("ff", 17, 33), 1.0e6, ALU.mult, SPARE, ALU.add)
+            if c == 15:
+                for b in range(early(t)):
                     values(t, b)
             if t > 1:
                 maxima(t, "s%d" % c)
+            else:
+                lo = 128 * (c // 2)
+                copy(R("wa%d" % (c % 2), 256 + lo, 384 + lo), R("ixi", lo, lo + 128))
 
-    def heads(b):
-        copy(R("d1", 512 * b + 15, 512 * b + 512, 16), R("g2", 512 * b, 512 * b + 512, 16), "s")
+    def heads(lo, hi):
+        copy(R("d1", 512 * lo + 15, 512 * hi, 16), R("g2", 512 * lo, 512 * hi, 16), "s")
 
     def values(t, b):
         copy(R("g2", 512 * b, 512 * b + 512), ind(R("xs", 0, 4096), R("sin", 256 * t + 32 * b, 256 * t + 32 * b + 32)), "s",
-             ext=[("rs%d" % t, neng)])
-        if b > 0 and b != early(t):
-            heads(b - 1)
-        if b == 7 or b == early(t) - 1:
-            heads(b)
+             ext=[("rs0" if t == 1 and b < 4 else "rs%d" % t, neng)])
+        for lo, hi in (HEADS if t > 1 else FIRST_HEADS).get(b, []):
+            heads(lo, hi)
 
     def early(t):
         return EARLY_VALUES if t > 1 else FIRST_VALUES
@@ -336,12 +382,12 @@ def rank_program(g, core, T, topo):
 
     def decide(t):
         scan(R("m3"), R("rs"), R("z3", 0, 256), -1.0e6, ALU.max, ALU.min)
-        ts(R("osn", 16 * t, 16 * t + 16), R("m3", 15, 256, 16), 2 * W, ALU.add)
+        ts(R("osn", 16 * t, 16 * t + 16), R("m3", 15, 256, 16), 4096.0 - SPARE, ALU.add)
         send(R("oin", 16 * t, 16 * t + 16), R("osn", 16 * t, 16 * t + 16), "ro%d" % t)
 
     def order_a(t):
         m = R("m3", 15, 256, 16)
-        ts(R("ff", 33, 49), m, 4096.0 - 2 * W, ALU.is_lt)
+        ts(R("ff", 33, 49), m, SPARE, ALU.is_lt)
         tt(R("ff", 1, 17), m, R("kth"), ALU.is_ge)
         scan(R("uu", 0, 49), R("ff", 0, 49), R("ff", 0, 49), 0.0, ALU.add, ALU.max)
         mm(R("pp", 0, 48), R("tle"), R("uu", 1, 49), True, False)
@@ -355,9 +401,9 @@ def rank_program(g, core, T, topo):
         for j in range(3):
             mm(R("pd", 0, 16), R("rotb") if t % 2 else R("idn"), R("tt", 16 * j, 16 * j + 16), j == 0, j == 2)
         ts(R("c1", 0, 1), R("pp", 64, 65), -1.0, ALU.mult, R("nx", 0, 1), ALU.add)
-        ts(R("old"), R("iw"), R("pp", 64, 65), ALU.is_lt, 4096.0 - 2 * W, ALU.mult)
+        ts(R("old"), R("iw"), R("pp", 64, 65), ALU.is_lt, SPARE, ALU.mult)
         if t % 2 == 0:
-            ts(R("oldr"), R("iw"), R("pp", 72, 73), ALU.is_lt, 4096.0 - 2 * W, ALU.mult)
+            ts(R("oldr"), R("iw"), R("pp", 72, 73), ALU.is_lt, SPARE, ALU.mult)
 
     def order_c(t):
         ts(R("du"), R("pd", 0, 16), -1.0, ALU.add)
@@ -380,40 +426,64 @@ def rank_program(g, core, T, topo):
         tt(ind(R("xs"), R("oin", 16 * t, 16 * t + 16)), R("mx", 15, 4096, 16), R("wv"), ALU.add, ext=[("ro%d" % t, neng)])
 
     def carry(t):
-        if t < NR - 1:
-            copy(R("wa%d" % (t % 2), 0, 256), ind(R("wa%d" % ((t - 1) % 2)), R("ou")), "s")
         copy(R("wq%d" % (t % 2), 0, 256), ind(R("wq%d" % ((t - 1) % 2)), R("ou")), "s")
 
     for t in range(1, NR + 1):
         if t == 1:
-            names(t, {})
-            copy(R("s32", 0, 256), R("pn", 0, 256), "s")
-            turn_stored(t)
-            twins_pe(t)
-            copy(R("ws", 0, 256), R("pn", 0, 256), "s")
+            for b in range(4):
+                digits(64 * b, 64 * b + 32, "s")
+                digits(64 * b + 32, 64 * b + 64, "v")
+                names(b)
+                if b == 2:
+                    copy(half("s16", 0), pn(0, 128))
+                    mm(R("pd", 0, 128), R("roth"), half("s16", 0), True, True)
+            ts(R("su", 256, 384), R("pd", 0, 128), 2048.0, ALU.add)
+            send(R("sin", 256, 384), R("su", 256, 384), "rs0")
             ts(R("nx", 0, 1), R("pp", 256, 257), 256.0, ALU.add)
-            copy(R("wa0", 256, 1280), R("ixi"))
-            send_stored(t)
-            iota(R("ws", 256, 1536), [[0, 1280]], -1, 0)
+            copy(half("s16", 1), pn(128, 256))
+            mm(R("pr", 0, 128), R("roth"), half("s16", 1), True, True)
+            twins_pe(t)
+            ts(R("su", 384, 512), R("pr", 0, 128), 2048.0, ALU.add)
+            send(R("sin", 384, 512), R("su", 384, 512), "rs1")
+            keep_names("ws", "s")
+            iota(R("ws", 256, 1536), [[0, 1280]], -2050, 0)
             iota(R("wq0", 256, 1280), [[1, 1024]], 0, 0)
             iota(R("wq0", 1280, 1536), [[1, 256]], 0, 0)
-            lock_base(t)
+            lock_base(t, 1)
+            lock_base(t, 0)
             twins_v(t)
+            lock_twins(t, 1)
+            lock_twins(t, 0)
             list_base(t)
-            copy(R("wa1", 256, 1536), R("wa0", 256, 1536), "s")
-            copy(R("wa0", 0, 256), ind(R("wa0", 256, 1536), R("ou")), "s")
+            firsts(1)
+            firsts(0)
+            lock_list(1)
+            lock_list(0)
         else:
-            names(t, {SEND_AT: [send_stored], 7: [twins_v]} if SEND_AT >= 0 else {7: [twins_v]})
-            kinds(t)
-            for b in range(PRE_VALUES):
-                values(t, b)
-            copy(R("ws", 0, 256), R("pn", 0, 256), "s")
-            if CARRY_LATE:
-                carry(t - 1)
+            digits(128, 160, "s")
+            digits(160, 192, "v")
+            names(2)
+            digits(192, 224, "s")
+            digits(224, 256, "v")
+            names(3)
+            digits(0, 32, "s")
+            digits(64, CUT, "s")
+            twins_v(t)
+            lock_twins(t, 1)
+            kinds(t, 1)
+            lock_base(t, 0)
+            lock_twins(t, 0)
+            digits(32, 64, "v")
+            names(0)
+            firsts(1)
+            rest_names(16)
+            lock_list(1)
         locks(t)
         lookups(t)
         for b in range(early(t), 8):
             values(t, b)
+            if t > 1 and b == (KEEP_AT if t < NR else min(KEEP_AT, 7)):
+                keep_names("ws", "s")
         decide(t)
         if t == 1:
             iota(R("wq1", 256, 1280), [[1, 1024]], 0, 0)
@@ -423,26 +493,27 @@ def rank_program(g, core, T, topo):
         order_b(t)
         maxima(t, "b")
         order_c(t)
-        copy(R("s32", 0, 256), ind(R("ws"), R("ou")), "s")
         if t == NR:
-            add("y", lambda e: e.dma_start(T.yd[:], T.s32[:, 0:256]), [], [R("s32", 0, 256)], dma="dyd")
             maxima(t, "c")
             wrap(t)
+            ts(R("s32", 0, 256), ind(R("ws"), R("ou")), 2048.0, ALU.add, -1.0, ALU.max)
+            add("y", lambda e: e.dma_start(T.yd[:], T.s32[:, 0:256]), [], [R("s32", 0, 256)], dma="dyd")
             write(t)
             add("y", lambda e: e.dma_start(T.yx[:], T.xs[:, 0:4096]), [], [R("xs", 0, 4096)], dma="dyx")
         if t < NR:
+            copy(R("wa%d" % (t % 2), 0, 256), ind(R("wa%d" % ((t - 1) % 2)), R("ou")), "s")
+            if t > 1 and KEEP_AT == 8:
+                keep_names("ws", "s")
+            copy(R("s32", 0, 256), ind(R("ws"), R("ou")), "s")
             turn_stored(t + 1)
-            twins_pe(t + 1)
-            lock_base(t + 1)
-            list_base(t + 1)
             maxima(t, "c")
-            copy(R("at"), ind(R("wa%d" % ((t - 1) % 2)), R("ou")))
+            twins_pe(t + 1)
+            lock_base(t + 1, 1)
             wrap(t)
-            if SEND_AT < 0:
-                send_stored(t + 1)
+            copy(R("at"), R("wa%d" % (t % 2), 0, 256))
             write(t)
-        if t == NR or not CARRY_LATE:
-            carry(t)
+            send_stored(t + 1)
+        carry(t)
     ql = "wq%d" % (NR % 2)
     add("s", lambda e: e.dma_start(T.yq[:], T[ql][0:128:16, 0:256]), [], [R(ql, 0, 256)], dma="dyq")
 

@@ -3,71 +3,174 @@ from concourse.mybir import AluOpType as ALU, ActivationFunctionType as ACT
 W = 16384.0
 NR = 7
 LOW = 32
+TAG = 17
+BASE = 64.0
+ROUND = 12582912.0
+SPARE = 2048.0 - 2 * W
+SLOT = 288
+SHIP = 4
+SEGS = [(192, 256), (128, 192), (64, 128), (0, 64)]
+PARTS = [(0, 8), (8, 16)]
+NAMES = [("s", 224, 256), ("v", 192, 224), ("s", 144, 192), ("v", 128, 144), ("s", 80, 128), ("v", 64, 80),
+         ("s", 16, 64), ("v", 0, 16)]
+FIRST_NAMES = [("sv"[j % 2], 32 * j, 32 * j + 32) for j in range(8)]
+LOOKS = [[("s", 0, 4), ("v", 4, 8), ("s", 8, 12), ("v", 12, 16)],
+         [("s", 0, 4), ("s", 4, 8), ("v", 8, 10), ("s", 10, 14), ("s", 14, 16)]]
+MAXIMA = [[0, 4, 8, 12, 16], [0, 4, 8, 10, 14, 16]]
+AT_CUTS = [(0, 256)]
+MOVES = {"at": "s", "s16": "s", "wx": "s", "wq": "s", "keep": "s", "su": "s", "r16": "s", "copy": "s", "orow": "s", "nd": "s",
+         "fill": "v"}
+CYC, WAKE, HOP, PE = 0.83e-3, 0.165, 2.45, 0.42e-3
+GATHER, SCATTER = 1.56, 3.8
+PASSES = 2
+SHIP_LAT = 4.0
+IDX_AFTER = 3
+EARLY = [2.0, 0.0]
 
 SCRATCH = {
-    "xs": ("sbuf", [128, 4096 + 256], "bfloat16"),
-    "ixi": ("sbuf", [128, 1024], "int32"),
+    "xs": ("sbuf", [128, 4096 + 256], "bfloat16"), "xr": ("sbuf", [128, 2048], "bfloat16"),
+    "pk": ("sbuf", [128, 2048], "bfloat16"), "hi": ("sbuf", [128, 2048], "bfloat16"), "id16": ("sbuf", [128, 128], "bfloat16"),
+    "r256": ("sbuf", [128, 128], "bfloat16"), "i256": ("sbuf", [128, 128], "bfloat16"),
+    "rp": ("sbuf", [128, LOW + 4096 + 256], "float32"),
     "qi": ("sbuf", [128, 272], "int32"),
     "qf": ("sbuf", [128, 272], "float32"),
-    "wa0": ("sbuf", [128, 1536], "float32"), "wa1": ("sbuf", [128, 1536], "float32"),
-    "wq0": ("sbuf", [128, 1536], "float32"), "wq1": ("sbuf", [128, 1536], "float32"),
-    "ws": ("sbuf", [128, 1536], "float32"),
-    "lt": ("sbuf", [128, LOW + 4096 + 256], "float32"),
-    "g1": ("sbuf", [128, 4096], "bfloat16"), "g2": ("sbuf", [128, 4096], "bfloat16"),
-    "lg": ("sbuf", [128, 4096], "bfloat16"), "mx": ("sbuf", [128, 4096], "bfloat16"),
-    "d1": ("sbuf", [128, 4096], "bfloat16"),
-    "wn": ("sbuf", [128, 2048], "bfloat16"),
-    "at": ("sbuf", [128, 256], "uint16"),
-    "su": ("sbuf", [128, 2048], "uint16"), "sin": ("sbuf", [128, 2048], "uint16"),
-    "osn": ("sbuf", [128, 128], "uint16"), "oin": ("sbuf", [128, 128], "uint16"),
-    "s32": ("sbuf", [128, 272], "float32"), "s16": ("sbuf", [128, 272], "float16"),
-    "df": ("sbuf", [128, 256], "bfloat16"), "ne": ("sbuf", [128, 256], "bfloat16"),
-    "wv": ("sbuf", [128, 256], "bfloat16"),
-    "hh": ("sbuf", [128, 272], "float32"),
-    "m1": ("sbuf", [128, 256], "float32"), "m3": ("sbuf", [128, 256], "float32"), "m4": ("sbuf", [128, 256], "float32"),
-    "mo": ("sbuf", [128, 256], "float32"), "orow": ("sbuf", [128, 256], "float32"),
-    "lo": ("sbuf", [128, 32], "uint16"), "du": ("sbuf", [128, 16], "uint16"), "ou": ("sbuf", [128, 16], "uint16"),
+    "wx": ("sbuf", [128, 1792], "int32"), "wq": ("sbuf", [128, 1792], "float32"), "ws": ("sbuf", [128, 1792], "float32"),
+    "g1": ("sbuf", [128, 4096], "bfloat16"), "g2": ("sbuf", [128, 4096], "float16"),
+    "mx": ("sbuf", [128, 4096], "bfloat16"), "d1": ("sbuf", [128, 1024], "float16"),
+    "wn": ("sbuf", [128, 2048], "bfloat16"), "ea": ("sbuf", [128, 2048], "float16"),
+    "at": ("sbuf", [128, 256], "uint16"), "su": ("sbuf", [128, 256], "uint16"),
+    "sb": ("sbuf", [128, NR * SLOT], "uint16"), "rb": ("sbuf", [128, NR * SLOT], "uint16"),
+    "s32": ("sbuf", [128, 256], "float32"), "s16": ("sbuf", [128, 272], "float16"),
+    "df": ("sbuf", [128, 256], "bfloat16"), "ne": ("sbuf", [128, 256], "bfloat16"), "nec": ("sbuf", [128, 128], "bfloat16"),
+    "hh": ("sbuf", [128, 272], "float32"), "hv": ("sbuf", [128, 256], "float32"), "n32": ("sbuf", [128, 256], "float32"),
+    "ec": ("sbuf", [128, NR * 256], "float32"),
+    "r16": ("sbuf", [128, 256], "float16"), "wt": ("sbuf", [128, 256], "bfloat16"),
+    "bd": ("sbuf", [128, 256], "float32"), "yy": ("sbuf", [128, 256], "float32"),
+    "si": ("sbuf", [128, 256], "int32"), "sj": ("sbuf", [128, 256], "int32"),
+    "m1": ("sbuf", [128, 512], "float32"), "m4": ("sbuf", [128, 256], "float32"),
+    "mo": ("sbuf", [128, 256], "float32"), "orow": ("sbuf", [128, 512], "float32"),
+    "lo": ("sbuf", [128, 16], "uint16"), "du": ("sbuf", [128, 16], "uint16"), "ou": ("sbuf", [128, 32], "uint16"),
+    "n0": ("sbuf", [128, 16], "uint16"), "lmx": ("sbuf", [128, 16], "uint16"),
     "ff": ("sbuf", [128, 64], "bfloat16"), "uu": ("sbuf", [128, 64], "bfloat16"), "tt": ("sbuf", [128, 48], "bfloat16"),
     "old": ("sbuf", [128, 16], "float32"), "oldr": ("sbuf", [128, 16], "float32"), "kth": ("sbuf", [128, 16], "float32"),
     "tl": ("sbuf", [128, 16], "float32"), "tl2": ("sbuf", [128, 16], "float32"), "om": ("sbuf", [128, 16], "float32"),
+    "ml": ("sbuf", [128, 16], "float32"), "mk": ("sbuf", [128, 16], "float32"), "lf": ("sbuf", [128, 16], "float32"),
     "c1": ("sbuf", [128, 4], "float32"), "cw": ("sbuf", [128, 4], "float32"), "nx": ("sbuf", [128, 4], "float32"),
     "ci": ("sbuf", [128, 32], "int32"), "cj": ("sbuf", [128, 32], "int32"), "cf": ("sbuf", [128, 32], "float32"),
     "col": ("sbuf", [128, 16], "float32"),
-    "wk": ("sbuf", [128, 64], "float32"), "bi": ("sbuf", [128, 128], "float32"),
-    "irow": ("sbuf", [128, 256], "float32"), "arow": ("sbuf", [128, 256], "float32"), "grow": ("sbuf", [128, 128], "float32"),
+    "wk": ("sbuf", [128, 64], "float32"), "wa": ("sbuf", [128, 16], "float32"),
+    "irow": ("sbuf", [128, 256], "float32"), "arow": ("sbuf", [128, 256], "float32"), "brow": ("sbuf", [128, 256], "float32"),
+    "jrow": ("sbuf", [128, 768], "float32"), "grow": ("sbuf", [128, 128], "float32"),
     "e8": ("sbuf", [128, 128], "float32"), "b8": ("sbuf", [128, 8], "float32"),
     "one1": ("sbuf", [128, 128], "bfloat16"), "onew": ("sbuf", [128, 128], "bfloat16"), "oner": ("sbuf", [128, 128], "bfloat16"),
     "oneb": ("sbuf", [128, 128], "bfloat16"), "onef": ("sbuf", [128, 128], "bfloat16"), "rotb": ("sbuf", [128, 128], "bfloat16"),
     "idn": ("sbuf", [128, 128], "bfloat16"), "idw": ("sbuf", [128, 128], "bfloat16"),
-    "sel": ("sbuf", [128, 128], "float32"), "selr": ("sbuf", [128, 128], "float32"), "rot": ("sbuf", [128, 128], "float32"),
-    "selh": ("sbuf", [128, 128], "float16"), "roth": ("sbuf", [128, 128], "float16"),
+    "sel": ("sbuf", [128, 128], "float16"), "selr": ("sbuf", [128, 128], "float16"),
+    "rot": ("sbuf", [128, 128], "float16"), "idh": ("sbuf", [128, 128], "float16"),
     "tle": ("sbuf", [128, 128], "bfloat16"), "tgt": ("sbuf", [128, 128], "bfloat16"), "tmp": ("sbuf", [128, 128], "bfloat16"),
-    "sgn": ("sbuf", [128, 256], "bfloat16"), "sgh": ("sbuf", [128, 256], "bfloat16"),
+    "sgn": ("sbuf", [128, 64], "bfloat16"), "sg2": ("sbuf", [128, 256], "bfloat16"),
     "dgm": ("sbuf", [128, 272], "bfloat16"), "nd": ("sbuf", [128, 272], "bfloat16"),
     "ko": ("sbuf", [128, 256], "bfloat16"), "ko1": ("sbuf", [128, 256], "bfloat16"), "ko2": ("sbuf", [128, 256], "bfloat16"),
-    "rs": ("sbuf", [128, 256], "float32"), "off": ("sbuf", [128, 64], "bfloat16"),
+    "eb": ("sbuf", [128, 256], "float32"), "ge": ("sbuf", [128, 256], "float32"),
+    "kc": ("sbuf", [128, 256], "float16"), "lift": ("sbuf", [128, 256], "float16"),
+    "rs": ("sbuf", [128, 256], "float32"), "rs2": ("sbuf", [128, 512], "float32"), "off": ("sbuf", [128, 64], "bfloat16"),
     "iw": ("sbuf", [128, 16], "float32"), "iwo": ("sbuf", [128, 16], "float32"),
-    "pn": ("psum", [128, 512], "float32"), "z1": ("psum", [128, 512], "float32"),
-    "z3": ("psum", [128, 512], "float32"), "z4": ("psum", [128, 512], "float32"), "ph": ("psum", [128, 512], "float32"),
-    "pr": ("psum", [128, 512], "float32"), "pp": ("psum", [128, 512], "float32"), "pd": ("psum", [128, 512], "float32"),
+    "pa": ("psum", [128, 512], "float32"), "pb": ("psum", [128, 512], "float32"),
+    "za": ("psum", [128, 512], "float32"), "zb": ("psum", [128, 512], "float32"),
+    "da": ("psum", [128, 512], "float32"), "db": ("psum", [128, 512], "float32"),
+    "ph": ("psum", [128, 512], "float32"), "pd": ("psum", [128, 512], "float32"),
 }
 PSUM = [k for k, v in SCRATCH.items() if v[0] == "psum"]
-SEMAPHORES = (["ev", "es", "et", "eg", "sent", "dq", "dc", "di", "dx", "dyx", "dyq", "dyd"]
-              + ["rs%d" % t for t in range(NR + 1)] + ["ro%d" % t for t in range(1, NR + 1)])
+SEMAPHORES = (["ev", "es", "et", "eg", "sent", "dq", "dc", "di", "dw", "dyx", "dyq", "dyd"]
+              + ["dx%d" % j for j in range(SHIP)] + ["rx%d" % j for j in range(SHIP)]
+              + ["ro%d_%d" % (t, j) for t in range(1, NR + 1) for j in range(len(PARTS))])
 ESEM = {"v": "ev", "s": "es", "t": "et", "g": "eg"}
+PLAN = {}
 
-LOCK_PLAN = "vsvsvsvsvsvsvsvs"
-EARLY_VALUES = 4
-HEADS = {2: [(0, 2)], 3: [(2, 4)], 4: [(4, 5)], 5: [(5, 6)], 6: [(6, 7)], 7: [(7, 8)]}
-FIRST_HEADS = {2: [(0, 3)], 4: [(3, 4)], 6: [(4, 6)], 7: [(6, 8)]}
-FIRST_VALUES = 3
-FIRST_MAX = {"l15": 6, "b": 8, "o": 12, "c": 16}
-KEEP_AT = 8
-CUT = 120
-PIECES = {16: (120, 128)}
-LOW_AT = (12, 10, 9, 6, 5, 4)
-MAX_PLAN = {"s3": 1, "s2": 2, "s1": 3, "l15": 8, "a": 10, "o": 12, "c": 16}
-SPARE = 2048.0 - 2 * W
+
+def meet(a, b):
+    if a[0] != b[0] or a[1] >= b[2] or b[1] >= a[2]:
+        return False
+    return a[3] != b[3] or a[3] == 1 or (a[1] - b[1]) % a[3] == 0
+
+
+def banks(o):
+    return set(r[0] for r in o["rd"] + o["wr"] if r[0] in PSUM)
+
+
+def clash(o, p):
+    return any(meet(a, b) for a in o["rd"] for b in p["wr"]) or any(meet(a, b) for a in o["wr"] for b in p["wr"] + p["rd"])
+
+
+def plan(ops):
+    n = len(ops)
+    pred, anc, byname, bysem, last = [], [], {}, {}, {}
+    for i, o in enumerate(ops):
+        cand = set()
+        for r in o["rd"] + o["wr"]:
+            cand.update(byname.get(r[0], []))
+        bk, edges = banks(o), {}
+        for m in cand:
+            p = ops[m]
+            if p["dma"] == "remote":
+                continue
+            both = p["q"] == o["q"]
+            if clash(o, p) or (bk & banks(p) and (not both or o["q"] == "t")):
+                edges[m] = 0.0 if both and o["q"] == "t" else p["lat"] + WAKE
+        for name, val in o["ext"]:
+            for m in bysem[name]:
+                edges[m] = ops[m]["lat"] + WAKE
+        if o["dma"] or o["q"] == "g":
+            if o["q"] in last:
+                edges.setdefault(last[o["q"]], 0.0)
+            last[o["q"]] = i
+        keep, seen = {}, 0
+        for m in sorted(edges, reverse=True):
+            if not seen >> m & 1 or ops[m]["lat"]:
+                keep[m] = edges[m]
+                seen |= anc[m]
+        pred.append(keep)
+        anc.append(seen | 1 << i)
+        for r in o["rd"] + o["wr"]:
+            byname.setdefault(r[0], []).append(i)
+        for name in o["sems"]:
+            bysem.setdefault(name, []).append(i)
+    succ = [{} for o in ops]
+    for i in range(n):
+        for m, d in pred[i].items():
+            succ[m][i] = d
+    cost = [o["cost"] for o in ops]
+
+    def place(turn, before, first):
+        busy = {q: [] for q in "vstgy"}
+        start = [0.0] * n
+        for i in turn:
+            at = max([start[m] + cost[m] + d for m, d in before[i].items()] + [first[i]])
+            b = busy[ops[i]["q"]]
+            lo, hi = 0, len(b)
+            while lo < hi:
+                mid = (lo + hi) // 2
+                lo, hi = (mid + 1, hi) if b[mid][1] <= at else (lo, mid)
+            while lo < len(b) and b[lo][0] < at + cost[i] - 1e-9:
+                at = b[lo][1]
+                lo += 1
+            start[i] = at
+            b.insert(lo, (at, at + cost[i]))
+        return start
+
+    tail = [o["lat"] if not succ[i] else 0.0 for i, o in enumerate(ops)]
+    way = list(tail)
+    best = None
+    for again in range(PASSES):
+        for i in range(n - 1, -1, -1):
+            way[i] = max([way[i] + ops[i]["lead"] + (0 if again else cost[i])] + [cost[i] + d + way[j] for j, d in succ[i].items()])
+        start = place(sorted(range(n), key=lambda i: (-way[i], i)), pred, [0.0] * n)
+        span = max(start[i] + cost[i] + tail[i] for i in range(n))
+        if best is None or span < best[0]:
+            best = (span, start)
+        back = place(sorted(range(n), key=lambda i: (-start[i] - cost[i], -i)), succ, tail)
+        way = [back[i] + cost[i] for i in range(n)]
+    return sorted(range(n), key=lambda i: (best[1][i], i))
 
 
 def rank_program(g, core, T, topo):
@@ -75,9 +178,11 @@ def rank_program(g, core, T, topo):
     if rank is None:
         return
     nxt = T.cores[(rank + 1) % len(T.cores)]
-    rid, pid = topo.addr(nxt)[0], topo.addr(nxt)[1]
-    mask = topo.mask(core, nxt)
+    prv = T.cores[(rank - 1) % len(T.cores)]
     neng = len(topo.engines(core, nxt))
+    nback = len(topo.engines(core, prv))
+    nin = len(topo.engines(prv, core))
+    ncopy = len(topo.engines(nxt, core))
     Q = {"v": g.vector, "s": g.scalar, "t": g.tensor, "g": g, "y": g.sync}
     ops = []
 
@@ -99,7 +204,20 @@ def rank_program(g, core, T, topo):
     def ind(win, off):
         return ("ind", win, off)
 
-    def add(q, fn, outs, ins, dma=None, ext=None):
+    def cols(r):
+        return 16 * cols(r[2]) if len(r) == 3 else len(range(r[1], r[2], r[3]))
+
+    def narrow(*rs):
+        return all(SCRATCH[r[0]][2] in ("bfloat16", "float16", "uint16") for r in rs)
+
+    def price(o, i, per=None):
+        if len(o) == 3:
+            return 0.05 + CYC * SCATTER * cols(o)
+        if len(i) == 3:
+            return 0.06 + CYC * GATHER * cols(o)
+        return CYC * max(64, cols(o) * (per or (0.5 if narrow(o, i) else 1)))
+
+    def add(q, fn, outs, ins, cost, dma=None, ext=None, lat=0.0, sems=()):
         rd, wr = [], []
         for r in ins:
             if isinstance(r, tuple):
@@ -110,50 +228,77 @@ def rank_program(g, core, T, topo):
                     wr.append(r[1]); rd.append(r[2])
                 else:
                     wr.append(r)
-        ops.append({"q": q, "fn": fn, "rd": rd, "wr": wr, "dma": dma, "ext": ext or []})
+        ops.append({"q": q, "fn": fn, "rd": rd, "wr": wr, "dma": dma, "ext": ext or [], "cost": cost, "lat": lat, "sems": sems,
+                    "lead": 0.0})
 
     def copy(o, i, q="v", ext=None):
         if q == "v":
-            add("v", lambda e: e.tensor_copy(A(o), A(i)), [o], [i], ext=ext)
+            add(q, lambda e: e.tensor_copy(A(o), A(i)), [o], [i], price(o, i), ext=ext)
+        elif len(o) == 3:
+            add(q, lambda e: e.activation(A(o), A(i), ACT.Silu), [o], [i], price(o, i), ext=ext)
         else:
-            add("s", lambda e: e.activation(A(o), A(i), ACT.Copy), [o], [i], ext=ext)
+            add(q, lambda e: e.activation(A(o), A(i), ACT.Copy), [o], [i], price(o, i, 1), ext=ext)
+
+    def shift(o, i, c, q, floor=False, ext=None):
+        if q == "v":
+            add(q, lambda e: e.tensor_scalar(A(o), A(i), A(c), None, ALU.add), [o], [i, c], price(o, i), ext=ext)
+        else:
+            add(q, lambda e: e.activation(A(o), A(i), ACT.Relu if floor else ACT.Identity, bias=A(c), scale=1.0), [o], [i, c],
+                price(o, i, 1), ext=ext)
 
     def ts(o, i, s1, op0, s2=None, op1=None):
         if op1 is None:
-            add("v", lambda e: e.tensor_scalar(A(o), A(i), A(s1), None, op0), [o], [i, s1])
+            add("v", lambda e: e.tensor_scalar(A(o), A(i), A(s1), None, op0), [o], [i, s1], price(o, i))
         else:
-            add("v", lambda e: e.tensor_scalar(A(o), A(i), A(s1), A(s2), op0, op1), [o], [i, s1, s2])
+            add("v", lambda e: e.tensor_scalar(A(o), A(i), A(s1), A(s2), op0, op1), [o], [i, s1, s2], price(o, i))
 
-    def tt(o, a, b, op, ext=None):
-        add("v", lambda e: e.tensor_tensor(A(o), A(a), A(b), op), [o], [a, b], ext=ext)
+    def tt(o, a, b, op):
+        add("v", lambda e: e.tensor_tensor(A(o), A(a), A(b), op), [o], [a, b], price(o, a, 1 if b[0] in PSUM else 2))
 
     def scan(o, d0, d1, init, op0, op1):
-        add("v", lambda e: e.tensor_tensor_scan(A(o), A(d0), A(d1), init, op0, op1), [o], [d0, d1])
+        add("v", lambda e: e.tensor_tensor_scan(A(o), A(d0), A(d1), init, op0, op1), [o], [d0, d1],
+            price(o, d0, 0.5 if narrow(o, d0, d1) else 1))
 
     def act(o, i, func, bias=0.0, scale=1.0):
-        add("s", lambda e: e.activation(A(o), A(i), func, bias=A(bias), scale=A(scale)), [o], [i, bias, scale])
+        add("s", lambda e: e.activation(A(o), A(i), func, bias=A(bias), scale=A(scale)), [o], [i, bias, scale], price(o, i, 1))
 
     def mset(o, c):
-        add("v", lambda e: e.memset(A(o), c), [o], [])
+        add("v", lambda e: e.memset(A(o), c), [o], [], price(o, o))
 
     def mm(o, l, r, start, stop):
-        add("t", lambda e: e.matmul(A(o), A(l), A(r), start, stop), [o], [l, r])
+        add("t", lambda e: e.matmul(A(o), A(l), A(r), start, stop), [o], [l, r], PE * max(64, cols(r)) * (1 if narrow(r) else 4))
 
     def iota(o, pat, base, cm):
+        cost = 0.13 + 2 * CYC * cols(o)
         if SCRATCH[o[0]][2] == "int32":
-            add("g", lambda e: e.iota(A(o), pat, base, cm), [o], [])
+            add("g", lambda e: e.iota(A(o), pat, base, cm), [o], [], cost)
         else:
-            add("g", lambda e: e.iota(A(o), pat, base, cm, allow_small_or_imprecise_dtypes=True), [o], [])
+            add("g", lambda e: e.iota(A(o), pat, base, cm, allow_small_or_imprecise_dtypes=True), [o], [], cost)
 
-    def send(dst, src, sem):
-        add("g", lambda e: e.remote_dma(A(dst), A(src), T.sem[sem], T.sem["sent"], pid, rid, mask), [], [src], dma="remote")
+    def send(to, dst, src, sem, local, lat):
+        rid, pid = topo.addr(to)[0], topo.addr(to)[1]
+        add("g", lambda e: e.remote_dma(A(dst), A(src), T.sem[sem], T.sem[local], pid, rid, topo.mask(core, to)), [], [src],
+            0.5, dma="remote", lat=lat, sems=(sem, local))
+
+    def load(q, dst, src, sem, lat):
+        add(q, lambda e: e.dma_start(A(dst), src), [dst], [], 0.1, dma=sem, lat=lat)
+
+    def store(q, dst, src, region, sem, lat):
+        add(q, lambda e: e.dma_start(dst, src), [], [region], 0.1, dma=sem, lat=lat)
 
     def col(j):
         return R("col", j, j + 1)
 
-    add("s", lambda e: e.dma_start(T.qi[0:8, 0:256], T.que[:]), [R("qi", 0, 256)], [], dma="dq")
-    add("y", lambda e: e.dma_start(T.ixi[:, :], T.idx[:]), [R("ixi")], [], dma="di")
-    add("y", lambda e: e.dma_start(T.xs[:, 0:4096], T.rec[:]), [R("xs", 0, 4096)], [], dma="dx")
+    piece = 4096 // SHIP
+    load("s", R("qi", 0, 256, 1, 8), T.que[:], "dq", 2.0)
+    due = 1.7
+    for j in range(SHIP):
+        due += 5.2 / SHIP
+        load("y", R("xs", piece * j, piece * j + piece), T.rec[:, piece * j:piece * j + piece], "dx%d" % j, due)
+        if j == IDX_AFTER:
+            due += 2.6
+            load("y", R("wx", 256, 1280), T.idx[:], "di", due)
+    load("y", R("wx", 1280, 1536), T.idx[:, 0:256], "dw", due + 0.7)
 
     iota(R("ci", 0, 16), [[-1, 16]], 16, 1)
     iota(R("ci", 16, 19), [[16, 3]], 0, 1)
@@ -161,19 +306,17 @@ def rank_program(g, core, T, topo):
     iota(R("e8", 0, 128, 1, 8), [[1, 8], [0, 16]], 0, -1)
     iota(R("grow"), [[16, 8], [0, 16]], 0, 0)
     iota(R("irow"), [[1, 256]], 0, 0)
-    iota(R("bi"), [[-256, 8], [16, 16]], -255, 0)
-    add("g", lambda e: e.dma_start(T.qi[0:8, 256:257], T.cur[:], allow_slow_non_contiguous=True), [R("qi", 256, 257)], [], dma="dc")
-    iota(R("lt"), [[0, LOW + 4096 + 256]], 0, 0)
-
+    iota(R("brow"), [[1, 16], [0, 16]], 0, 0)
     mset(R("wn"), 0.0)
-    copy(R("d1", 0, 2048), R("wn"), "s")
-    copy(R("d1", 2048, 4096), R("wn"), "s")
+    copy(R("ea"), R("wn"), "s")
+    copy(R("d1"), R("wn", 0, 1024), "s")
     ts(R("ci", 18, 19), R("ci", 18, 19), 80.0, ALU.add)
     ts(R("cj", 0, 17), R("ci", 0, 17), 15, ALU.bitwise_and)
     copy(col(0), R("ci", 16, 17))
     ts(R("cj", 17, 19), R("ci", 17, 19), 127, ALU.bitwise_and)
     ts(R("cj", 19, 22), R("ci", 16, 19), 112, ALU.bitwise_and)
     mset(R("rs"), -1.0e6)
+    mset(R("rs2"), -1.0e6)
     copy(R("cf", 0, 22), R("cj", 0, 22))
     mset(R("dgm", 256, 272), 0.0)
     copy(R("s16", 256, 272), R("cf", 0, 16))
@@ -181,6 +324,7 @@ def rank_program(g, core, T, topo):
     cg, cgr, cgb = R("cf", 19, 20), R("cf", 20, 21), R("cf", 21, 22)
     ts(col(9), ca, 0.0, ALU.is_equal, -8192.0, ALU.mult)
     ts(col(5), ca, -1.0, ALU.mult)
+    ts(col(6), ca, 16.0, ALU.add)
     ts(R("wk", 0, 16), R("cf", 0, 16), 0.0, ALU.is_equal, 256.0, ALU.mult)
     ts(R("wk", 16, 32), R("cf", 0, 16), 1.0, ALU.is_equal, 16.0, ALU.mult)
     ts(R("wk", 32, 48), R("cf", 0, 16), 2.0, ALU.is_equal)
@@ -189,31 +333,44 @@ def rank_program(g, core, T, topo):
     tt(R("wk", 48, 64), R("wk", 0, 16), R("wk", 16, 32), ALU.add)
     ts(R("e8", 0, 128, 1, 8), R("e8", 0, 128, 1, 8), 0.0, ALU.is_equal)
     copy(R("qf", 0, 256, 1, 8), R("qi", 0, 256, 1, 8))
-    mm(R("pp", 0, 256), R("e8", 0, 128, 1, 8), R("qf", 0, 256, 1, 8), True, True)
+    mm(R("da", 0, 256), R("e8", 0, 128, 1, 8), R("qf", 0, 256, 1, 8), True, True)
     tt(R("ko"), R("ko1"), R("ko2"), ALU.add)
     tt(R("wk", 0, 16), R("wk", 48, 64), R("wk", 32, 48), ALU.add)
     ts(R("b8"), R("grow", 0, 128, 16), cg, ALU.is_equal)
+    ts(R("wa"), R("arow", 0, 16), ca, ALU.is_equal)
     ts(col(8), col(9), -1.0, ALU.mult, -4096.0, ALU.add)
+    ts(col(4), col(8), 0.25 - BASE, ALU.add)
     ts(R("ko", 15, 256, 16), R("ko", 15, 256, 16), col(9), ALU.add)
-    ts(col(7), col(9), 4096.0, ALU.add)
-    act(R("sgn"), R("arow"), ACT.Sign, col(5), 1.0)
+    ts(col(7), col(9), 4096.0 + BASE, ALU.add)
+    act(R("sgn", 0, 16), R("arow", 0, 16), ACT.Sign, col(5), 1.0)
     for k in range(16):
         act(R("wn", 129 * k, 128 * k + 128, 16), R("b8"), ACT.Identity, 0.0, R("wk", k, k + 1))
-    act(R("sgh"), R("sgn"), ACT.Identity, -2.0, 0.5)
+    mset(R("sg2"), 1.0)
+    for h in range(0, 256, 64):
+        mset(R("sg2", h + 32, h + 48), -2.5)
+        act(R("sg2", h + 16, h + 32), R("sgn", 0, 16), ACT.Identity, -2.0, 0.5)
+        act(R("sg2", h + 48, h + 64), R("sgn", 0, 16), ACT.Identity, -2.0, 0.5)
     ts(R("dgm", 0, 256), R("arow"), ca, ALU.is_equal, -2.0, ALU.mult)
-    scan(R("mo"), R("pp", 0, 256), R("ko"), -1.0, ALU.max, ALU.add)
+    scan(R("mo"), R("da", 0, 256), R("ko"), -1.0, ALU.max, ALU.add)
     act(R("nd"), R("dgm"), ACT.Identity, 1.0, 0.5)
-    copy(R("wq0", 0, 256), R("pp", 0, 256), "s")
+    copy(R("wq", 0, 256), R("da", 0, 256), "s")
+    for k in range(16):
+        act(R("ea", 129 * k, 128 * k + 128, 16), R("b8"), ACT.Identity, 0.0, R("wa", k, k + 1))
     ts(R("rot"), R("irow", 0, 128), cpr, ALU.is_equal)
-    ts(R("ou"), R("mo", 15, 256, 16), col(8), ALU.add)
+    ts(R("ou", 0, 16), R("mo", 15, 256, 16), col(8), ALU.add)
     ts(R("selr"), R("grow"), cpr, ALU.is_equal)
     ts(R("idw"), R("irow", 0, 128), cp, ALU.is_equal, W, ALU.mult)
     ts(R("onew"), R("grow"), cg, ALU.is_equal, W, ALU.mult)
     ts(R("iw"), R("irow", 0, 256, 16), ca, ALU.add)
-    ts(R("bi"), R("bi"), ca, ALU.add)
+    ts(R("ge"), R("arow"), ca, ALU.is_ge)
     ts(R("rs", 0, 256, 16), R("iw"), SPARE, ALU.add)
-    copy(R("at"), ind(R("ixi"), R("ou")))
+    ts(R("rs2", 0, 512, 32), R("iw"), SPARE, ALU.add)
     ts(R("idn"), R("irow", 0, 128), cp, ALU.is_equal)
+    ts(R("id16"), R("irow", 0, 128), cp, ALU.is_equal, 16.0, ALU.mult)
+    ts(R("i256"), R("irow", 0, 128), cp, ALU.is_equal, 256.0, ALU.mult)
+    ts(R("r256"), R("irow", 0, 128), cpb, ALU.is_equal, 256.0, ALU.mult)
+    ts(R("idh"), R("irow", 0, 128), cp, ALU.is_equal)
+    tt(R("eb"), R("ge"), R("brow"), ALU.add)
     ts(R("sel"), R("grow"), cp, ALU.is_equal)
     ts(R("rotb"), R("irow", 0, 128), cpb, ALU.is_equal)
     ts(R("one1"), R("grow"), cg, ALU.is_equal)
@@ -224,367 +381,316 @@ def rank_program(g, core, T, topo):
     ts(R("iwo"), R("iw"), col(7), ALU.add)
     tt(R("tle"), R("tmp"), R("one1"), ALU.mult)
     mset(R("ff", 0, 33), 0.0)
-    mset(R("kth"), SPARE)
+    mset(R("kth"), 0.0)
     tt(R("tgt"), R("one1"), R("tle"), ALU.subtract)
-    mset(R("d1", 0, 4096, 16), -64.0)
-    copy(R("wa0", 1280, 1536), R("ixi", 0, 256))
-    copy(R("wa1", 1280, 1536), R("wa0", 1280, 1536), "s")
+    for t in range(NR):
+        act(R("ec", 256 * t, 256 * t + 256), R("eb"), ACT.Identity, (16.0 + TAG * t) / 256, -1.0 / 256)
+    for j, c in enumerate((-256.0, 0.0, 1280.0)):
+        shift(R("jrow", 256 * j, 256 * j + 256), R("irow"), BASE + c, "s")
+    if "s" in (MOVES["copy"], MOVES["orow"]):
+        act(R("orow", 0, 16), R("jrow", 256, 272), ACT.Silu)
+        ops[-1]["cost"] += 1.3
+    mset(R("d1", 0, 1024, 16), -64.0)
+    mset(R("d1", 15, 1024, 16), 7.6875)
     mset(R("off"), -2048.0 / W)
-    copy(R("wa0", 0, 256), R("at"))
-    copy(R("s32", 256, 272), R("cf", 0, 16), "s")
-    ts(R("roth"), R("irow", 0, 128), cpr, ALU.is_equal)
-    ts(R("selh"), R("grow"), cpr, ALU.is_equal)
+    ts(R("kc"), R("brow"), -15.5, ALU.add, 1.0 / 256, ALU.mult)
+    mset(R("lift"), 1536.0)
+    mset(R("bd"), 1.0)
+    for j, (c0, c1) in enumerate(PARTS):
+        ts(col(10 + j), ca, 16.0 * (c1 - c0), ALU.mult, 15.0, ALU.add)
+        ts(R("lmx", c0, c1), R("irow", 0, 16 * (c1 - c0), 16), col(10 + j), ALU.add)
+    for o in ops:
+        o["lead"] = 20.0
+    half = piece // 2
+    for j in range(SHIP):
+        z = R(("pa", "pb", "za", "zb")[j % 4], 0, half)
+        mm(z, R("id16"), R("xs", piece * j, piece * j + half), True, False)
+        mm(z, R("idn"), R("xs", piece * j + half, piece * j + piece), False, True)
+        copy(R("pk", half * j, half * j + half), z, "vs"[j % 2])
+        send(prv, R("xr", half * j, half * j + half), R("pk", half * j, half * j + half), "rx%d" % j, "sent", HOP + SHIP_LAT)
+        ops[-1]["lead"] = 30.0
+    add("g", lambda e: e.dma_start(T.qi[0:8, 256:257], T.cur[:], allow_slow_non_contiguous=True), [R("qi", 256, 257)], [],
+        1.5, dma="dc", lat=2.0)
+    copy(R("at"), ind(R("wx", 256, 1280), R("ou", 0, 16)))
+    copy(R("wx", 0, 256), R("at"))
+    iota(R("ws", 256, 1536), [[0, 1280]], -2050, 0)
+    iota(R("wq", 256, 1280), [[1, 1024]], 0, 0)
+    iota(R("wq", 1280, 1536), [[1, 256]], 0, 0)
     copy(R("qf", 256, 257, 1, 8), R("qi", 256, 257, 1, 8))
-    mm(R("pp", 256, 257), R("e8", 0, 128, 1, 8), R("qf", 256, 257, 1, 8), True, True)
+    mm(R("pd", 32, 33), R("e8", 0, 128, 1, 8), R("qf", 256, 257, 1, 8), True, True)
+    ts(R("nx", 0, 1), R("pd", 32, 33), 256.0, ALU.add)
+    for j in range(SHIP):
+        xr, hi, z = R("xr", half * j, half * j + half), R("hi", half * j, half * j + half), R(("db", "da")[j % 2], 0, half)
+        add("v", lambda e, xr=xr, hi=hi: e.tensor_scalar(A(hi), A(xr), -1.0 / 16, 15.0 / 32 - 192, ALU.mult, ALU.add), [hi], [xr],
+            price(hi, xr), ext=[("rx%d" % j, ncopy)])
+        act(R("rp", LOW + piece * j, LOW + piece * j + half), hi, ACT.Identity, BASE - 192, -1.0)
+        mm(z, R("id16"), hi, True, False)
+        mm(z, R("idn"), xr, False, True)
+        shift(R("rp", LOW + piece * j + half, LOW + piece * j + piece), z, BASE + 16 * 192, "vs"[j % 2])
 
-    def pn(lo, hi):
-        return R("pn", lo, hi) if lo < 128 else R("pr", 128 + lo, 128 + hi)
+    RP = R("rp", LOW, LOW + 4096)
 
-    def z1(h):
-        return R("pp", 256, 384) if h else R("z1", 0, 128)
+    def ou(t):
+        return R("ou", 16 * (t % 2), 16 * (t % 2) + 16)
 
-    def half(name, h):
-        return R(name, 128 * h, 128 * h + 128)
+    def pn(b, t=2):
+        return R(("pb", "pa", "pb", "pa")[b] if t > 1 else ("pb", "pa", "zb", "za")[b], 64 * b, 64 * b + 64)
 
-    def digits(lo, hi, q):
-        copy(R("g1", 16 * lo, 16 * hi), ind(R("xs", 0, 4096), R("at", lo, hi)), q)
-
-    def names(b):
-        mm(pn(64 * b, 64 * b + 64), R("idw"), R("off"), True, False)
+    def names(t, b):
+        for q, lo, hi in NAMES if t > 1 else FIRST_NAMES:
+            if lo // 64 == b:
+                copy(R("g1", 16 * lo, 16 * hi), ind(R("xs", 0, 4096), R("at", lo, hi)), q)
+        mm(pn(b, t), R("idw"), R("off"), True, False)
         for k in range(16):
-            mm(pn(64 * b, 64 * b + 64), R("wn", 128 * k, 128 * k + 128), R("g1", 1024 * b + k, 1024 * b + 1024, 16), False, k == 15)
+            mm(pn(b, t), R("wn", 128 * k, 128 * k + 128), R("g1", 1024 * b + k, 1024 * b + 1024, 16), False, k == 15)
 
-    def rest_names(slot):
-        if slot in PIECES:
-            digits(PIECES[slot][0], PIECES[slot][1], "v")
-            if PIECES[slot][1] == 128:
-                names(1)
+    def keep(t, dst, b, q, at=0):
+        copy(R(dst, at + 64 * b, at + 64 * b + 64), pn(b, t), q)
 
-    def keep_names(dst, q):
-        for h in (1, 0):
-            copy(half(dst, h), pn(128 * h, 128 * h + 128), q)
+    def home(t):
+        return 1536 * (t % 2)
 
-    def turn_stored(t):
-        if t % 2:
-            mm(R("pr", 0, 256), R("rot"), stored(t, 256), True, True)
-
-    def stored(t, n):
-        return R("s32" if t > 1 else "s16", 0, n)
+    def moved(name, t):
+        lo = 256 * ((t - 1) % 2)
+        return ind(R(name, lo, lo + 1536), ou(t))
 
     def first_rows(t):
-        return R("selh" if t == 1 else "selr" if t % 2 else "sel")
+        return R("selr" if t % 2 else "sel")
 
-    def send_stored(t):
-        su = R("su", 256 * t, 256 * t + 256)
-        ts(su, R("pr", 0, 256) if t % 2 else R("s32", 0, 256), 2048.0, ALU.add)
-        send(R("sin", 256 * t, 256 * t + 256), su, "rs%d" % t)
+    def ones(t):
+        return R("oner" if t % 2 else "onew")
 
-    def twins_pe(t):
-        mm(R("ph", 0, 272), first_rows(t), stored(t, 272), True, False)
+    def from_stored(t):
+        mm(R("ph", 0, 272), first_rows(t), R("s16"), True, False)
         mm(R("ph", 0, 272), R("idw"), R("dgm"), False, True)
-        mm(R("pd", 256, 512), first_rows(t), stored(t, 256), True, False)
+        mm(R("pd", 256, 512), first_rows(t), R("s16", 0, 256), True, False)
         mm(R("pd", 256, 512), R("onew"), R("dgm", 0, 256), False, True)
-
-    def twins_v(t):
         scan(R("hh"), R("nd"), R("ph", 0, 272), 0.0, ALU.mult, ALU.min)
-        tt(R("ne"), R("hh", 15, 271), R("pd", 256, 512), ALU.not_equal)
+        for h in (1, 0):
+            tt(R("ne", 128 * h, 128 * h + 128), R("hh", 128 * h + 15, 128 * h + 143), R("pd", 128 * h + 256, 128 * h + 384), ALU.not_equal)
+        for p in range(7, -1, -1):
+            ts(R("nec", 16 * p, 16 * p + 16), R("pd", 256 + 32 * p, 272 + 32 * p), R("hh", 32 * p + 31, 32 * p + 32), ALU.not_equal)
+        ts(R("n0"), R("hh", 15, 256, 16), 2 * W + 2048.0, ALU.add)
+        for h in (1, 0):
+            ts(R("hv", 128 * h, 128 * h + 128), ind(RP, R("n0", 8 * h, 8 * h + 8)), ROUND, ALU.add, ROUND, ALU.subtract)
+        for c0, c1 in PARTS:
+            for a in range(16):
+                m = 256 + 16 * c0 + (c1 - c0) * a
+                mm(R("da", m, m + c1 - c0), R("rot" if t % 2 else "idh"), R("s16", 16 * c0 + a, 16 * c1, 16), True, True)
+        shift(R("su"), R("da", 256, 512), 2048.0, MOVES["su"], True)
 
-    def lock_base(t, h):
-        mm(z1(h), first_rows(t), half("s32" if t > 1 else "s16", h), True, False)
-        mm(z1(h), R("idw"), half("sgh", h), False, False)
+    def locks(t, j):
+        lo, hi = SEGS[j]
+        z = "zb" if j % 2 else "za"
+        pairs = range(hi // 32 - 1, lo // 32 - 1, -1)
 
-    def lock_twins(t, h):
-        mm(z1(h), R("idw"), half("ne", h), False, t == 1)
+        def both(l, name, last):
+            for p in pairs:
+                mm(R(z, 64 * p + 16, 64 * p + 32), l, R(name, 32 * p, 32 * p + 16), False, False)
+                mm(R(z, 64 * p + 32, 64 * p + 64), l, R(name, 32 * p, 32 * p + 32), False, last and p == lo // 32)
 
-    def list_base(t):
-        mm(R("z3", 0, 256), first_rows(t), stored(t, 256), True, False)
-        mm(R("z3", 0, 256), R("idw"), R("dgm", 0, 256), False, False)
+        mm(R(z, 2 * lo, 2 * hi), R("idw"), R("sg2", 0, 2 * (hi - lo)), True, False)
+        for p in pairs:
+            mm(R(z, 64 * p + 16, 64 * p + 32), R("idw"), R("ne", 32 * p, 32 * p + 16), False, False)
+            mm(R(z, 64 * p + 32, 64 * p + 48), R("idw"), R("nec", 16 * p, 16 * p + 16), False, False)
+            mm(R(z, 64 * p + 48, 64 * p + 64), R("idw"), R("ne", 32 * p + 16, 32 * p + 32), False, False)
+        both(first_rows(t), "s16", t == 1)
         if t > 1:
-            mm(R("z4", 0, 256), R("idw"), R("dgm", 0, 256), True, False)
+            for b in range((hi - 1) // 64, lo // 64 - 1, -1):
+                x0, x1 = max(lo, 64 * b), min(hi, 64 * b + 64)
+                tt(R("df", x0, x1), R("s16", x0, x1), R(pn(b)[0], x0, x1), ALU.not_equal)
+            both(ones(t), "df", True)
+        scan(R("m1", 2 * lo, 2 * hi), R("rs2", 2 * lo, 2 * hi), R(z, 2 * lo, 2 * hi), -1.0e6, ALU.max, ALU.min)
+        ts(R("lo", lo // 16 + 1, hi // 16, 2), R("m1", 2 * lo + 63, 2 * hi, 64), 4096.0 - SPARE + LOW, ALU.add, col(6), ALU.max)
+        ts(R("lo", lo // 16, hi // 16, 2), R("m1", 2 * lo + 31, 2 * hi, 64), 4096.0 - SPARE + LOW, ALU.add, ca, ALU.max)
+        for p in pairs:
+            tt(ind(R("rp"), R("lo", 2 * p, 2 * p + 2)), R("hv", 32 * p, 32 * p + 32),
+               R("ec", 256 * (t - 1) + 32 * p, 256 * (t - 1) + 32 * p + 32), ALU.add)
 
-    def kinds(t, h):
-        one = R("oner") if t % 2 else R("onew")
-        tt(half("df", h), half("s32", h), pn(128 * h, 128 * h + 128), ALU.not_equal)
-        mm(z1(h), one, half("df", h), False, True)
-        if h == 0:
-            list_base(t)
-            mm(R("z4", 0, 256), one, R("df"), False, True)
-            mm(R("z3", 0, 256), one, R("df"), False, False)
+    def kinds(t):
+        if t > 1:
+            mm(R("db", 256, 512), R("idw"), R("dgm", 0, 256), True, False)
+            mm(R("db", 256, 512), ones(t), R("df"), False, True)
+            for h in (0, 128):
+                scan(R("m4", h, h + 128), R("rs", h, h + 128), R("db", h + 256, h + 384), -1.0e6, ALU.max, ALU.min)
+            tt(R("ff", 17, 33), R("m4", 15, 256, 16), R("old"), ALU.is_ge)
+            ts(R("kth"), R("ff", 17, 33), -1.0e6, ALU.mult)
+        tt(R("bd", 15, 256, 16), R("m1", 31, 512, 32), R("rs", 0, 256, 16), ALU.subtract)
+        ts(R("ml"), R("m1", 31, 512, 32), -SPARE, ALU.add)
+        ts(R("lf"), R("m1", 31, 512, 32), 4096.0 - SPARE, ALU.add)
+        tt(R("mk"), R("ml"), R("kth"), ALU.add)
 
-    def firsts(h):
-        scan(half("m1", h), half("rs", h), z1(h), -1.0e6, ALU.max, ALU.min)
+    def part(name, j):
+        return R(name, 16 * PARTS[j][0], 16 * PARTS[j][1])
 
-    def lock_list(h):
-        ts(R("lo", 16 * h, 16 * h + 16, 2), R("m1", 128 * h + 15, 128 * h + 128, 16), 4096.0 - SPARE + LOW, ALU.add, ca, ALU.max)
+    def slot(name, t, j):
+        at = SLOT * (t - 1) + sum(16 + 16 * (c1 - c0) for c0, c1 in PARTS[:j])
+        n = PARTS[j][1] - PARTS[j][0]
+        return R(name, at, at + n), R(name, at + n, at + 17 * n), R(name, at, at + 17 * n)
 
-    def locks(t):
-        for c in range(15, -1, -1):
-            ts(ind(R("lt"), R("lo", 2 * c, 2 * c + 1)), R("irow", 16 * c, 16 * c + 16), -1.0, ALU.mult, 256.0 * t + 255.0, ALU.add)
-            if t > 1:
-                rest_names(c)
-            if t > 1 and c == LOW_AT[0]:
-                kinds(t, 0)
-            if t > 1 and c == LOW_AT[1]:
-                firsts(0)
-            if t > 1 and c == LOW_AT[2]:
-                lock_list(0)
-            if t > 1 and c == LOW_AT[3]:
-                scan(R("m4"), R("rs"), R("z4", 0, 256), -1.0e6, ALU.max, ALU.min)
-            if t > 1 and c == LOW_AT[4]:
-                tt(R("ff", 17, 33), R("m4", 15, 256, 16), R("oldr") if t % 2 else R("old"), ALU.is_ge)
-            if t > 1 and c == LOW_AT[5]:
-                ts(R("kth"), R("ff", 17, 33), 1.0e6, ALU.mult, SPARE, ALU.add)
-            if c == 15:
-                for b in range(early(t)):
-                    values(t, b)
-            if t > 1:
-                maxima(t, "s%d" % c)
-            else:
-                lo = 128 * (c // 2)
-                copy(R("wa%d" % (c % 2), 256 + lo, 384 + lo), R("ixi", lo, lo + 128))
+    def look(t, j):
+        c0, c1 = PARTS[j]
+        n = c1 - c0
+        zd = R("db" if j % 2 else "da", 0, 16 * n)
+        lst, dig, whole = slot("sb", t, j)
+        mm(zd, R("idh"), part("kc", j), True, False)
+        mm(zd, R("idh"), part("lift", j), False, False)
+        for q, a0, a1 in LOOKS[j]:
+            lo, hi = 16 * c0 + n * a0, 16 * c0 + n * a1
+            shift(R("g2", 16 * lo, 16 * hi), ind(RP, R("su", lo, hi)), -7.5 - BASE - TAG * (t - 1) / 256, q)
+        for a in range(16):
+            m = 16 * (16 * c0 + n * a)
+            mm(zd, R("ea", 128 * a, 128 * a + 128), R("g2", m, m + 16 * n), False, a == 15)
+        for a0, a1 in zip(MAXIMA[j], MAXIMA[j][1:]):
+            lo, hi = 16 * (16 * c0 + n * a0), 16 * (16 * c0 + n * a1)
+            scan(R("mx", lo, hi), R("g2", lo, hi), R("d1", 0, hi - lo), 0.0, ALU.max, ALU.add)
+        copy(part("r16", j), zd, MOVES["r16"])
+        tt(part("wt", j), part("r16", j), zd, ALU.is_gt)
+        scan(part("yy", j), part("wt", j), part("bd", j), 0.0, ALU.max, ALU.mult)
+        y = R("yy", 16 * c0 + 15, 16 * c1, 16)
+        tt(lst, R("lf", c0, c1), y, ALU.subtract)
+        tt(R("ff", 33 + c0, 33 + c1), y, R("ml", c0, c1), ALU.is_gt)
+        tt(R("ff", 1 + c0, 1 + c1), y, R("mk", c0, c1), ALU.is_le)
+        tt(part("si", j), ind(R("mx", 256 * c0, 256 * c1), R("lmx", c0, c1)), part("hv", j), ALU.add)
+        ts(part("sj", j), part("si", j), 15, ALU.bitwise_and)
+        copy(dig, part("sj", j))
+        send(nxt, slot("rb", t, j)[2], whole, "ro%d_%d" % (t, j), "sent", HOP)
+        ops[-1]["lead"] = EARLY[j]
 
-    def heads(lo, hi):
-        copy(R("d1", 512 * lo + 15, 512 * hi, 16), R("g2", 512 * lo, 512 * hi, 16), "s")
+    def write(t, j):
+        lst, dig, whole = slot("rb", t, j)
+        copy(ind(R("xs"), lst), dig, ext=[("ro%d_%d" % (t, j), nin)])
 
-    def values(t, b):
-        copy(R("g2", 512 * b, 512 * b + 512), ind(R("xs", 0, 4096), R("sin", 256 * t + 32 * b, 256 * t + 32 * b + 32)), "s",
-             ext=[("rs0" if t == 1 and b < 4 else "rs%d" % t, neng)])
-        for lo, hi in (HEADS if t > 1 else FIRST_HEADS).get(b, []):
-            heads(lo, hi)
+    def write_copy(t, j):
+        lst, dig, whole = slot("sb", t, j)
+        shift(part("n32", j), dig, BASE, MOVES["nd"])
+        copy(ind(R("rp", LOW, LOW + 4096 + 256), lst), part("n32", j), MOVES["copy"])
 
-    def early(t):
-        return EARLY_VALUES if t > 1 else FIRST_VALUES
-
-    done = [0]
-
-    def maxima(t, slot):
-        upto = 16 * t + (MAX_PLAN if t > 1 else FIRST_MAX).get(slot, 0)
-        done[0] = max(done[0], 16 * t)
-        if upto > done[0]:
-            lo, hi = 256 * (done[0] - 16 * t), 256 * (upto - 16 * t)
-            scan(R("mx", lo, hi), R("g2", lo, hi), R("d1", lo, hi), 0.0, ALU.max, ALU.add)
-            done[0] = upto
-
-    def lookups(t):
-        for c in range(16):
-            o = R("lg", 256 * c, 256 * c + 256)
-            src = ind(R("lt", LOW, LOW + 4096), R("su", 256 * t + 16 * c, 256 * t + 16 * c + 16))
-            bias = R("bi", 16 * t + c, 16 * t + c + 1)
-            if LOCK_PLAN[c] == "v":
-                ts(o, src, bias, ALU.add, 0.0, ALU.max)
-            else:
-                act(o, src, ACT.Relu, bias, 1.0)
-            if c % 4 == 3:
-                b = c // 4
-                for k in range(16):
-                    mm(R("z3", 64 * b, 64 * b + 64), R("idw"), R("lg", 1024 * b + k, 1024 * b + 1024, 16), False, c == 15 and k == 15)
-            maxima(t, "l%d" % c)
-
-    def decide(t):
-        scan(R("m3"), R("rs"), R("z3", 0, 256), -1.0e6, ALU.max, ALU.min)
-        ts(R("osn", 16 * t, 16 * t + 16), R("m3", 15, 256, 16), 4096.0 - SPARE, ALU.add)
-        send(R("oin", 16 * t, 16 * t + 16), R("osn", 16 * t, 16 * t + 16), "ro%d" % t)
-
-    def order_a(t):
-        m = R("m3", 15, 256, 16)
-        ts(R("ff", 33, 49), m, SPARE, ALU.is_lt)
-        tt(R("ff", 1, 17), m, R("kth"), ALU.is_ge)
+    def order(t):
         scan(R("uu", 0, 49), R("ff", 0, 49), R("ff", 0, 49), 0.0, ALU.add, ALU.max)
-        mm(R("pp", 0, 48), R("tle"), R("uu", 1, 49), True, False)
-        mm(R("pp", 0, 48), R("tgt"), R("uu", 0, 48), False, True)
-        mm(R("pp", 64, 65), R("oneb") if t % 2 else R("one1"), R("uu", 32, 33), True, True)
+        mm(R("ph", 0, 48), R("tle"), R("uu", 1, 49), True, False)
+        mm(R("ph", 0, 48), R("tgt"), R("uu", 0, 48), False, True)
+        mm(R("ph", 64, 65), R("oneb") if t % 2 else R("one1"), R("uu", 32, 33), True, True)
         if t % 2 == 0:
-            mm(R("pp", 72, 73), R("onef"), R("uu", 32, 33), True, True)
-
-    def order_b(t):
-        tt(R("tt"), R("ff", 1, 49), R("pp", 0, 48), ALU.mult)
+            mm(R("ph", 72, 73), R("onef"), R("uu", 32, 33), True, True)
+        mm(R("pd", 0, 16), R("r256") if t % 2 else R("i256"), R("ff", 33, 49), True, False)
+        tt(R("tt"), R("ff", 1, 49), R("ph", 0, 48), ALU.mult)
         for j in range(3):
-            mm(R("pd", 0, 16), R("rotb") if t % 2 else R("idn"), R("tt", 16 * j, 16 * j + 16), j == 0, j == 2)
-        ts(R("c1", 0, 1), R("pp", 64, 65), -1.0, ALU.mult, R("nx", 0, 1), ALU.add)
-        ts(R("old"), R("iw"), R("pp", 64, 65), ALU.is_lt, SPARE, ALU.mult)
-        if t % 2 == 0:
-            ts(R("oldr"), R("iw"), R("pp", 72, 73), ALU.is_lt, SPARE, ALU.mult)
-
-    def order_c(t):
+            mm(R("pd", 0, 16), R("rotb") if t % 2 else R("idn"), R("tt", 16 * j, 16 * j + 16), False, j == 2)
+        ts(R("c1", 0, 1), R("ph", 64, 65), -1.0, ALU.mult, R("nx", 0, 1), ALU.add)
+        shift(R("orow", 0, 256), R("jrow", 256 * (t % 2), 256 * (t % 2) + 256), R("c1", 0, 1), MOVES["fill"])
         ts(R("du"), R("pd", 0, 16), -1.0, ALU.add)
-        ts(R("tl"), R("iwo"), R("c1", 0, 1), ALU.add)
-        copy(ind(R("orow"), R("du")), R("irow"))
-        tt(R("tl2"), R("tl"), R("old"), ALU.add)
-        maxima(t, "o")
-        scan(R("mo"), R("orow"), R("ko"), -1.0, ALU.max, ALU.add)
+        copy(ind(R("orow"), R("du")), R("jrow", 512 - 256 * (t % 2), 768 - 256 * (t % 2)), MOVES["orow"])
+        for h in (1, 0):
+            scan(R("mo", 128 * h, 128 * h + 128), R("orow", 128 * h, 128 * h + 128), R("ko", 0, 128), -1.0, ALU.max, ALU.add)
+            ts(R("ou", 16 * (t % 2) + 8 * h, 16 * (t % 2) + 8 * h + 8), R("mo", 128 * h + 15, 128 * h + 128, 16), col(4), ALU.add)
         if t < NR:
+            ts(R("old"), R("iw"), R("ph", 72 if t % 2 == 0 else 64, 73 if t % 2 == 0 else 65), ALU.is_lt, SPARE, ALU.mult)
             ts(R("cw", 0, 1), R("c1", 0, 1), 1024.0, ALU.is_ge, -1024.0, ALU.mult)
-        tt(R("om"), R("mo", 15, 256, 16), R("tl2"), ALU.max)
-        if t < NR:
             ts(R("nx", 0, 1), R("c1", 0, 1), R("cw", 0, 1), ALU.add, 256.0, ALU.add)
-        ts(R("ou"), R("om"), col(8), ALU.add)
 
-    def wrap(t):
-        ts(R("wv"), R("mx", 15, 4096, 16), 16.0, ALU.is_ge, -16.0, ALU.mult)
-
-    def write(t):
-        tt(ind(R("xs"), R("oin", 16 * t, 16 * t + 16)), R("mx", 15, 4096, 16), R("wv"), ALU.add, ext=[("ro%d" % t, neng)])
-
-    def carry(t):
-        copy(R("wq%d" % (t % 2), 0, 256), ind(R("wq%d" % ((t - 1) % 2)), R("ou")), "s")
+    def carry(name, t):
+        copy(R(name, home(t), home(t) + 256), moved(name, t), MOVES[name])
 
     for t in range(1, NR + 1):
         if t == 1:
-            for b in range(4):
-                digits(64 * b, 64 * b + 32, "s")
-                digits(64 * b + 32, 64 * b + 64, "v")
-                names(b)
-                if b == 2:
-                    copy(half("s16", 0), pn(0, 128))
-                    mm(R("pd", 0, 128), R("roth"), half("s16", 0), True, True)
-            ts(R("su", 256, 384), R("pd", 0, 128), 2048.0, ALU.add)
-            send(R("sin", 256, 384), R("su", 256, 384), "rs0")
-            ts(R("nx", 0, 1), R("pp", 256, 257), 256.0, ALU.add)
-            copy(half("s16", 1), pn(128, 256))
-            mm(R("pr", 0, 128), R("roth"), half("s16", 1), True, True)
-            twins_pe(t)
-            ts(R("su", 384, 512), R("pr", 0, 128), 2048.0, ALU.add)
-            send(R("sin", 384, 512), R("su", 384, 512), "rs1")
-            keep_names("ws", "s")
-            iota(R("ws", 256, 1536), [[0, 1280]], -2050, 0)
-            iota(R("wq0", 256, 1280), [[1, 1024]], 0, 0)
-            iota(R("wq0", 1280, 1536), [[1, 256]], 0, 0)
-            lock_base(t, 1)
-            lock_base(t, 0)
-            twins_v(t)
-            lock_twins(t, 1)
-            lock_twins(t, 0)
-            list_base(t)
-            firsts(1)
-            firsts(0)
-            lock_list(1)
-            lock_list(0)
-        else:
-            digits(128, 160, "s")
-            digits(160, 192, "v")
-            names(2)
-            digits(192, 224, "s")
-            digits(224, 256, "v")
-            names(3)
-            digits(0, 32, "s")
-            digits(64, CUT, "s")
-            twins_v(t)
-            lock_twins(t, 1)
-            kinds(t, 1)
-            lock_base(t, 0)
-            lock_twins(t, 0)
-            digits(32, 64, "v")
-            names(0)
-            firsts(1)
-            rest_names(16)
-            lock_list(1)
-        locks(t)
-        lookups(t)
-        for b in range(early(t), 8):
-            values(t, b)
-            if t > 1 and b == (KEEP_AT if t < NR else min(KEEP_AT, 7)):
-                keep_names("ws", "s")
-        decide(t)
-        if t == 1:
-            iota(R("wq1", 256, 1280), [[1, 1024]], 0, 0)
-            iota(R("wq1", 1280, 1536), [[1, 256]], 0, 0)
-        order_a(t)
-        maxima(t, "a")
-        order_b(t)
-        maxima(t, "b")
-        order_c(t)
+            for b in range(3, -1, -1):
+                names(t, b)
+                keep(t, "s16", b, "vs"[b % 2])
+            copy(R("ws", 0, 256), R("s16", 0, 256), "s")
+        from_stored(t)
+        done = 4
+        for j in range(len(SEGS)):
+            while t > 1 and 64 * done > SEGS[j][0]:
+                done -= 1
+                names(t, done)
+            locks(t, j)
+        kinds(t)
+        for b in range(3, -1, -1) if t > 1 else ():
+            keep(t, "ws", b, MOVES["keep"], home(t - 1))
+        for j in range(len(PARTS)):
+            look(t, j)
+        order(t)
+        for j in range(len(PARTS)):
+            write(t, j)
         if t == NR:
-            maxima(t, "c")
-            wrap(t)
-            ts(R("s32", 0, 256), ind(R("ws"), R("ou")), 2048.0, ALU.add, -1.0, ALU.max)
-            add("y", lambda e: e.dma_start(T.yd[:], T.s32[:, 0:256]), [], [R("s32", 0, 256)], dma="dyd")
-            write(t)
-            add("y", lambda e: e.dma_start(T.yx[:], T.xs[:, 0:4096]), [], [R("xs", 0, 4096)], dma="dyx")
-        if t < NR:
-            copy(R("wa%d" % (t % 2), 0, 256), ind(R("wa%d" % ((t - 1) % 2)), R("ou")), "s")
-            if t > 1 and KEEP_AT == 8:
-                keep_names("ws", "s")
-            copy(R("s32", 0, 256), ind(R("ws"), R("ou")), "s")
-            turn_stored(t + 1)
-            maxima(t, "c")
-            twins_pe(t + 1)
-            lock_base(t + 1, 1)
-            wrap(t)
-            copy(R("at"), R("wa%d" % (t % 2), 0, 256))
-            write(t)
-            send_stored(t + 1)
-        carry(t)
-    ql = "wq%d" % (NR % 2)
-    add("s", lambda e: e.dma_start(T.yq[:], T[ql][0:128:16, 0:256]), [], [R(ql, 0, 256)], dma="dyq")
+            ts(R("s32"), moved("ws", t), 2048.0, ALU.add, -1.0, ALU.max)
+            store("y", T.yd[:], T.s32[:, 0:256], R("s32"), "dyd", 2.5)
+            store("y", T.yx[:], T.xs[:, 0:4096], R("xs", 0, 4096), "dyx", 7.0)
+        else:
+            for j in range(len(PARTS)):
+                write_copy(t, j)
+            for lo, hi in AT_CUTS:
+                copy(R("at", lo, hi), ind(moved("wx", t)[1], R("ou", 16 * (t % 2) + lo // 16, 16 * (t % 2) + hi // 16)), MOVES["at"])
+            copy(R("s16", 0, 256), moved("ws", t), MOVES["s16"])
+            carry("wx", t)
+        carry("wq", t)
+    store("s", T.yq[:], T.wq[0:128:16, home(NR):home(NR) + 256], R("wq", home(NR), home(NR) + 256), "dyq", 2.0)
 
-    def meet(a, b):
-        if a[0] != b[0] or a[1] >= b[2] or b[1] >= a[2]:
-            return False
-        return a[3] != b[3] or a[3] == 1 or (a[1] - b[1]) % a[3] == 0
+    if "order" not in PLAN:
+        PLAN["order"] = plan(ops)
+    ops = [ops[i] for i in PLAN["order"]]
 
-    def banks(o):
-        return set(r[0] for r in o["rd"] + o["wr"] if r[0] in PSUM)
-
-    known = {q: {} for q in Q}
-    byname = {}
-    for n, o in enumerate(ops):
-        q = o["q"]
-        cand = set()
-        for r in o["rd"] + o["wr"]:
-            cand.update(byname.get(r[0], []))
-        need = {}
-        bk = banks(o)
-        for m in cand:
-            p = ops[m]
-            same = p["q"] == q and p["dma"] is None and o["dma"] is None
-            hit = any(meet(a, b) for a in o["rd"] for b in p["wr"]) or any(meet(a, b) for a in o["wr"] for b in p["wr"] + p["rd"])
-            if same:
-                hit = hit and q != "t"
-            else:
-                hit = hit or bool(bk & banks(p))
-            if hit:
+    if "waits" not in PLAN:
+        known = {q: {} for q in Q}
+        byname, clock, waits = {}, [], []
+        for n, o in enumerate(ops):
+            q = o["q"]
+            cand = set()
+            for r in o["rd"] + o["wr"]:
+                cand.update(byname.get(r[0], []))
+            need = {}
+            bk = banks(o)
+            for m in cand:
+                p = ops[m]
                 if p["dma"] == "remote":
-                    raise ValueError("a buffer that a remote write reads is written again")
-                key = p["dma"] or p["q"]
-                need[key] = max(need.get(key, -1), m)
-        o["wait"] = []
-        for key, m in sorted(need.items(), key=lambda kv: -kv[1]):
-            if known[q].get(key, -1) < m:
-                o["wait"].append(m)
-                ops[m]["sig"] = True
-                for k2, v2 in ops[m]["clock"].items():
-                    known[q][k2] = max(known[q].get(k2, -1), v2)
-        o["xw"] = []
-        for name, val in o["ext"]:
-            if name not in known[q]:
-                known[q][name] = 0
-                o["xw"].append((name, val))
-        o["clock"] = dict(known[q])
-        o["clock"][o["dma"] or q] = n
-        for r in o["rd"] + o["wr"]:
-            byname.setdefault(r[0], []).append(n)
+                    continue
+                if p["q"] == q and p["dma"] is None and o["dma"] is None:
+                    hit = q != "t" and clash(o, p)
+                else:
+                    hit = clash(o, p) or bool(bk & banks(p))
+                if hit:
+                    key = p["dma"] or p["q"]
+                    need[key] = max(need.get(key, -1), m)
+            wait, xw = [], []
+            for key, m in sorted(need.items(), key=lambda kv: -kv[1]):
+                if known[q].get(key, -1) < m:
+                    wait.append(m)
+                    for k2, v2 in clock[m].items():
+                        known[q][k2] = max(known[q].get(k2, -1), v2)
+            for name, val in o["ext"]:
+                if name not in known[q]:
+                    known[q][name] = 0
+                    xw.append(name)
+            waits.append((wait, xw))
+            clock.append(dict(known[q]))
+            clock[n][o["dma"] or q] = n
+            for r in o["rd"] + o["wr"]:
+                byname.setdefault(r[0], []).append(n)
+        PLAN["waits"] = waits
+    awaited = set(m for wait, xw in PLAN["waits"] for m in wait)
     count = {q: 0 for q in ESEM}
-    nsent = 0
-    for o in ops:
+    for n, o in enumerate(ops):
         e = Q[o["q"]]
-        for m in o["wait"]:
+        for m in PLAN["waits"][n][0]:
             p = ops[m]
             if p["dma"]:
                 e.wait_ge(T.sem[p["dma"]], 16)
             else:
                 e.wait_ge(T.sem[ESEM[p["q"]]], p["count"])
-        for name, val in o["xw"]:
-            e.wait_ge(T.sem[name], val)
+        for name, val in o["ext"]:
+            if name in PLAN["waits"][n][1]:
+                e.wait_ge(T.sem[name], val)
         ins = o["fn"](e)
         if o["dma"] == "remote":
-            nsent += neng
-        elif o["dma"]:
+            continue
+        if o["dma"]:
             ins.then_inc(T.sem[o["dma"]], 16)
-        elif o.get("sig"):
+        elif n in awaited:
             count[o["q"]] += 1
             o["count"] = count[o["q"]]
             ins.then_inc(T.sem[ESEM[o["q"]]], 1)
-    g.wait_ge(T.sem["sent"], nsent)
+    g.wait_ge(T.sem["sent"], NR * len(PARTS) * neng + SHIP * nback)
     g.sync.wait_ge(T.sem["dyd"], 16)
     g.sync.wait_ge(T.sem["dyx"], 16)
     g.scalar.wait_ge(T.sem["dyq"], 16)

@@ -7,25 +7,31 @@ TAG = 17
 BASE = 64.0
 ROUND = 12582912.0
 SPARE = 2048.0 - 2 * W
-SLOT = 288
-SHIP = 4
-SEGS = [(192, 256), (128, 192), (64, 128), (0, 64)]
-PARTS = [(0, 8), (8, 16)]
-NAMES = [("s", 224, 256), ("v", 192, 224), ("s", 144, 192), ("v", 128, 144), ("s", 80, 128), ("v", 64, 80),
+SLOT = 320
+SHIP = 8
+SEGS = [(192, 256), (128, 192), (64, 128), (32, 64), (0, 32)]
+FIRST_SEGS = [(128, 256), (0, 128)]
+FIRST_STEP = 64
+FIRST_KEEP = "ssss"
+FIRST_BANKS = ("pb", "pa", "pb", "pa")
+PARTS = [(0, 10), (10, 16)]
+NAMES = [("s", 224, 256), ("v", 192, 224), ("s", 160, 192), ("v", 128, 160), ("s", 80, 128), ("v", 64, 80),
          ("s", 16, 64), ("v", 0, 16)]
 FIRST_NAMES = [("sv"[j % 2], 32 * j, 32 * j + 32) for j in range(8)]
 LOOKS = [[("s", 0, 4), ("v", 4, 8), ("s", 8, 12), ("v", 12, 16)],
-         [("s", 0, 4), ("s", 4, 8), ("v", 8, 10), ("s", 10, 14), ("s", 14, 16)]]
-MAXIMA = [[0, 4, 8, 12, 16], [0, 4, 8, 10, 14, 16]]
-AT_CUTS = [(0, 256)]
-MOVES = {"at": "s", "s16": "s", "wx": "s", "wq": "s", "keep": "s", "su": "s", "r16": "s", "copy": "s", "orow": "s", "nd": "s",
-         "fill": "v"}
-CYC, WAKE, HOP, PE = 0.83e-3, 0.165, 2.45, 0.42e-3
+         [("s", 0, 6), ("s", 6, 12), ("s", 12, 16)]]
+MAXIMA = [[0, 3, 4, 7, 8, 11, 12, 15, 16], [0, 5, 6, 11, 12, 16]]
+LAST_PARTS, LAST_LOOKS, LAST_MAXIMA = list(PARTS), list(LOOKS), list(MAXIMA)
+BIG = 1536.0
+MOVES = {"tx": "s", "tn": "v", "tq": "s", "at": "s", "s16": "s", "wx": "s", "wq": "s", "keep": "s", "su": "s", "r16": "s", "copy": "s", "orow": "s", "nd": "s",
+         "fill": "s", "nec": "ssvvvvvv", "dig": "vv", "lo": 128, "ml": "s"}
+CYC, WAKE, HOP, PE = 0.83e-3, 0.19, 1.5, 0.42e-3
 GATHER, SCATTER = 1.56, 3.8
-PASSES = 2
-SHIP_LAT = 4.0
-IDX_AFTER = 3
-EARLY = [2.0, 0.0]
+LEADS = {"s s16 0": 5.5, "v hh 0": 3.5, "v xs/rb 176": 2.5, "g sb 0": 4.0, "v rp/lo 6": 1.25, "v df 192": 3.0, "v g1 2048": 0.75,
+         "v n0 0": 2.75, "v si 160": 4.25}
+SHIP_LAT = 2.5
+IDX_AFTER = 7
+EARLY = [3.0, 0.0]
 
 SCRATCH = {
     "xs": ("sbuf", [128, 4096 + 256], "bfloat16"), "xr": ("sbuf", [128, 2048], "bfloat16"),
@@ -34,9 +40,15 @@ SCRATCH = {
     "rp": ("sbuf", [128, LOW + 4096 + 256], "float32"),
     "qi": ("sbuf", [128, 272], "int32"),
     "qf": ("sbuf", [128, 272], "float32"),
-    "wx": ("sbuf", [128, 1792], "int32"), "wq": ("sbuf", [128, 1792], "float32"), "ws": ("sbuf", [128, 1792], "float32"),
+    "wx": ("sbuf", [128, 1536], "int32"), "wq": ("sbuf", [128, 1536], "float32"), "ws": ("sbuf", [128, 1536], "float32"),
+    "tx": ("sbuf", [128, 256], "int32"), "tq": ("sbuf", [128, 256], "float32"), "tn": ("sbuf", [128, 256], "float32"),
+    "sr": ("sbuf", [128, 32], "uint16"), "nxr": ("sbuf", [128, 16], "float16"),
+    "gg": ("sbuf", [128, 32], "bfloat16"), "gu": ("sbuf", [128, 32], "bfloat16"),
+    "gs": ("sbuf", [128, 16], "bfloat16"), "gr": ("sbuf", [128, 16], "bfloat16"),
+    "tleb": ("sbuf", [128, 128], "bfloat16"), "tgtb": ("sbuf", [128, 128], "bfloat16"),
+    "ibig": ("sbuf", [128, 128], "bfloat16"), "rbig": ("sbuf", [128, 128], "bfloat16"),
     "g1": ("sbuf", [128, 4096], "bfloat16"), "g2": ("sbuf", [128, 4096], "float16"),
-    "mx": ("sbuf", [128, 4096], "bfloat16"), "d1": ("sbuf", [128, 1024], "float16"),
+    "mx": ("sbuf", [128, 4096], "bfloat16"), "d1": ("sbuf", [128, 512], "float16"),
     "wn": ("sbuf", [128, 2048], "bfloat16"), "ea": ("sbuf", [128, 2048], "float16"),
     "at": ("sbuf", [128, 256], "uint16"), "su": ("sbuf", [128, 256], "uint16"),
     "sb": ("sbuf", [128, NR * SLOT], "uint16"), "rb": ("sbuf", [128, NR * SLOT], "uint16"),
@@ -48,20 +60,18 @@ SCRATCH = {
     "bd": ("sbuf", [128, 256], "float32"), "yy": ("sbuf", [128, 256], "float32"),
     "si": ("sbuf", [128, 256], "int32"), "sj": ("sbuf", [128, 256], "int32"),
     "m1": ("sbuf", [128, 512], "float32"), "m4": ("sbuf", [128, 256], "float32"),
-    "mo": ("sbuf", [128, 256], "float32"), "orow": ("sbuf", [128, 512], "float32"),
+    "mo": ("sbuf", [128, 256], "float32"), "orow": ("sbuf", [128, 512], "float32"), "sn": ("sbuf", [128, 512], "float32"),
     "lo": ("sbuf", [128, 16], "uint16"), "du": ("sbuf", [128, 16], "uint16"), "ou": ("sbuf", [128, 32], "uint16"),
-    "n0": ("sbuf", [128, 16], "uint16"), "lmx": ("sbuf", [128, 16], "uint16"),
-    "ff": ("sbuf", [128, 64], "bfloat16"), "uu": ("sbuf", [128, 64], "bfloat16"), "tt": ("sbuf", [128, 48], "bfloat16"),
-    "old": ("sbuf", [128, 16], "float32"), "oldr": ("sbuf", [128, 16], "float32"), "kth": ("sbuf", [128, 16], "float32"),
-    "tl": ("sbuf", [128, 16], "float32"), "tl2": ("sbuf", [128, 16], "float32"), "om": ("sbuf", [128, 16], "float32"),
-    "ml": ("sbuf", [128, 16], "float32"), "mk": ("sbuf", [128, 16], "float32"), "lf": ("sbuf", [128, 16], "float32"),
+    "n0": ("sbuf", [128, 16], "uint16"), "lmx": ("sbuf", [128, 32], "uint16"),
+    "ff": ("sbuf", [128, 80], "bfloat16"), "uu": ("sbuf", [128, 80], "bfloat16"), "tt": ("sbuf", [128, 64], "bfloat16"),
+    "ml": ("sbuf", [128, 16], "float32"), "lf": ("sbuf", [128, 16], "float32"),
     "c1": ("sbuf", [128, 4], "float32"), "cw": ("sbuf", [128, 4], "float32"), "nx": ("sbuf", [128, 4], "float32"),
     "ci": ("sbuf", [128, 32], "int32"), "cj": ("sbuf", [128, 32], "int32"), "cf": ("sbuf", [128, 32], "float32"),
     "col": ("sbuf", [128, 16], "float32"),
     "wk": ("sbuf", [128, 64], "float32"), "wa": ("sbuf", [128, 16], "float32"),
-    "irow": ("sbuf", [128, 256], "float32"), "arow": ("sbuf", [128, 256], "float32"), "brow": ("sbuf", [128, 256], "float32"),
-    "jrow": ("sbuf", [128, 768], "float32"), "grow": ("sbuf", [128, 128], "float32"),
-    "e8": ("sbuf", [128, 128], "float32"), "b8": ("sbuf", [128, 8], "float32"),
+    "irow": ("sbuf", [128, 256], "bfloat16"), "arow": ("sbuf", [128, 256], "bfloat16"), "brow": ("sbuf", [128, 256], "bfloat16"),
+    "jrow": ("sbuf", [128, 768], "float32"), "grow": ("sbuf", [128, 128], "bfloat16"),
+    "e8": ("sbuf", [128, 128], "float32"), "ck": ("sbuf", [128, 16], "float32"),
     "one1": ("sbuf", [128, 128], "bfloat16"), "onew": ("sbuf", [128, 128], "bfloat16"), "oner": ("sbuf", [128, 128], "bfloat16"),
     "oneb": ("sbuf", [128, 128], "bfloat16"), "onef": ("sbuf", [128, 128], "bfloat16"), "rotb": ("sbuf", [128, 128], "bfloat16"),
     "idn": ("sbuf", [128, 128], "bfloat16"), "idw": ("sbuf", [128, 128], "bfloat16"),
@@ -70,8 +80,8 @@ SCRATCH = {
     "tle": ("sbuf", [128, 128], "bfloat16"), "tgt": ("sbuf", [128, 128], "bfloat16"), "tmp": ("sbuf", [128, 128], "bfloat16"),
     "sgn": ("sbuf", [128, 64], "bfloat16"), "sg2": ("sbuf", [128, 256], "bfloat16"),
     "dgm": ("sbuf", [128, 272], "bfloat16"), "nd": ("sbuf", [128, 272], "bfloat16"),
-    "ko": ("sbuf", [128, 256], "bfloat16"), "ko1": ("sbuf", [128, 256], "bfloat16"), "ko2": ("sbuf", [128, 256], "bfloat16"),
-    "eb": ("sbuf", [128, 256], "float32"), "ge": ("sbuf", [128, 256], "float32"),
+    "ko": ("sbuf", [128, 128], "bfloat16"), "ko1": ("sbuf", [128, 128], "bfloat16"), "ko2": ("sbuf", [128, 128], "bfloat16"),
+    "eb": ("sbuf", [128, 256], "bfloat16"), "ge": ("sbuf", [128, 256], "bfloat16"),
     "kc": ("sbuf", [128, 256], "float16"), "lift": ("sbuf", [128, 256], "float16"),
     "rs": ("sbuf", [128, 256], "float32"), "rs2": ("sbuf", [128, 512], "float32"), "off": ("sbuf", [128, 64], "bfloat16"),
     "iw": ("sbuf", [128, 16], "float32"), "iwo": ("sbuf", [128, 16], "float32"),
@@ -159,18 +169,15 @@ def plan(ops):
         return start
 
     tail = [o["lat"] if not succ[i] else 0.0 for i, o in enumerate(ops)]
-    way = list(tail)
-    best = None
-    for again in range(PASSES):
-        for i in range(n - 1, -1, -1):
-            way[i] = max([way[i] + ops[i]["lead"] + (0 if again else cost[i])] + [cost[i] + d + way[j] for j, d in succ[i].items()])
-        start = place(sorted(range(n), key=lambda i: (-way[i], i)), pred, [0.0] * n)
-        span = max(start[i] + cost[i] + tail[i] for i in range(n))
-        if best is None or span < best[0]:
-            best = (span, start)
-        back = place(sorted(range(n), key=lambda i: (-start[i] - cost[i], -i)), succ, tail)
-        way = [back[i] + cost[i] for i in range(n)]
-    return sorted(range(n), key=lambda i: (best[1][i], i))
+    way = [0.0] * n
+    for i in range(n - 1, -1, -1):
+        way[i] = cost[i] + max([d + way[j] for j, d in succ[i].items()] + [tail[i]])
+    start = place(sorted(range(n), key=lambda i: (-way[i], i)), pred, [0.0] * n)
+    back = place(sorted(range(n), key=lambda i: (-start[i] - cost[i], -i)), succ, tail)
+    for i in range(n - 1, -1, -1):
+        way[i] = max([back[i] + cost[i] + ops[i]["lead"] + LEADS.get(ops[i]["tag"], 0.0)] + [1e-6 + way[j] for j in succ[i]])
+    start = place(sorted(range(n), key=lambda i: (-way[i], i)), pred, [0.0] * n)
+    return sorted(range(n), key=lambda i: (start[i], i))
 
 
 def rank_program(g, core, T, topo):
@@ -217,6 +224,13 @@ def rank_program(g, core, T, topo):
             return 0.06 + CYC * GATHER * cols(o)
         return CYC * max(64, cols(o) * (per or (0.5 if narrow(o, i) else 1)))
 
+    now = [0]
+
+    def tag(q, r):
+        name, lo = (r[1][0] + "/" + r[2][0], r[2][1]) if len(r) == 3 else r[:2]
+        lo %= {"sb": SLOT, "rb": SLOT, "ou": 16, "sr": 16, "ec": 256}.get(name[-2:], 4096)
+        return "%s%s %s %d" % ("" if now[0] > 1 else now[0], q, name, lo)
+
     def add(q, fn, outs, ins, cost, dma=None, ext=None, lat=0.0, sems=()):
         rd, wr = [], []
         for r in ins:
@@ -229,7 +243,7 @@ def rank_program(g, core, T, topo):
                 else:
                     wr.append(r)
         ops.append({"q": q, "fn": fn, "rd": rd, "wr": wr, "dma": dma, "ext": ext or [], "cost": cost, "lat": lat, "sems": sems,
-                    "lead": 0.0})
+                    "lead": 0.0, "tag": tag(q, outs[0] if outs else ins[0])})
 
     def copy(o, i, q="v", ext=None):
         if q == "v":
@@ -307,16 +321,15 @@ def rank_program(g, core, T, topo):
     iota(R("grow"), [[16, 8], [0, 16]], 0, 0)
     iota(R("irow"), [[1, 256]], 0, 0)
     iota(R("brow"), [[1, 16], [0, 16]], 0, 0)
-    mset(R("wn"), 0.0)
-    copy(R("ea"), R("wn"), "s")
-    copy(R("d1"), R("wn", 0, 1024), "s")
+    mset(R("d1"), 0.0)
     ts(R("ci", 18, 19), R("ci", 18, 19), 80.0, ALU.add)
     ts(R("cj", 0, 17), R("ci", 0, 17), 15, ALU.bitwise_and)
     copy(col(0), R("ci", 16, 17))
     ts(R("cj", 17, 19), R("ci", 17, 19), 127, ALU.bitwise_and)
     ts(R("cj", 19, 22), R("ci", 16, 19), 112, ALU.bitwise_and)
-    mset(R("rs"), -1.0e6)
-    mset(R("rs2"), -1.0e6)
+    for r in (R("rs"), R("rs2", 0, 256), R("rs2", 256, 512)):
+        act(r, R("arow"), ACT.Identity, -1.0e6, 0.0)
+    act(R("bd"), R("arow"), ACT.Identity, 1.0, 0.0)
     copy(R("cf", 0, 22), R("cj", 0, 22))
     mset(R("dgm", 256, 272), 0.0)
     copy(R("s16", 256, 272), R("cf", 0, 16))
@@ -328,34 +341,32 @@ def rank_program(g, core, T, topo):
     ts(R("wk", 0, 16), R("cf", 0, 16), 0.0, ALU.is_equal, 256.0, ALU.mult)
     ts(R("wk", 16, 32), R("cf", 0, 16), 1.0, ALU.is_equal, 16.0, ALU.mult)
     ts(R("wk", 32, 48), R("cf", 0, 16), 2.0, ALU.is_equal)
-    ts(R("ko1"), R("arow"), ca, ALU.is_equal, 4096.0, ALU.mult)
-    ts(R("ko2"), R("arow"), ca, ALU.is_lt, -8192.0, ALU.mult)
+    ts(R("ko1"), R("arow", 0, 128), ca, ALU.is_equal, 4096.0, ALU.mult)
+    ts(R("ko2"), R("arow", 0, 128), ca, ALU.is_lt, -8192.0, ALU.mult)
     tt(R("wk", 48, 64), R("wk", 0, 16), R("wk", 16, 32), ALU.add)
     ts(R("e8", 0, 128, 1, 8), R("e8", 0, 128, 1, 8), 0.0, ALU.is_equal)
     copy(R("qf", 0, 256, 1, 8), R("qi", 0, 256, 1, 8))
     mm(R("da", 0, 256), R("e8", 0, 128, 1, 8), R("qf", 0, 256, 1, 8), True, True)
     tt(R("ko"), R("ko1"), R("ko2"), ALU.add)
     tt(R("wk", 0, 16), R("wk", 48, 64), R("wk", 32, 48), ALU.add)
-    ts(R("b8"), R("grow", 0, 128, 16), cg, ALU.is_equal)
+    ts(R("ck"), R("arow", 0, 16), cg, ALU.add)
     ts(R("wa"), R("arow", 0, 16), ca, ALU.is_equal)
     ts(col(8), col(9), -1.0, ALU.mult, -4096.0, ALU.add)
     ts(col(4), col(8), 0.25 - BASE, ALU.add)
-    ts(R("ko", 15, 256, 16), R("ko", 15, 256, 16), col(9), ALU.add)
-    ts(col(7), col(9), 4096.0 + BASE, ALU.add)
+    ts(R("ko", 15, 128, 16), R("ko", 15, 128, 16), col(9), ALU.add)
     act(R("sgn", 0, 16), R("arow", 0, 16), ACT.Sign, col(5), 1.0)
     for k in range(16):
-        act(R("wn", 129 * k, 128 * k + 128, 16), R("b8"), ACT.Identity, 0.0, R("wk", k, k + 1))
-    mset(R("sg2"), 1.0)
-    for h in range(0, 256, 64):
-        mset(R("sg2", h + 32, h + 48), -2.5)
-        act(R("sg2", h + 16, h + 32), R("sgn", 0, 16), ACT.Identity, -2.0, 0.5)
-        act(R("sg2", h + 48, h + 64), R("sgn", 0, 16), ACT.Identity, -2.0, 0.5)
+        ts(R("wn", 128 * k, 128 * k + 128), R("irow", 0, 128), R("ck", k, k + 1), ALU.is_equal, R("wk", k, k + 1), ALU.mult)
+    mset(R("sg2"), 3.0)
+    for h in range(0, 128, 64):
+        mset(R("sg2", h + 32, h + 48), (2048.0 + LOW) / W - 0.5)
+        act(R("sg2", h + 16, h + 32), R("sgn", 0, 16), ACT.Identity, (2048.0 + LOW) / W, 0.5)
+        act(R("sg2", h + 48, h + 64), R("sgn", 0, 16), ACT.Identity, (2048.0 + LOW) / W, 0.5)
     ts(R("dgm", 0, 256), R("arow"), ca, ALU.is_equal, -2.0, ALU.mult)
-    scan(R("mo"), R("da", 0, 256), R("ko"), -1.0, ALU.max, ALU.add)
+    for h in (0, 128):
+        scan(R("mo", h, h + 128), R("da", h, h + 128), R("ko"), -1.0, ALU.max, ALU.add)
     act(R("nd"), R("dgm"), ACT.Identity, 1.0, 0.5)
     copy(R("wq", 0, 256), R("da", 0, 256), "s")
-    for k in range(16):
-        act(R("ea", 129 * k, 128 * k + 128, 16), R("b8"), ACT.Identity, 0.0, R("wa", k, k + 1))
     ts(R("rot"), R("irow", 0, 128), cpr, ALU.is_equal)
     ts(R("ou", 0, 16), R("mo", 15, 256, 16), col(8), ALU.add)
     ts(R("selr"), R("grow"), cpr, ALU.is_equal)
@@ -364,10 +375,13 @@ def rank_program(g, core, T, topo):
     ts(R("iw"), R("irow", 0, 256, 16), ca, ALU.add)
     ts(R("ge"), R("arow"), ca, ALU.is_ge)
     ts(R("rs", 0, 256, 16), R("iw"), SPARE, ALU.add)
-    ts(R("rs2", 0, 512, 32), R("iw"), SPARE, ALU.add)
+    ts(R("rs2", 0, 512, 32), R("iw"), 4096.0 + LOW, ALU.add)
+    ts(R("rs2", 31, 512, 64), R("arow", 0, 128, 16), ca, ALU.add)
+    ts(R("rs2", 63, 512, 64), R("arow", 0, 128, 16), col(6), ALU.add)
     ts(R("idn"), R("irow", 0, 128), cp, ALU.is_equal)
     ts(R("id16"), R("irow", 0, 128), cp, ALU.is_equal, 16.0, ALU.mult)
-    ts(R("i256"), R("irow", 0, 128), cp, ALU.is_equal, 256.0, ALU.mult)
+    ts(R("ibig"), R("irow", 0, 128), cp, ALU.is_equal, BIG, ALU.mult)
+    ts(R("rbig"), R("irow", 0, 128), cpb, ALU.is_equal, BIG, ALU.mult)
     ts(R("r256"), R("irow", 0, 128), cpb, ALU.is_equal, 256.0, ALU.mult)
     ts(R("idh"), R("irow", 0, 128), cp, ALU.is_equal)
     tt(R("eb"), R("ge"), R("brow"), ALU.add)
@@ -375,30 +389,29 @@ def rank_program(g, core, T, topo):
     ts(R("rotb"), R("irow", 0, 128), cpb, ALU.is_equal)
     ts(R("one1"), R("grow"), cg, ALU.is_equal)
     ts(R("oner"), R("grow"), cgr, ALU.is_equal, W, ALU.mult)
-    ts(R("onef"), R("grow"), cgr, ALU.is_equal)
     ts(R("oneb"), R("grow"), cgb, ALU.is_equal)
-    ts(R("tmp"), R("irow", 0, 128), cp, ALU.is_ge)
-    ts(R("iwo"), R("iw"), col(7), ALU.add)
+    ts(R("tmp"), R("arow", 0, 128), ca, ALU.is_ge)
     tt(R("tle"), R("tmp"), R("one1"), ALU.mult)
-    mset(R("ff", 0, 33), 0.0)
-    mset(R("kth"), 0.0)
+    tt(R("tleb"), R("tmp"), R("oneb"), ALU.mult)
+    mset(R("ff", 0, 1), 0.0)
+    mset(R("gg", 0, 1), 0.0)
     tt(R("tgt"), R("one1"), R("tle"), ALU.subtract)
-    for t in range(NR):
-        act(R("ec", 256 * t, 256 * t + 256), R("eb"), ACT.Identity, (16.0 + TAG * t) / 256, -1.0 / 256)
-    for j, c in enumerate((-256.0, 0.0, 1280.0)):
-        shift(R("jrow", 256 * j, 256 * j + 256), R("irow"), BASE + c, "s")
-    if "s" in (MOVES["copy"], MOVES["orow"]):
-        act(R("orow", 0, 16), R("jrow", 256, 272), ACT.Silu)
-        ops[-1]["cost"] += 1.3
-    mset(R("d1", 0, 1024, 16), -64.0)
-    mset(R("d1", 15, 1024, 16), 7.6875)
+    tt(R("tgtb"), R("oneb"), R("tleb"), ALU.subtract)
+    for j in range(2):
+        shift(R("jrow", 256 * j, 256 * j + 256), R("irow"), BASE + 256 * j, "s")
+    act(R("orow", 256, 512), R("arow"), ACT.Identity, 0.0, 0.0)
+    act(R("orow", 0, 16), R("jrow", 256, 272), ACT.Silu)
+    ops[-1]["cost"] += 1.3
+    for k in range(16):
+        act(R("ea", 128 * k, 128 * k + 128), R("idh"), ACT.Identity, 0.0, R("wa", k, k + 1))
+    mset(R("d1", 0, 512, 16), -64.0)
+    mset(R("d1", 15, 512, 16), 7.6875)
     mset(R("off"), -2048.0 / W)
     ts(R("kc"), R("brow"), -15.5, ALU.add, 1.0 / 256, ALU.mult)
     mset(R("lift"), 1536.0)
-    mset(R("bd"), 1.0)
-    for j, (c0, c1) in enumerate(PARTS):
+    for j, (c0, c1) in enumerate(PARTS + LAST_PARTS):
         ts(col(10 + j), ca, 16.0 * (c1 - c0), ALU.mult, 15.0, ALU.add)
-        ts(R("lmx", c0, c1), R("irow", 0, 16 * (c1 - c0), 16), col(10 + j), ALU.add)
+        ts(R("lmx", 16 * (j // 2) + c0, 16 * (j // 2) + c1), R("irow", 0, 16 * (c1 - c0), 16), col(10 + j), ALU.add)
     for o in ops:
         o["lead"] = 20.0
     half = piece // 2
@@ -418,7 +431,8 @@ def rank_program(g, core, T, topo):
     iota(R("wq", 1280, 1536), [[1, 256]], 0, 0)
     copy(R("qf", 256, 257, 1, 8), R("qi", 256, 257, 1, 8))
     mm(R("pd", 32, 33), R("e8", 0, 128, 1, 8), R("qf", 256, 257, 1, 8), True, True)
-    ts(R("nx", 0, 1), R("pd", 32, 33), 256.0, ALU.add)
+    copy(R("nx", 0, 1), R("pd", 32, 33))
+    ts(R("nxr"), R("brow", 0, 16), R("nx", 0, 1), ALU.add, 255.0 - BIG, ALU.add)
     for j in range(SHIP):
         xr, hi, z = R("xr", half * j, half * j + half), R("hi", half * j, half * j + half), R(("db", "da")[j % 2], 0, half)
         add("v", lambda e, xr=xr, hi=hi: e.tensor_scalar(A(hi), A(xr), -1.0 / 16, 15.0 / 32 - 192, ALU.mult, ALU.add), [hi], [xr],
@@ -430,11 +444,14 @@ def rank_program(g, core, T, topo):
 
     RP = R("rp", LOW, LOW + 4096)
 
+    def parts(t):
+        return LAST_PARTS if t == NR else PARTS
+
     def ou(t):
         return R("ou", 16 * (t % 2), 16 * (t % 2) + 16)
 
     def pn(b, t=2):
-        return R(("pb", "pa", "pb", "pa")[b] if t > 1 else ("pb", "pa", "zb", "za")[b], 64 * b, 64 * b + 64)
+        return R(("pb", "pa", "pb", "pa")[b] if t > 1 else FIRST_BANKS[b], 64 * b, 64 * b + 64)
 
     def names(t, b):
         for q, lo, hi in NAMES if t > 1 else FIRST_NAMES:
@@ -447,12 +464,8 @@ def rank_program(g, core, T, topo):
     def keep(t, dst, b, q, at=0):
         copy(R(dst, at + 64 * b, at + 64 * b + 64), pn(b, t), q)
 
-    def home(t):
-        return 1536 * (t % 2)
-
-    def moved(name, t):
-        lo = 256 * ((t - 1) % 2)
-        return ind(R(name, lo, lo + 1536), ou(t))
+    def src(t):
+        return R("sr", 16 * (t % 2), 16 * (t % 2) + 16)
 
     def first_rows(t):
         return R("selr" if t % 2 else "sel")
@@ -460,28 +473,32 @@ def rank_program(g, core, T, topo):
     def ones(t):
         return R("oner" if t % 2 else "onew")
 
-    def from_stored(t):
-        mm(R("ph", 0, 272), first_rows(t), R("s16"), True, False)
-        mm(R("ph", 0, 272), R("idw"), R("dgm"), False, True)
-        mm(R("pd", 256, 512), first_rows(t), R("s16", 0, 256), True, False)
-        mm(R("pd", 256, 512), R("onew"), R("dgm", 0, 256), False, True)
-        scan(R("hh"), R("nd"), R("ph", 0, 272), 0.0, ALU.mult, ALU.min)
-        for h in (1, 0):
-            tt(R("ne", 128 * h, 128 * h + 128), R("hh", 128 * h + 15, 128 * h + 143), R("pd", 128 * h + 256, 128 * h + 384), ALU.not_equal)
-        for p in range(7, -1, -1):
-            ts(R("nec", 16 * p, 16 * p + 16), R("pd", 256 + 32 * p, 272 + 32 * p), R("hh", 32 * p + 31, 32 * p + 32), ALU.not_equal)
-        ts(R("n0"), R("hh", 15, 256, 16), 2 * W + 2048.0, ALU.add)
-        for h in (1, 0):
-            ts(R("hv", 128 * h, 128 * h + 128), ind(RP, R("n0", 8 * h, 8 * h + 8)), ROUND, ALU.add, ROUND, ALU.subtract)
-        for c0, c1 in PARTS:
+    def twins(t, lo, hi):
+        mm(R("ph", lo, hi + 15), first_rows(t), R("s16", lo, hi + 15), True, False)
+        mm(R("ph", lo, hi + 15), R("idw"), R("dgm", lo, hi + 15), False, True)
+        mm(R("pd", 256 + lo, 256 + hi), first_rows(t), R("s16", lo, hi), True, False)
+        mm(R("pd", 256 + lo, 256 + hi), R("onew"), R("dgm", lo, hi), False, True)
+        scan(R("hh", lo, hi + 15), R("nd", lo, hi + 15), R("ph", lo, hi + 15), 0.0, ALU.mult, ALU.min)
+        n = min(128, hi - lo)
+        for h in range(hi - n, lo - 1, -n):
+            tt(R("ne", h, h + n), R("hh", h + 15, h + n + 15), R("pd", h + 256, h + n + 256), ALU.not_equal)
+        for p in range(hi // 32 - 1, lo // 32 - 1, -1):
+            o, i, c = R("nec", 16 * p, 16 * p + 16), R("pd", 256 + 32 * p, 272 + 32 * p), R("hh", 32 * p + 31, 32 * p + 32)
+            if MOVES["nec"][p] == "v":
+                ts(o, i, c, ALU.not_equal)
+            else:
+                act(o, i, ACT.Abs, c, -1.0)
+        ts(R("n0", lo // 16, hi // 16), R("hh", lo + 15, hi, 16), 2 * W + 2048.0, ALU.add)
+        ts(R("hv", lo, hi), ind(RP, R("n0", lo // 16, hi // 16)), ROUND, ALU.add, ROUND, ALU.subtract)
+
+    def look_list(t):
+        for c0, c1 in parts(t):
             for a in range(16):
                 m = 256 + 16 * c0 + (c1 - c0) * a
                 mm(R("da", m, m + c1 - c0), R("rot" if t % 2 else "idh"), R("s16", 16 * c0 + a, 16 * c1, 16), True, True)
         shift(R("su"), R("da", 256, 512), 2048.0, MOVES["su"], True)
 
-    def locks(t, j):
-        lo, hi = SEGS[j]
-        z = "zb" if j % 2 else "za"
+    def locks(t, lo, hi, z):
         pairs = range(hi // 32 - 1, lo // 32 - 1, -1)
 
         def both(l, name, last):
@@ -501,47 +518,51 @@ def rank_program(g, core, T, topo):
                 tt(R("df", x0, x1), R("s16", x0, x1), R(pn(b)[0], x0, x1), ALU.not_equal)
             both(ones(t), "df", True)
         scan(R("m1", 2 * lo, 2 * hi), R("rs2", 2 * lo, 2 * hi), R(z, 2 * lo, 2 * hi), -1.0e6, ALU.max, ALU.min)
-        ts(R("lo", lo // 16 + 1, hi // 16, 2), R("m1", 2 * lo + 63, 2 * hi, 64), 4096.0 - SPARE + LOW, ALU.add, col(6), ALU.max)
-        ts(R("lo", lo // 16, hi // 16, 2), R("m1", 2 * lo + 31, 2 * hi, 64), 4096.0 - SPARE + LOW, ALU.add, ca, ALU.max)
+        copy(R("lo", lo // 16, hi // 16), R("m1", 2 * lo + 31, 2 * hi, 32), "s" if hi <= MOVES["lo"] else "v")
         for p in pairs:
             tt(ind(R("rp"), R("lo", 2 * p, 2 * p + 2)), R("hv", 32 * p, 32 * p + 32),
                R("ec", 256 * (t - 1) + 32 * p, 256 * (t - 1) + 32 * p + 32), ALU.add)
 
     def kinds(t):
+        m = R("m1", 31, 512, 32)
+        tt(R("bd", 15, 256, 16), m, R("rs2", 0, 512, 32), ALU.subtract)
+        shift(R("ml"), m, -4096.0 - LOW, MOVES["ml"])
+        shift(R("lf"), m, -1.0 * LOW, MOVES["ml"])
         if t > 1:
             mm(R("db", 256, 512), R("idw"), R("dgm", 0, 256), True, False)
             mm(R("db", 256, 512), ones(t), R("df"), False, True)
             for h in (0, 128):
                 scan(R("m4", h, h + 128), R("rs", h, h + 128), R("db", h + 256, h + 384), -1.0e6, ALU.max, ALU.min)
-            tt(R("ff", 17, 33), R("m4", 15, 256, 16), R("old"), ALU.is_ge)
-            ts(R("kth"), R("ff", 17, 33), -1.0e6, ALU.mult)
-        tt(R("bd", 15, 256, 16), R("m1", 31, 512, 32), R("rs", 0, 256, 16), ALU.subtract)
-        ts(R("ml"), R("m1", 31, 512, 32), -SPARE, ALU.add)
-        ts(R("lf"), R("m1", 31, 512, 32), 4096.0 - SPARE, ALU.add)
-        tt(R("mk"), R("ml"), R("kth"), ALU.add)
-
-    def part(name, j):
-        return R(name, 16 * PARTS[j][0], 16 * PARTS[j][1])
+            ts(R("ff", 1, 17) if t < NR else R("gs"), R("m4", 15, 256, 16), SPARE, ALU.is_lt)
+            ts(R("ff", 17, 33), R("hh", 15, 256, 16), -2049.0 - 2 * W, ALU.is_lt)
+            ts(R("gr"), R("m4", 15, 256, 16), SPARE, ALU.is_ge)
+            tt(R("ff", 33, 49), R("gr"), R("ff", 17, 33), ALU.subtract)
 
     def slot(name, t, j):
-        at = SLOT * (t - 1) + sum(16 + 16 * (c1 - c0) for c0, c1 in PARTS[:j])
-        n = PARTS[j][1] - PARTS[j][0]
+        at = SLOT * (t - 1) + sum(16 + 16 * (c1 - c0) for c0, c1 in parts(t)[:j])
+        n = parts(t)[j][1] - parts(t)[j][0]
         return R(name, at, at + n), R(name, at + n, at + 17 * n), R(name, at, at + 17 * n)
 
     def look(t, j):
-        c0, c1 = PARTS[j]
+        c0, c1 = parts(t)[j]
         n = c1 - c0
+        last = t == NR
+
+        def part(name, j):
+            return R(name, 16 * c0, 16 * c1)
+
         zd = R("db" if j % 2 else "da", 0, 16 * n)
         lst, dig, whole = slot("sb", t, j)
         mm(zd, R("idh"), part("kc", j), True, False)
         mm(zd, R("idh"), part("lift", j), False, False)
-        for q, a0, a1 in LOOKS[j]:
+        for q, a0, a1 in (LAST_LOOKS if last else LOOKS)[j]:
             lo, hi = 16 * c0 + n * a0, 16 * c0 + n * a1
             shift(R("g2", 16 * lo, 16 * hi), ind(RP, R("su", lo, hi)), -7.5 - BASE - TAG * (t - 1) / 256, q)
         for a in range(16):
             m = 16 * (16 * c0 + n * a)
             mm(zd, R("ea", 128 * a, 128 * a + 128), R("g2", m, m + 16 * n), False, a == 15)
-        for a0, a1 in zip(MAXIMA[j], MAXIMA[j][1:]):
+        cuts = (LAST_MAXIMA if last else MAXIMA)[j]
+        for a0, a1 in zip(cuts, cuts[1:]):
             lo, hi = 16 * (16 * c0 + n * a0), 16 * (16 * c0 + n * a1)
             scan(R("mx", lo, hi), R("g2", lo, hi), R("d1", 0, hi - lo), 0.0, ALU.max, ALU.add)
         copy(part("r16", j), zd, MOVES["r16"])
@@ -549,11 +570,9 @@ def rank_program(g, core, T, topo):
         scan(part("yy", j), part("wt", j), part("bd", j), 0.0, ALU.max, ALU.mult)
         y = R("yy", 16 * c0 + 15, 16 * c1, 16)
         tt(lst, R("lf", c0, c1), y, ALU.subtract)
-        tt(R("ff", 33 + c0, 33 + c1), y, R("ml", c0, c1), ALU.is_gt)
-        tt(R("ff", 1 + c0, 1 + c1), y, R("mk", c0, c1), ALU.is_le)
-        tt(part("si", j), ind(R("mx", 256 * c0, 256 * c1), R("lmx", c0, c1)), part("hv", j), ALU.add)
+        tt(part("si", j), ind(R("mx", 256 * c0, 256 * c1), R("lmx", 16 * last + c0, 16 * last + c1)), part("hv", j), ALU.add)
         ts(part("sj", j), part("si", j), 15, ALU.bitwise_and)
-        copy(dig, part("sj", j))
+        copy(dig, part("sj", j), MOVES["dig"][j])
         send(nxt, slot("rb", t, j)[2], whole, "ro%d_%d" % (t, j), "sent", HOP)
         ops[-1]["lead"] = EARLY[j]
 
@@ -563,69 +582,102 @@ def rank_program(g, core, T, topo):
 
     def write_copy(t, j):
         lst, dig, whole = slot("sb", t, j)
-        shift(part("n32", j), dig, BASE, MOVES["nd"])
-        copy(ind(R("rp", LOW, LOW + 4096 + 256), lst), part("n32", j), MOVES["copy"])
+        n32 = R("n32", 16 * PARTS[j][0], 16 * PARTS[j][1])
+        shift(n32, dig, BASE, MOVES["nd"])
+        copy(ind(R("rp", LOW, LOW + 4096 + 256), lst), n32, MOVES["copy"])
 
     def order(t):
-        scan(R("uu", 0, 49), R("ff", 0, 49), R("ff", 0, 49), 0.0, ALU.add, ALU.max)
-        mm(R("ph", 0, 48), R("tle"), R("uu", 1, 49), True, False)
-        mm(R("ph", 0, 48), R("tgt"), R("uu", 0, 48), False, True)
-        mm(R("ph", 64, 65), R("oneb") if t % 2 else R("one1"), R("uu", 32, 33), True, True)
-        if t % 2 == 0:
-            mm(R("ph", 72, 73), R("onef"), R("uu", 32, 33), True, True)
-        mm(R("pd", 0, 16), R("r256") if t % 2 else R("i256"), R("ff", 33, 49), True, False)
-        tt(R("tt"), R("ff", 1, 49), R("ph", 0, 48), ALU.mult)
-        for j in range(3):
-            mm(R("pd", 0, 16), R("rotb") if t % 2 else R("idn"), R("tt", 16 * j, 16 * j + 16), False, j == 2)
-        ts(R("c1", 0, 1), R("ph", 64, 65), -1.0, ALU.mult, R("nx", 0, 1), ALU.add)
-        shift(R("orow", 0, 256), R("jrow", 256 * (t % 2), 256 * (t % 2) + 256), R("c1", 0, 1), MOVES["fill"])
+        n = 64 if t == NR else 48
+        if t == NR:
+            tt(R("ff", 49, 65), R("yy", 15, 256, 16), R("ml"), ALU.is_gt)
+            tt(R("ff", 1, 17), R("gs"), R("ff", 49, 65), ALU.subtract)
+        scan(R("uu", 0, n + 1), R("ff", 0, n + 1), R("ff", 0, n + 1), 0.0, ALU.add, ALU.max)
+        mm(R("ph", 0, n), R("tle"), R("uu", 1, n + 1), True, False)
+        mm(R("ph", 0, n), R("tgt"), R("uu", 0, n), False, True)
+        if t == NR:
+            mm(R("ph", 72, 73), R("oneb") if t % 2 else R("one1"), R("uu", 48, 49), True, True)
+            mm(R("pd", 0, 16), R("r256"), R("ff", 49, 65), True, False)
+        tt(R("tt", 0, n), R("ff", 1, n + 1), R("ph", 0, n), ALU.mult)
+        for j in range(n // 16):
+            mm(R("pd", 0, 16), R("rotb") if t % 2 else R("idn"), R("tt", 16 * j, 16 * j + 16), j == 0 and t < NR, j == n // 16 - 1)
+        if t == NR:
+            ts(R("c1", 0, 1), R("ph", 72, 73), -1.0, ALU.mult, R("nx", 0, 1), ALU.add)
+            shift(R("orow", 0, 256), R("jrow", 256, 512), R("c1", 0, 1), "s")
         ts(R("du"), R("pd", 0, 16), -1.0, ALU.add)
-        copy(ind(R("orow"), R("du")), R("jrow", 512 - 256 * (t % 2), 768 - 256 * (t % 2)), MOVES["orow"])
+        copy(ind(R("orow"), R("du")), R("jrow", 0, 256), MOVES["orow"])
         for h in (1, 0):
             scan(R("mo", 128 * h, 128 * h + 128), R("orow", 128 * h, 128 * h + 128), R("ko", 0, 128), -1.0, ALU.max, ALU.add)
-            ts(R("ou", 16 * (t % 2) + 8 * h, 16 * (t % 2) + 8 * h + 8), R("mo", 128 * h + 15, 128 * h + 128, 16), col(4), ALU.add)
-        if t < NR:
-            ts(R("old"), R("iw"), R("ph", 72 if t % 2 == 0 else 64, 73 if t % 2 == 0 else 65), ALU.is_lt, SPARE, ALU.mult)
-            ts(R("cw", 0, 1), R("c1", 0, 1), 1024.0, ALU.is_ge, -1024.0, ALU.mult)
-            ts(R("nx", 0, 1), R("c1", 0, 1), R("cw", 0, 1), ALU.add, 256.0, ALU.add)
+        ts(ou(t), R("mo", 15, 256, 16), col(4), ALU.add)
 
-    def carry(name, t):
-        copy(R(name, home(t), home(t) + 256), moved(name, t), MOVES[name])
+    def refill(t):
+        odd = t % 2
+        tt(R("gg", 1, 17), R("yy", 15, 256, 16), R("ml"), ALU.is_gt)
+        scan(R("gu", 0, 17), R("gg", 0, 17), R("gg", 0, 17), 0.0, ALU.add, ALU.max)
+        mm(R("za", 0, 16), R("idh"), R("nxr"), True, False)
+        mm(R("za", 0, 16), R("rbig" if odd else "ibig"), R("gg", 1, 17), False, False)
+        mm(R("za", 0, 16), R("tleb" if odd else "tle"), R("gu", 1, 17), False, False)
+        mm(R("za", 0, 16), R("tgtb" if odd else "tgt"), R("gu", 0, 16), False, True)
+        mm(R("za", 16, 17), R("oneb" if odd else "one1"), R("gu", 16, 17), True, True)
+        tt(src(t), R("iw"), R("za", 0, 16), ALU.max)
+        ts(R("c1", 0, 1), R("za", 16, 17), R("nx", 0, 1), ALU.add)
+        ts(R("cw", 0, 1), R("c1", 0, 1), 1024.0, ALU.is_ge, -1024.0, ALU.mult)
+        ts(R("nx", 0, 1), R("c1", 0, 1), R("cw", 0, 1), ALU.add)
+        ts(R("nxr"), R("brow", 0, 16), R("nx", 0, 1), ALU.add, 255.0 - BIG, ALU.add)
+
+    def carry(t):
+        for name, tmp, out in (("wx", "tx", R("at")), ("ws", "tn", R("s16", 0, 256)), ("wq", "tq", R("wq", 0, 256))):
+            if t == 1:
+                copy(out if name != "wq" else R(tmp), ind(R(name), src(t)), MOVES[tmp])
+                if name == "wq":
+                    copy(out, R(tmp), "s")
+            else:
+                copy(R(tmp), ind(R(name), src(t)), MOVES[tmp])
+                copy(out, ind(R(tmp), ou(t)), MOVES[out[0]])
+        copy(R("wx", 0, 256), R("at"), MOVES["wx"])
 
     for t in range(1, NR + 1):
+        now[0] = t
+        act(R("ec", 256 * (t - 1), 256 * t), R("eb"), ACT.Identity, (16.0 + TAG * (t - 1)) / 256, -1.0 / 256)
         if t == 1:
-            for b in range(3, -1, -1):
-                names(t, b)
-                keep(t, "s16", b, "vs"[b % 2])
+            for j, (lo, hi) in enumerate(FIRST_SEGS):
+                for b in range(hi // 64 - 1, lo // 64 - 1, -1):
+                    names(t, b)
+                    keep(t, "s16", b, FIRST_KEEP[b])
+                twins(t, lo, hi)
+                for x in range(hi - FIRST_STEP, lo - 1, -FIRST_STEP):
+                    locks(t, x, x + FIRST_STEP, ("za", "zb")[x // FIRST_STEP % 2])
             copy(R("ws", 0, 256), R("s16", 0, 256), "s")
-        from_stored(t)
-        done = 4
-        for j in range(len(SEGS)):
-            while t > 1 and 64 * done > SEGS[j][0]:
-                done -= 1
-                names(t, done)
-            locks(t, j)
+            look_list(t)
+        else:
+            twins(t, 0, 256)
+            look_list(t)
+            done = 4
+            for j, (lo, hi) in enumerate(SEGS):
+                while 64 * done > lo:
+                    done -= 1
+                    names(t, done)
+                locks(t, lo, hi, ("za", "zb")[j % 2])
         kinds(t)
         for b in range(3, -1, -1) if t > 1 else ():
-            keep(t, "ws", b, MOVES["keep"], home(t - 1))
+            keep(t, "ws", b, MOVES["keep"])
+        if 1 < t < NR:
+            order(t)
         for j in range(len(PARTS)):
             look(t, j)
-        order(t)
         for j in range(len(PARTS)):
             write(t, j)
         if t == NR:
-            ts(R("s32"), moved("ws", t), 2048.0, ALU.add, -1.0, ALU.max)
-            store("y", T.yd[:], T.s32[:, 0:256], R("s32"), "dyd", 2.5)
             store("y", T.yx[:], T.xs[:, 0:4096], R("xs", 0, 4096), "dyx", 7.0)
+            order(t)
+            ts(R("s32"), ind(R("ws"), ou(t)), 2048.0, ALU.add, -1.0, ALU.max)
+            store("s", T.yd[:], T.s32[:, 0:256], R("s32"), "dyd", 2.5)
+            copy(R("tq"), ind(R("wq"), ou(t)), "s")
+            store("s", T.yq[:], T.tq[0:128:16, 0:256], R("tq"), "dyq", 2.0)
         else:
+            refill(t)
             for j in range(len(PARTS)):
                 write_copy(t, j)
-            for lo, hi in AT_CUTS:
-                copy(R("at", lo, hi), ind(moved("wx", t)[1], R("ou", 16 * (t % 2) + lo // 16, 16 * (t % 2) + hi // 16)), MOVES["at"])
-            copy(R("s16", 0, 256), moved("ws", t), MOVES["s16"])
-            carry("wx", t)
-        carry("wq", t)
-    store("s", T.yq[:], T.wq[0:128:16, home(NR):home(NR) + 256], R("wq", home(NR), home(NR) + 256), "dyq", 2.0)
+            carry(t)
 
     if "order" not in PLAN:
         PLAN["order"] = plan(ops)
@@ -691,6 +743,6 @@ def rank_program(g, core, T, topo):
             o["count"] = count[o["q"]]
             ins.then_inc(T.sem[ESEM[o["q"]]], 1)
     g.wait_ge(T.sem["sent"], NR * len(PARTS) * neng + SHIP * nback)
-    g.sync.wait_ge(T.sem["dyd"], 16)
+    g.scalar.wait_ge(T.sem["dyd"], 16)
     g.sync.wait_ge(T.sem["dyx"], 16)
     g.scalar.wait_ge(T.sem["dyq"], 16)

from concourse.mybir import AluOpType as ALU, ActivationFunctionType as ACT

W = 16384.0
NR = 7
LOW = 32
TAG = 17
BASE = 64.0
ROUND = 12582912.0
SPARE = 2048.0 - 2 * W
SLOT = 320
SHIP = 8
SEGS = [(192, 256), (128, 192), (64, 128), (32, 64), (0, 32)]
FIRST_SEGS = [(128, 256), (0, 128)]
FIRST_STEP = 64
FIRST_KEEP = "ssss"
FIRST_BANKS = ("pb", "pa", "pb", "pa")
PARTS = [(0, 10), (10, 16)]
NAMES = [("s", 224, 256), ("v", 192, 224), ("s", 160, 192), ("v", 128, 160), ("s", 80, 128), ("v", 64, 80),
         ("s", 16, 64), ("v", 0, 16)]
FIRST_NAMES = [("sv"[j % 2], 32 * j, 32 * j + 32) for j in range(8)]
LOOKS = [[("s", 0, 4), ("v", 4, 8), ("s", 8, 12), ("v", 12, 16)],
         [("s", 0, 6), ("s", 6, 12), ("s", 12, 16)]]
MAXIMA = [[0, 3, 4, 7, 8, 11, 12, 15, 16], [0, 5, 6, 11, 12, 16]]
LAST_PARTS, LAST_LOOKS, LAST_MAXIMA = list(PARTS), list(LOOKS), list(MAXIMA)
BIG = 1536.0
MOVES = {"tx": "s", "tn": "v", "tq": "s", "at": "s", "s16": "s", "wx": "s", "wq": "s", "keep": "s", "su": "s", "r16": "s", "copy": "s", "orow": "s", "nd": "s",
         "fill": "s", "nec": "ssvvvvvv", "dig": "vv", "lo": 128, "ml": "s"}
CYC, WAKE, HOP, PE = 0.83e-3, 0.19, 1.5, 0.42e-3
GATHER, SCATTER = 1.56, 3.8
LEADS = {"s s16 0": 5.5, "v hh 0": 3.5, "v xs/rb 176": 2.5, "g sb 0": 4.0, "v rp/lo 6": 1.25, "v df 192": 3.0, "v g1 2048": 0.75,
         "v n0 0": 2.75, "v si 160": 4.25}
SHIP_LAT = 2.5
IDX_AFTER = 7
EARLY = [3.0, 0.0]

SCRATCH = {
    "xs": ("sbuf", [128, 4096 + 256], "bfloat16"), "xr": ("sbuf", [128, 2048], "bfloat16"),
    "pk": ("sbuf", [128, 2048], "bfloat16"), "hi": ("sbuf", [128, 2048], "bfloat16"), "id16": ("sbuf", [128, 128], "bfloat16"),
    "r256": ("sbuf", [128, 128], "bfloat16"), "i256": ("sbuf", [128, 128], "bfloat16"),
    "rp": ("sbuf", [128, LOW + 4096 + 256], "float32"),
    "qi": ("sbuf", [128, 272], "int32"),
    "qf": ("sbuf", [128, 272], "float32"),
    "wx": ("sbuf", [128, 1536], "int32"), "wq": ("sbuf", [128, 1536], "float32"), "ws": ("sbuf", [128, 1536], "float32"),
    "tx": ("sbuf", [128, 256], "int32"), "tq": ("sbuf", [128, 256], "float32"), "tn": ("sbuf", [128, 256], "float32"),
    "sr": ("sbuf", [128, 32], "uint16"), "nxr": ("sbuf", [128, 16], "float16"),
    "gg": ("sbuf", [128, 32], "bfloat16"), "gu": ("sbuf", [128, 32], "bfloat16"),
    "gs": ("sbuf", [128, 16], "bfloat16"), "gr": ("sbuf", [128, 16], "bfloat16"),
    "tleb": ("sbuf", [128, 128], "bfloat16"), "tgtb": ("sbuf", [128, 128], "bfloat16"),
    "ibig": ("sbuf", [128, 128], "bfloat16"), "rbig": ("sbuf", [128, 128], "bfloat16"),
    "g1": ("sbuf", [128, 4096], "bfloat16"), "g2": ("sbuf", [128, 4096], "float16"),
    "mx": ("sbuf", [128, 4096], "bfloat16"), "d1": ("sbuf", [128, 512], "float16"),
    "wn": ("sbuf", [128, 2048], "bfloat16"), "ea": ("sbuf", [128, 2048], "float16"),
    "at": ("sbuf", [128, 256], "uint16"), "su": ("sbuf", [128, 256], "uint16"),
    "sb": ("sbuf", [128, NR * SLOT], "uint16"), "rb": ("sbuf", [128, NR * SLOT], "uint16"),
    "s32": ("sbuf", [128, 256], "float32"), "s16": ("sbuf", [128, 272], "float16"),
    "df": ("sbuf", [128, 256], "bfloat16"), "ne": ("sbuf", [128, 256], "bfloat16"), "nec": ("sbuf", [128, 128], "bfloat16"),
    "hh": ("sbuf", [128, 272], "float32"), "hv": ("sbuf", [128, 256], "float32"), "n32": ("sbuf", [128, 256], "float32"),
    "ec": ("sbuf", [128, NR * 256], "float32"),
    "r16": ("sbuf", [128, 256], "float16"), "wt": ("sbuf", [128, 256], "bfloat16"),
    "bd": ("sbuf", [128, 256], "float32"), "yy": ("sbuf", [128, 256], "float32"),
    "si": ("sbuf", [128, 256], "int32"), "sj": ("sbuf", [128, 256], "int32"),
    "m1": ("sbuf", [128, 512], "float32"), "m4": ("sbuf", [128, 256], "float32"),
    "mo": ("sbuf", [128, 256], "float32"), "orow": ("sbuf", [128, 512], "float32"), "sn": ("sbuf", [128, 512], "float32"),
    "lo": ("sbuf", [128, 16], "uint16"), "du": ("sbuf", [128, 16], "uint16"), "ou": ("sbuf", [128, 32], "uint16"),
    "n0": ("sbuf", [128, 16], "uint16"), "lmx": ("sbuf", [128, 32], "uint16"),
    "ff": ("sbuf", [128, 80], "bfloat16"), "uu": ("sbuf", [128, 80], "bfloat16"), "tt": ("sbuf", [128, 64], "bfloat16"),
    "ml": ("sbuf", [128, 16], "float32"), "lf": ("sbuf", [128, 16], "float32"),
    "c1": ("sbuf", [128, 4], "float32"), "cw": ("sbuf", [128, 4], "float32"), "nx": ("sbuf", [128, 4], "float32"),
    "ci": ("sbuf", [128, 32], "int32"), "cj": ("sbuf", [128, 32], "int32"), "cf": ("sbuf", [128, 32], "float32"),
    "col": ("sbuf", [128, 16], "float32"),
    "wk": ("sbuf", [128, 64], "float32"), "wa": ("sbuf", [128, 16], "float32"),
    "irow": ("sbuf", [128, 256], "bfloat16"), "arow": ("sbuf", [128, 256], "bfloat16"), "brow": ("sbuf", [128, 256], "bfloat16"),
    "jrow": ("sbuf", [128, 768], "float32"), "grow": ("sbuf", [128, 128], "bfloat16"),
    "e8": ("sbuf", [128, 128], "float32"), "ck": ("sbuf", [128, 16], "float32"),
    "one1": ("sbuf", [128, 128], "bfloat16"), "onew": ("sbuf", [128, 128], "bfloat16"), "oner": ("sbuf", [128, 128], "bfloat16"),
    "oneb": ("sbuf", [128, 128], "bfloat16"), "onef": ("sbuf", [128, 128], "bfloat16"), "rotb": ("sbuf", [128, 128], "bfloat16"),
    "idn": ("sbuf", [128, 128], "bfloat16"), "idw": ("sbuf", [128, 128], "bfloat16"),
    "sel": ("sbuf", [128, 128], "float16"), "selr": ("sbuf", [128, 128], "float16"),
    "rot": ("sbuf", [128, 128], "float16"), "idh": ("sbuf", [128, 128], "float16"),
    "tle": ("sbuf", [128, 128], "bfloat16"), "tgt": ("sbuf", [128, 128], "bfloat16"), "tmp": ("sbuf", [128, 128], "bfloat16"),
    "sgn": ("sbuf", [128, 64], "bfloat16"), "sg2": ("sbuf", [128, 256], "bfloat16"),
    "dgm": ("sbuf", [128, 272], "bfloat16"), "nd": ("sbuf", [128, 272], "bfloat16"),
    "ko": ("sbuf", [128, 128], "bfloat16"), "ko1": ("sbuf", [128, 128], "bfloat16"), "ko2": ("sbuf", [128, 128], "bfloat16"),
    "eb": ("sbuf", [128, 256], "bfloat16"), "ge": ("sbuf", [128, 256], "bfloat16"),
    "kc": ("sbuf", [128, 256], "float16"), "lift": ("sbuf", [128, 256], "float16"),
    "rs": ("sbuf", [128, 256], "float32"), "rs2": ("sbuf", [128, 512], "float32"), "off": ("sbuf", [128, 64], "bfloat16"),
    "iw": ("sbuf", [128, 16], "float32"), "iwo": ("sbuf", [128, 16], "float32"),
    "pa": ("psum", [128, 512], "float32"), "pb": ("psum", [128, 512], "float32"),
    "za": ("psum", [128, 512], "float32"), "zb": ("psum", [128, 512], "float32"),
    "da": ("psum", [128, 512], "float32"), "db": ("psum", [128, 512], "float32"),
    "ph": ("psum", [128, 512], "float32"), "pd": ("psum", [128, 512], "float32"),
}
PSUM = [k for k, v in SCRATCH.items() if v[0] == "psum"]
SEMAPHORES = (["ev", "es", "et", "eg", "sent", "dq", "dc", "di", "dw", "dyx", "dyq", "dyd"]
              + ["dx%d" % j for j in range(SHIP)] + ["rx%d" % j for j in range(SHIP)]
              + ["ro%d_%d" % (t, j) for t in range(1, NR + 1) for j in range(len(PARTS))])
ESEM = {"v": "ev", "s": "es", "t": "et", "g": "eg"}
PLAN = {}


def meet(a, b):
    if a[0] != b[0] or a[1] >= b[2] or b[1] >= a[2]:
        return False
    return a[3] != b[3] or a[3] == 1 or (a[1] - b[1]) % a[3] == 0


def banks(o):
    return set(r[0] for r in o["rd"] + o["wr"] if r[0] in PSUM)


def clash(o, p):
    return any(meet(a, b) for a in o["rd"] for b in p["wr"]) or any(meet(a, b) for a in o["wr"] for b in p["wr"] + p["rd"])


def plan(ops):
    n = len(ops)
    pred, anc, byname, bysem, last = [], [], {}, {}, {}
    for i, o in enumerate(ops):
        cand = set()
        for r in o["rd"] + o["wr"]:
            cand.update(byname.get(r[0], []))
        bk, edges = banks(o), {}
        for m in cand:
            p = ops[m]
            if p["dma"] == "remote":
                continue
            both = p["q"] == o["q"]
            if clash(o, p) or (bk & banks(p) and (not both or o["q"] == "t")):
                edges[m] = 0.0 if both and o["q"] == "t" else p["lat"] + WAKE
        for name, val in o["ext"]:
            for m in bysem[name]:
                edges[m] = ops[m]["lat"] + WAKE
        if o["dma"] or o["q"] == "g":
            if o["q"] in last:
                edges.setdefault(last[o["q"]], 0.0)
            last[o["q"]] = i
        keep, seen = {}, 0
        for m in sorted(edges, reverse=True):
            if not seen >> m & 1 or ops[m]["lat"]:
                keep[m] = edges[m]
                seen |= anc[m]
        pred.append(keep)
        anc.append(seen | 1 << i)
        for r in o["rd"] + o["wr"]:
            byname.setdefault(r[0], []).append(i)
        for name in o["sems"]:
            bysem.setdefault(name, []).append(i)
    succ = [{} for o in ops]
    for i in range(n):
        for m, d in pred[i].items():
            succ[m][i] = d
    cost = [o["cost"] for o in ops]

    def place(turn, before, first):
        busy = {q: [] for q in "vstgy"}
        start = [0.0] * n
        for i in turn:
            at = max([start[m] + cost[m] + d for m, d in before[i].items()] + [first[i]])
            b = busy[ops[i]["q"]]
            lo, hi = 0, len(b)
            while lo < hi:
                mid = (lo + hi) // 2
                lo, hi = (mid + 1, hi) if b[mid][1] <= at else (lo, mid)
            while lo < len(b) and b[lo][0] < at + cost[i] - 1e-9:
                at = b[lo][1]
                lo += 1
            start[i] = at
            b.insert(lo, (at, at + cost[i]))
        return start

    tail = [o["lat"] if not succ[i] else 0.0 for i, o in enumerate(ops)]
    way = [0.0] * n
    for i in range(n - 1, -1, -1):
        way[i] = cost[i] + max([d + way[j] for j, d in succ[i].items()] + [tail[i]])
    start = place(sorted(range(n), key=lambda i: (-way[i], i)), pred, [0.0] * n)
    back = place(sorted(range(n), key=lambda i: (-start[i] - cost[i], -i)), succ, tail)
    for i in range(n - 1, -1, -1):
        way[i] = max([back[i] + cost[i] + ops[i]["lead"] + LEADS.get(ops[i]["tag"], 0.0)] + [1e-6 + way[j] for j in succ[i]])
    start = place(sorted(range(n), key=lambda i: (-way[i], i)), pred, [0.0] * n)
    return sorted(range(n), key=lambda i: (start[i], i))


def rank_program(g, core, T, topo):
    rank = T.rank_of(core)
    if rank is None:
        return
    nxt = T.cores[(rank + 1) % len(T.cores)]
    prv = T.cores[(rank - 1) % len(T.cores)]
    neng = len(topo.engines(core, nxt))
    nback = len(topo.engines(core, prv))
    nin = len(topo.engines(prv, core))
    ncopy = len(topo.engines(nxt, core))
    Q = {"v": g.vector, "s": g.scalar, "t": g.tensor, "g": g, "y": g.sync}
    ops = []

    def R(name, lo=None, hi=None, step=1, parts=128):
        if lo is None:
            lo, hi = 0, SCRATCH[name][1][1]
        return (name, lo, hi, step, parts)

    def A(r):
        if not isinstance(r, tuple):
            return r
        if len(r) == 3:
            return A(r[1]).indirect(A(r[2]))
        name, lo, hi, step, parts = r
        if step == 1:
            return T[name][0:parts, lo:hi]
        return T[name][0:parts, lo:hi:step]

    def ind(win, off):
        return ("ind", win, off)

    def cols(r):
        return 16 * cols(r[2]) if len(r) == 3 else len(range(r[1], r[2], r[3]))

    def narrow(*rs):
        return all(SCRATCH[r[0]][2] in ("bfloat16", "float16", "uint16") for r in rs)

    def price(o, i, per=None):
        if len(o) == 3:
            return 0.05 + CYC * SCATTER * cols(o)
        if len(i) == 3:
            return 0.06 + CYC * GATHER * cols(o)
        return CYC * max(64, cols(o) * (per or (0.5 if narrow(o, i) else 1)))

    now = [0]

    def tag(q, r):
        name, lo = (r[1][0] + "/" + r[2][0], r[2][1]) if len(r) == 3 else r[:2]
        lo %= {"sb": SLOT, "rb": SLOT, "ou": 16, "sr": 16, "ec": 256}.get(name[-2:], 4096)
        return "%s%s %s %d" % ("" if now[0] > 1 else now[0], q, name, lo)

    def add(q, fn, outs, ins, cost, dma=None, ext=None, lat=0.0, sems=()):
        rd, wr = [], []
        for r in ins:
            if isinstance(r, tuple):
                rd += [r[1], r[2]] if len(r) == 3 else [r]
        for r in outs:
            if isinstance(r, tuple):
                if len(r) == 3:
                    wr.append(r[1]); rd.append(r[2])
                else:
                    wr.append(r)
        ops.append({"q": q, "fn": fn, "rd": rd, "wr": wr, "dma": dma, "ext": ext or [], "cost": cost, "lat": lat, "sems": sems,
                    "lead": 0.0, "tag": tag(q, outs[0] if outs else ins[0])})

    def copy(o, i, q="v", ext=None):
        if q == "v":
            add(q, lambda e: e.tensor_copy(A(o), A(i)), [o], [i], price(o, i), ext=ext)
        elif len(o) == 3:
            add(q, lambda e: e.activation(A(o), A(i), ACT.Silu), [o], [i], price(o, i), ext=ext)
        else:
            add(q, lambda e: e.activation(A(o), A(i), ACT.Copy), [o], [i], price(o, i, 1), ext=ext)

    def shift(o, i, c, q, floor=False, ext=None):
        if q == "v":
            add(q, lambda e: e.tensor_scalar(A(o), A(i), A(c), None, ALU.add), [o], [i, c], price(o, i), ext=ext)
        else:
            add(q, lambda e: e.activation(A(o), A(i), ACT.Relu if floor else ACT.Identity, bias=A(c), scale=1.0), [o], [i, c],
                price(o, i, 1), ext=ext)

    def ts(o, i, s1, op0, s2=None, op1=None):
        if op1 is None:
            add("v", lambda e: e.tensor_scalar(A(o), A(i), A(s1), None, op0), [o], [i, s1], price(o, i))
        else:
            add("v", lambda e: e.tensor_scalar(A(o), A(i), A(s1), A(s2), op0, op1), [o], [i, s1, s2], price(o, i))

    def tt(o, a, b, op):
        add("v", lambda e: e.tensor_tensor(A(o), A(a), A(b), op), [o], [a, b], price(o, a, 1 if b[0] in PSUM else 2))

    def scan(o, d0, d1, init, op0, op1):
        add("v", lambda e: e.tensor_tensor_scan(A(o), A(d0), A(d1), init, op0, op1), [o], [d0, d1],
            price(o, d0, 0.5 if narrow(o, d0, d1) else 1))

    def act(o, i, func, bias=0.0, scale=1.0):
        add("s", lambda e: e.activation(A(o), A(i), func, bias=A(bias), scale=A(scale)), [o], [i, bias, scale], price(o, i, 1))

    def mset(o, c):
        add("v", lambda e: e.memset(A(o), c), [o], [], price(o, o))

    def mm(o, l, r, start, stop):
        add("t", lambda e: e.matmul(A(o), A(l), A(r), start, stop), [o], [l, r], PE * max(64, cols(r)) * (1 if narrow(r) else 4))

    def iota(o, pat, base, cm):
        cost = 0.13 + 2 * CYC * cols(o)
        if SCRATCH[o[0]][2] == "int32":
            add("g", lambda e: e.iota(A(o), pat, base, cm), [o], [], cost)
        else:
            add("g", lambda e: e.iota(A(o), pat, base, cm, allow_small_or_imprecise_dtypes=True), [o], [], cost)

    def send(to, dst, src, sem, local, lat):
        rid, pid = topo.addr(to)[0], topo.addr(to)[1]
        add("g", lambda e: e.remote_dma(A(dst), A(src), T.sem[sem], T.sem[local], pid, rid, topo.mask(core, to)), [], [src],
            0.5, dma="remote", lat=lat, sems=(sem, local))

    def load(q, dst, src, sem, lat):
        add(q, lambda e: e.dma_start(A(dst), src), [dst], [], 0.1, dma=sem, lat=lat)

    def store(q, dst, src, region, sem, lat):
        add(q, lambda e: e.dma_start(dst, src), [], [region], 0.1, dma=sem, lat=lat)

    def col(j):
        return R("col", j, j + 1)

    piece = 4096 // SHIP
    load("s", R("qi", 0, 256, 1, 8), T.que[:], "dq", 2.0)
    due = 1.7
    for j in range(SHIP):
        due += 5.2 / SHIP
        load("y", R("xs", piece * j, piece * j + piece), T.rec[:, piece * j:piece * j + piece], "dx%d" % j, due)
        if j == IDX_AFTER:
            due += 2.6
            load("y", R("wx", 256, 1280), T.idx[:], "di", due)
    load("y", R("wx", 1280, 1536), T.idx[:, 0:256], "dw", due + 0.7)

    iota(R("ci", 0, 16), [[-1, 16]], 16, 1)
    iota(R("ci", 16, 19), [[16, 3]], 0, 1)
    iota(R("arow"), [[0, 16], [1, 16]], 0, 0)
    iota(R("e8", 0, 128, 1, 8), [[1, 8], [0, 16]], 0, -1)
    iota(R("grow"), [[16, 8], [0, 16]], 0, 0)
    iota(R("irow"), [[1, 256]], 0, 0)
    iota(R("brow"), [[1, 16], [0, 16]], 0, 0)
    mset(R("d1"), 0.0)
    ts(R("ci", 18, 19), R("ci", 18, 19), 80.0, ALU.add)
    ts(R("cj", 0, 17), R("ci", 0, 17), 15, ALU.bitwise_and)
    copy(col(0), R("ci", 16, 17))
    ts(R("cj", 17, 19), R("ci", 17, 19), 127, ALU.bitwise_and)
    ts(R("cj", 19, 22), R("ci", 16, 19), 112, ALU.bitwise_and)
    for r in (R("rs"), R("rs2", 0, 256), R("rs2", 256, 512)):
        act(r, R("arow"), ACT.Identity, -1.0e6, 0.0)
    act(R("bd"), R("arow"), ACT.Identity, 1.0, 0.0)
    copy(R("cf", 0, 22), R("cj", 0, 22))
    mset(R("dgm", 256, 272), 0.0)
    copy(R("s16", 256, 272), R("cf", 0, 16))
    ca, cp, cpr, cpb = R("cf", 16, 17), col(0), R("cf", 17, 18), R("cf", 18, 19)
    cg, cgr, cgb = R("cf", 19, 20), R("cf", 20, 21), R("cf", 21, 22)
    ts(col(9), ca, 0.0, ALU.is_equal, -8192.0, ALU.mult)
    ts(col(5), ca, -1.0, ALU.mult)
    ts(col(6), ca, 16.0, ALU.add)
    ts(R("wk", 0, 16), R("cf", 0, 16), 0.0, ALU.is_equal, 256.0, ALU.mult)
    ts(R("wk", 16, 32), R("cf", 0, 16), 1.0, ALU.is_equal, 16.0, ALU.mult)
    ts(R("wk", 32, 48), R("cf", 0, 16), 2.0, ALU.is_equal)
    ts(R("ko1"), R("arow", 0, 128), ca, ALU.is_equal, 4096.0, ALU.mult)
    ts(R("ko2"), R("arow", 0, 128), ca, ALU.is_lt, -8192.0, ALU.mult)
    tt(R("wk", 48, 64), R("wk", 0, 16), R("wk", 16, 32), ALU.add)
    ts(R("e8", 0, 128, 1, 8), R("e8", 0, 128, 1, 8), 0.0, ALU.is_equal)
    copy(R("qf", 0, 256, 1, 8), R("qi", 0, 256, 1, 8))
    mm(R("da", 0, 256), R("e8", 0, 128, 1, 8), R("qf", 0, 256, 1, 8), True, True)
    tt(R("ko"), R("ko1"), R("ko2"), ALU.add)
    tt(R("wk", 0, 16), R("wk", 48, 64), R("wk", 32, 48), ALU.add)
    ts(R("ck"), R("arow", 0, 16), cg, ALU.add)
    ts(R("wa"), R("arow", 0, 16), ca, ALU.is_equal)
    ts(col(8), col(9), -1.0, ALU.mult, -4096.0, ALU.add)
    ts(col(4), col(8), 0.25 - BASE, ALU.add)
    ts(R("ko", 15, 128, 16), R("ko", 15, 128, 16), col(9), ALU.add)
    act(R("sgn", 0, 16), R("arow", 0, 16), ACT.Sign, col(5), 1.0)
    for k in range(16):
        ts(R("wn", 128 * k, 128 * k + 128), R("irow", 0, 128), R("ck", k, k + 1), ALU.is_equal, R("wk", k, k + 1), ALU.mult)
    mset(R("sg2"), 3.0)
    for h in range(0, 128, 64):
        mset(R("sg2", h + 32, h + 48), (2048.0 + LOW) / W - 0.5)
        act(R("sg2", h + 16, h + 32), R("sgn", 0, 16), ACT.Identity, (2048.0 + LOW) / W, 0.5)
        act(R("sg2", h + 48, h + 64), R("sgn", 0, 16), ACT.Identity, (2048.0 + LOW) / W, 0.5)
    ts(R("dgm", 0, 256), R("arow"), ca, ALU.is_equal, -2.0, ALU.mult)
    for h in (0, 128):
        scan(R("mo", h, h + 128), R("da", h, h + 128), R("ko"), -1.0, ALU.max, ALU.add)
    act(R("nd"), R("dgm"), ACT.Identity, 1.0, 0.5)
    copy(R("wq", 0, 256), R("da", 0, 256), "s")
    ts(R("rot"), R("irow", 0, 128), cpr, ALU.is_equal)
    ts(R("ou", 0, 16), R("mo", 15, 256, 16), col(8), ALU.add)
    ts(R("selr"), R("grow"), cpr, ALU.is_equal)
    ts(R("idw"), R("irow", 0, 128), cp, ALU.is_equal, W, ALU.mult)
    ts(R("onew"), R("grow"), cg, ALU.is_equal, W, ALU.mult)
    ts(R("iw"), R("irow", 0, 256, 16), ca, ALU.add)
    ts(R("ge"), R("arow"), ca, ALU.is_ge)
    ts(R("rs", 0, 256, 16), R("iw"), SPARE, ALU.add)
    ts(R("rs2", 0, 512, 32), R("iw"), 4096.0 + LOW, ALU.add)
    ts(R("rs2", 31, 512, 64), R("arow", 0, 128, 16), ca, ALU.add)
    ts(R("rs2", 63, 512, 64), R("arow", 0, 128, 16), col(6), ALU.add)
    ts(R("idn"), R("irow", 0, 128), cp, ALU.is_equal)
    ts(R("id16"), R("irow", 0, 128), cp, ALU.is_equal, 16.0, ALU.mult)
    ts(R("ibig"), R("irow", 0, 128), cp, ALU.is_equal, BIG, ALU.mult)
    ts(R("rbig"), R("irow", 0, 128), cpb, ALU.is_equal, BIG, ALU.mult)
    ts(R("r256"), R("irow", 0, 128), cpb, ALU.is_equal, 256.0, ALU.mult)
    ts(R("idh"), R("irow", 0, 128), cp, ALU.is_equal)
    tt(R("eb"), R("ge"), R("brow"), ALU.add)
    ts(R("sel"), R("grow"), cp, ALU.is_equal)
    ts(R("rotb"), R("irow", 0, 128), cpb, ALU.is_equal)
    ts(R("one1"), R("grow"), cg, ALU.is_equal)
    ts(R("oner"), R("grow"), cgr, ALU.is_equal, W, ALU.mult)
    ts(R("oneb"), R("grow"), cgb, ALU.is_equal)
    ts(R("tmp"), R("arow", 0, 128), ca, ALU.is_ge)
    tt(R("tle"), R("tmp"), R("one1"), ALU.mult)
    tt(R("tleb"), R("tmp"), R("oneb"), ALU.mult)
    mset(R("ff", 0, 1), 0.0)
    mset(R("gg", 0, 1), 0.0)
    tt(R("tgt"), R("one1"), R("tle"), ALU.subtract)
    tt(R("tgtb"), R("oneb"), R("tleb"), ALU.subtract)
    for j in range(2):
        shift(R("jrow", 256 * j, 256 * j + 256), R("irow"), BASE + 256 * j, "s")
    act(R("orow", 256, 512), R("arow"), ACT.Identity, 0.0, 0.0)
    act(R("orow", 0, 16), R("jrow", 256, 272), ACT.Silu)
    ops[-1]["cost"] += 1.3
    for k in range(16):
        act(R("ea", 128 * k, 128 * k + 128), R("idh"), ACT.Identity, 0.0, R("wa", k, k + 1))
    mset(R("d1", 0, 512, 16), -64.0)
    mset(R("d1", 15, 512, 16), 7.6875)
    mset(R("off"), -2048.0 / W)
    ts(R("kc"), R("brow"), -15.5, ALU.add, 1.0 / 256, ALU.mult)
    mset(R("lift"), 1536.0)
    for j, (c0, c1) in enumerate(PARTS + LAST_PARTS):
        ts(col(10 + j), ca, 16.0 * (c1 - c0), ALU.mult, 15.0, ALU.add)
        ts(R("lmx", 16 * (j // 2) + c0, 16 * (j // 2) + c1), R("irow", 0, 16 * (c1 - c0), 16), col(10 + j), ALU.add)
    for o in ops:
        o["lead"] = 20.0
    half = piece // 2
    for j in range(SHIP):
        z = R(("pa", "pb", "za", "zb")[j % 4], 0, half)
        mm(z, R("id16"), R("xs", piece * j, piece * j + half), True, False)
        mm(z, R("idn"), R("xs", piece * j + half, piece * j + piece), False, True)
        copy(R("pk", half * j, half * j + half), z, "vs"[j % 2])
        send(prv, R("xr", half * j, half * j + half), R("pk", half * j, half * j + half), "rx%d" % j, "sent", HOP + SHIP_LAT)
        ops[-1]["lead"] = 30.0
    add("g", lambda e: e.dma_start(T.qi[0:8, 256:257], T.cur[:], allow_slow_non_contiguous=True), [R("qi", 256, 257)], [],
        1.5, dma="dc", lat=2.0)
    copy(R("at"), ind(R("wx", 256, 1280), R("ou", 0, 16)))
    copy(R("wx", 0, 256), R("at"))
    iota(R("ws", 256, 1536), [[0, 1280]], -2050, 0)
    iota(R("wq", 256, 1280), [[1, 1024]], 0, 0)
    iota(R("wq", 1280, 1536), [[1, 256]], 0, 0)
    copy(R("qf", 256, 257, 1, 8), R("qi", 256, 257, 1, 8))
    mm(R("pd", 32, 33), R("e8", 0, 128, 1, 8), R("qf", 256, 257, 1, 8), True, True)
    copy(R("nx", 0, 1), R("pd", 32, 33))
    ts(R("nxr"), R("brow", 0, 16), R("nx", 0, 1), ALU.add, 255.0 - BIG, ALU.add)
    for j in range(SHIP):
        xr, hi, z = R("xr", half * j, half * j + half), R("hi", half * j, half * j + half), R(("db", "da")[j % 2], 0, half)
        add("v", lambda e, xr=xr, hi=hi: e.tensor_scalar(A(hi), A(xr), -1.0 / 16, 15.0 / 32 - 192, ALU.mult, ALU.add), [hi], [xr],
            price(hi, xr), ext=[("rx%d" % j, ncopy)])
        act(R("rp", LOW + piece * j, LOW + piece * j + half), hi, ACT.Identity, BASE - 192, -1.0)
        mm(z, R("id16"), hi, True, False)
        mm(z, R("idn"), xr, False, True)
        shift(R("rp", LOW + piece * j + half, LOW + piece * j + piece), z, BASE + 16 * 192, "vs"[j % 2])

    RP = R("rp", LOW, LOW + 4096)

    def parts(t):
        return LAST_PARTS if t == NR else PARTS

    def ou(t):
        return R("ou", 16 * (t % 2), 16 * (t % 2) + 16)

    def pn(b, t=2):
        return R(("pb", "pa", "pb", "pa")[b] if t > 1 else FIRST_BANKS[b], 64 * b, 64 * b + 64)

    def names(t, b):
        for q, lo, hi in NAMES if t > 1 else FIRST_NAMES:
            if lo // 64 == b:
                copy(R("g1", 16 * lo, 16 * hi), ind(R("xs", 0, 4096), R("at", lo, hi)), q)
        mm(pn(b, t), R("idw"), R("off"), True, False)
        for k in range(16):
            mm(pn(b, t), R("wn", 128 * k, 128 * k + 128), R("g1", 1024 * b + k, 1024 * b + 1024, 16), False, k == 15)

    def keep(t, dst, b, q, at=0):
        copy(R(dst, at + 64 * b, at + 64 * b + 64), pn(b, t), q)

    def src(t):
        return R("sr", 16 * (t % 2), 16 * (t % 2) + 16)

    def first_rows(t):
        return R("selr" if t % 2 else "sel")

    def ones(t):
        return R("oner" if t % 2 else "onew")

    def twins(t, lo, hi):
        mm(R("ph", lo, hi + 15), first_rows(t), R("s16", lo, hi + 15), True, False)
        mm(R("ph", lo, hi + 15), R("idw"), R("dgm", lo, hi + 15), False, True)
        mm(R("pd", 256 + lo, 256 + hi), first_rows(t), R("s16", lo, hi), True, False)
        mm(R("pd", 256 + lo, 256 + hi), R("onew"), R("dgm", lo, hi), False, True)
        scan(R("hh", lo, hi + 15), R("nd", lo, hi + 15), R("ph", lo, hi + 15), 0.0, ALU.mult, ALU.min)
        n = min(128, hi - lo)
        for h in range(hi - n, lo - 1, -n):
            tt(R("ne", h, h + n), R("hh", h + 15, h + n + 15), R("pd", h + 256, h + n + 256), ALU.not_equal)
        for p in range(hi // 32 - 1, lo // 32 - 1, -1):
            o, i, c = R("nec", 16 * p, 16 * p + 16), R("pd", 256 + 32 * p, 272 + 32 * p), R("hh", 32 * p + 31, 32 * p + 32)
            if MOVES["nec"][p] == "v":
                ts(o, i, c, ALU.not_equal)
            else:
                act(o, i, ACT.Abs, c, -1.0)
        ts(R("n0", lo // 16, hi // 16), R("hh", lo + 15, hi, 16), 2 * W + 2048.0, ALU.add)
        ts(R("hv", lo, hi), ind(RP, R("n0", lo // 16, hi // 16)), ROUND, ALU.add, ROUND, ALU.subtract)

    def look_list(t):
        for c0, c1 in parts(t):
            for a in range(16):
                m = 256 + 16 * c0 + (c1 - c0) * a
                mm(R("da", m, m + c1 - c0), R("rot" if t % 2 else "idh"), R("s16", 16 * c0 + a, 16 * c1, 16), True, True)
        shift(R("su"), R("da", 256, 512), 2048.0, MOVES["su"], True)

    def locks(t, lo, hi, z):
        pairs = range(hi // 32 - 1, lo // 32 - 1, -1)

        def both(l, name, last):
            for p in pairs:
                mm(R(z, 64 * p + 16, 64 * p + 32), l, R(name, 32 * p, 32 * p + 16), False, False)
                mm(R(z, 64 * p + 32, 64 * p + 64), l, R(name, 32 * p, 32 * p + 32), False, last and p == lo // 32)

        mm(R(z, 2 * lo, 2 * hi), R("idw"), R("sg2", 0, 2 * (hi - lo)), True, False)
        for p in pairs:
            mm(R(z, 64 * p + 16, 64 * p + 32), R("idw"), R("ne", 32 * p, 32 * p + 16), False, False)
            mm(R(z, 64 * p + 32, 64 * p + 48), R("idw"), R("nec", 16 * p, 16 * p + 16), False, False)
            mm(R(z, 64 * p + 48, 64 * p + 64), R("idw"), R("ne", 32 * p + 16, 32 * p + 32), False, False)
        both(first_rows(t), "s16", t == 1)
        if t > 1:
            for b in range((hi - 1) // 64, lo // 64 - 1, -1):
                x0, x1 = max(lo, 64 * b), min(hi, 64 * b + 64)
                tt(R("df", x0, x1), R("s16", x0, x1), R(pn(b)[0], x0, x1), ALU.not_equal)
            both(ones(t), "df", True)
        scan(R("m1", 2 * lo, 2 * hi), R("rs2", 2 * lo, 2 * hi), R(z, 2 * lo, 2 * hi), -1.0e6, ALU.max, ALU.min)
        copy(R("lo", lo // 16, hi // 16), R("m1", 2 * lo + 31, 2 * hi, 32), "s" if hi <= MOVES["lo"] else "v")
        for p in pairs:
            tt(ind(R("rp"), R("lo", 2 * p, 2 * p + 2)), R("hv", 32 * p, 32 * p + 32),
               R("ec", 256 * (t - 1) + 32 * p, 256 * (t - 1) + 32 * p + 32), ALU.add)

    def kinds(t):
        m = R("m1", 31, 512, 32)
        tt(R("bd", 15, 256, 16), m, R("rs2", 0, 512, 32), ALU.subtract)
        shift(R("ml"), m, -4096.0 - LOW, MOVES["ml"])
        shift(R("lf"), m, -1.0 * LOW, MOVES["ml"])
        if t > 1:
            mm(R("db", 256, 512), R("idw"), R("dgm", 0, 256), True, False)
            mm(R("db", 256, 512), ones(t), R("df"), False, True)
            for h in (0, 128):
                scan(R("m4", h, h + 128), R("rs", h, h + 128), R("db", h + 256, h + 384), -1.0e6, ALU.max, ALU.min)
            ts(R("ff", 1, 17) if t < NR else R("gs"), R("m4", 15, 256, 16), SPARE, ALU.is_lt)
            ts(R("ff", 17, 33), R("hh", 15, 256, 16), -2049.0 - 2 * W, ALU.is_lt)
            ts(R("gr"), R("m4", 15, 256, 16), SPARE, ALU.is_ge)
            tt(R("ff", 33, 49), R("gr"), R("ff", 17, 33), ALU.subtract)

    def slot(name, t, j):
        at = SLOT * (t - 1) + sum(16 + 16 * (c1 - c0) for c0, c1 in parts(t)[:j])
        n = parts(t)[j][1] - parts(t)[j][0]
        return R(name, at, at + n), R(name, at + n, at + 17 * n), R(name, at, at + 17 * n)

    def look(t, j):
        c0, c1 = parts(t)[j]
        n = c1 - c0
        last = t == NR

        def part(name, j):
            return R(name, 16 * c0, 16 * c1)

        zd = R("db" if j % 2 else "da", 0, 16 * n)
        lst, dig, whole = slot("sb", t, j)
        mm(zd, R("idh"), part("kc", j), True, False)
        mm(zd, R("idh"), part("lift", j), False, False)
        for q, a0, a1 in (LAST_LOOKS if last else LOOKS)[j]:
            lo, hi = 16 * c0 + n * a0, 16 * c0 + n * a1
            shift(R("g2", 16 * lo, 16 * hi), ind(RP, R("su", lo, hi)), -7.5 - BASE - TAG * (t - 1) / 256, q)
        for a in range(16):
            m = 16 * (16 * c0 + n * a)
            mm(zd, R("ea", 128 * a, 128 * a + 128), R("g2", m, m + 16 * n), False, a == 15)
        cuts = (LAST_MAXIMA if last else MAXIMA)[j]
        for a0, a1 in zip(cuts, cuts[1:]):
            lo, hi = 16 * (16 * c0 + n * a0), 16 * (16 * c0 + n * a1)
            scan(R("mx", lo, hi), R("g2", lo, hi), R("d1", 0, hi - lo), 0.0, ALU.max, ALU.add)
        copy(part("r16", j), zd, MOVES["r16"])
        tt(part("wt", j), part("r16", j), zd, ALU.is_gt)
        scan(part("yy", j), part("wt", j), part("bd", j), 0.0, ALU.max, ALU.mult)
        y = R("yy", 16 * c0 + 15, 16 * c1, 16)
        tt(lst, R("lf", c0, c1), y, ALU.subtract)
        tt(part("si", j), ind(R("mx", 256 * c0, 256 * c1), R("lmx", 16 * last + c0, 16 * last + c1)), part("hv", j), ALU.add)
        ts(part("sj", j), part("si", j), 15, ALU.bitwise_and)
        copy(dig, part("sj", j), MOVES["dig"][j])
        send(nxt, slot("rb", t, j)[2], whole, "ro%d_%d" % (t, j), "sent", HOP)
        ops[-1]["lead"] = EARLY[j]

    def write(t, j):
        lst, dig, whole = slot("rb", t, j)
        copy(ind(R("xs"), lst), dig, ext=[("ro%d_%d" % (t, j), nin)])

    def write_copy(t, j):
        lst, dig, whole = slot("sb", t, j)
        n32 = R("n32", 16 * PARTS[j][0], 16 * PARTS[j][1])
        shift(n32, dig, BASE, MOVES["nd"])
        copy(ind(R("rp", LOW, LOW + 4096 + 256), lst), n32, MOVES["copy"])

    def order(t):
        n = 64 if t == NR else 48
        if t == NR:
            tt(R("ff", 49, 65), R("yy", 15, 256, 16), R("ml"), ALU.is_gt)
            tt(R("ff", 1, 17), R("gs"), R("ff", 49, 65), ALU.subtract)
        scan(R("uu", 0, n + 1), R("ff", 0, n + 1), R("ff", 0, n + 1), 0.0, ALU.add, ALU.max)
        mm(R("ph", 0, n), R("tle"), R("uu", 1, n + 1), True, False)
        mm(R("ph", 0, n), R("tgt"), R("uu", 0, n), False, True)
        if t == NR:
            mm(R("ph", 72, 73), R("oneb") if t % 2 else R("one1"), R("uu", 48, 49), True, True)
            mm(R("pd", 0, 16), R("r256"), R("ff", 49, 65), True, False)
        tt(R("tt", 0, n), R("ff", 1, n + 1), R("ph", 0, n), ALU.mult)
        for j in range(n // 16):
            mm(R("pd", 0, 16), R("rotb") if t % 2 else R("idn"), R("tt", 16 * j, 16 * j + 16), j == 0 and t < NR, j == n // 16 - 1)
        if t == NR:
            ts(R("c1", 0, 1), R("ph", 72, 73), -1.0, ALU.mult, R("nx", 0, 1), ALU.add)
            shift(R("orow", 0, 256), R("jrow", 256, 512), R("c1", 0, 1), "s")
        ts(R("du"), R("pd", 0, 16), -1.0, ALU.add)
        copy(ind(R("orow"), R("du")), R("jrow", 0, 256), MOVES["orow"])
        for h in (1, 0):
            scan(R("mo", 128 * h, 128 * h + 128), R("orow", 128 * h, 128 * h + 128), R("ko", 0, 128), -1.0, ALU.max, ALU.add)
        ts(ou(t), R("mo", 15, 256, 16), col(4), ALU.add)

    def refill(t):
        odd = t % 2
        tt(R("gg", 1, 17), R("yy", 15, 256, 16), R("ml"), ALU.is_gt)
        scan(R("gu", 0, 17), R("gg", 0, 17), R("gg", 0, 17), 0.0, ALU.add, ALU.max)
        mm(R("za", 0, 16), R("idh"), R("nxr"), True, False)
        mm(R("za", 0, 16), R("rbig" if odd else "ibig"), R("gg", 1, 17), False, False)
        mm(R("za", 0, 16), R("tleb" if odd else "tle"), R("gu", 1, 17), False, False)
        mm(R("za", 0, 16), R("tgtb" if odd else "tgt"), R("gu", 0, 16), False, True)
        mm(R("za", 16, 17), R("oneb" if odd else "one1"), R("gu", 16, 17), True, True)
        tt(src(t), R("iw"), R("za", 0, 16), ALU.max)
        ts(R("c1", 0, 1), R("za", 16, 17), R("nx", 0, 1), ALU.add)
        ts(R("cw", 0, 1), R("c1", 0, 1), 1024.0, ALU.is_ge, -1024.0, ALU.mult)
        ts(R("nx", 0, 1), R("c1", 0, 1), R("cw", 0, 1), ALU.add)
        ts(R("nxr"), R("brow", 0, 16), R("nx", 0, 1), ALU.add, 255.0 - BIG, ALU.add)

    def carry(t):
        for name, tmp, out in (("wx", "tx", R("at")), ("ws", "tn", R("s16", 0, 256)), ("wq", "tq", R("wq", 0, 256))):
            if t == 1:
                copy(out if name != "wq" else R(tmp), ind(R(name), src(t)), MOVES[tmp])
                if name == "wq":
                    copy(out, R(tmp), "s")
            else:
                copy(R(tmp), ind(R(name), src(t)), MOVES[tmp])
                copy(out, ind(R(tmp), ou(t)), MOVES[out[0]])
        copy(R("wx", 0, 256), R("at"), MOVES["wx"])

    for t in range(1, NR + 1):
        now[0] = t
        act(R("ec", 256 * (t - 1), 256 * t), R("eb"), ACT.Identity, (16.0 + TAG * (t - 1)) / 256, -1.0 / 256)
        if t == 1:
            for j, (lo, hi) in enumerate(FIRST_SEGS):
                for b in range(hi // 64 - 1, lo // 64 - 1, -1):
                    names(t, b)
                    keep(t, "s16", b, FIRST_KEEP[b])
                twins(t, lo, hi)
                for x in range(hi - FIRST_STEP, lo - 1, -FIRST_STEP):
                    locks(t, x, x + FIRST_STEP, ("za", "zb")[x // FIRST_STEP % 2])
            copy(R("ws", 0, 256), R("s16", 0, 256), "s")
            look_list(t)
        else:
            twins(t, 0, 256)
            look_list(t)
            done = 4
            for j, (lo, hi) in enumerate(SEGS):
                while 64 * done > lo:
                    done -= 1
                    names(t, done)
                locks(t, lo, hi, ("za", "zb")[j % 2])
        kinds(t)
        for b in range(3, -1, -1) if t > 1 else ():
            keep(t, "ws", b, MOVES["keep"])
        if 1 < t < NR:
            order(t)
        for j in range(len(PARTS)):
            look(t, j)
        for j in range(len(PARTS)):
            write(t, j)
        if t == NR:
            store("y", T.yx[:], T.xs[:, 0:4096], R("xs", 0, 4096), "dyx", 7.0)
            order(t)
            ts(R("s32"), ind(R("ws"), ou(t)), 2048.0, ALU.add, -1.0, ALU.max)
            store("s", T.yd[:], T.s32[:, 0:256], R("s32"), "dyd", 2.5)
            copy(R("tq"), ind(R("wq"), ou(t)), "s")
            store("s", T.yq[:], T.tq[0:128:16, 0:256], R("tq"), "dyq", 2.0)
        else:
            refill(t)
            for j in range(len(PARTS)):
                write_copy(t, j)
            carry(t)

    if "order" not in PLAN:
        PLAN["order"] = plan(ops)
    ops = [ops[i] for i in PLAN["order"]]

    if "waits" not in PLAN:
        known = {q: {} for q in Q}
        byname, clock, waits = {}, [], []
        for n, o in enumerate(ops):
            q = o["q"]
            cand = set()
            for r in o["rd"] + o["wr"]:
                cand.update(byname.get(r[0], []))
            need = {}
            bk = banks(o)
            for m in cand:
                p = ops[m]
                if p["dma"] == "remote":
                    continue
                if p["q"] == q and p["dma"] is None and o["dma"] is None:
                    hit = q != "t" and clash(o, p)
                else:
                    hit = clash(o, p) or bool(bk & banks(p))
                if hit:
                    key = p["dma"] or p["q"]
                    need[key] = max(need.get(key, -1), m)
            wait, xw = [], []
            for key, m in sorted(need.items(), key=lambda kv: -kv[1]):
                if known[q].get(key, -1) < m:
                    wait.append(m)
                    for k2, v2 in clock[m].items():
                        known[q][k2] = max(known[q].get(k2, -1), v2)
            for name, val in o["ext"]:
                if name not in known[q]:
                    known[q][name] = 0
                    xw.append(name)
            waits.append((wait, xw))
            clock.append(dict(known[q]))
            clock[n][o["dma"] or q] = n
            for r in o["rd"] + o["wr"]:
                byname.setdefault(r[0], []).append(n)
        PLAN["waits"] = waits
    awaited = set(m for wait, xw in PLAN["waits"] for m in wait)
    count = {q: 0 for q in ESEM}
    for n, o in enumerate(ops):
        e = Q[o["q"]]
        for m in PLAN["waits"][n][0]:
            p = ops[m]
            if p["dma"]:
                e.wait_ge(T.sem[p["dma"]], 16)
            else:
                e.wait_ge(T.sem[ESEM[p["q"]]], p["count"])
        for name, val in o["ext"]:
            if name in PLAN["waits"][n][1]:
                e.wait_ge(T.sem[name], val)
        ins = o["fn"](e)
        if o["dma"] == "remote":
            continue
        if o["dma"]:
            ins.then_inc(T.sem[o["dma"]], 16)
        elif n in awaited:
            count[o["q"]] += 1
            o["count"] = count[o["q"]]
            ins.then_inc(T.sem[ESEM[o["q"]]], 1)
    g.wait_ge(T.sem["sent"], NR * len(PARTS) * neng + SHIP * nback)
    g.scalar.wait_ge(T.sem["dyd"], 16)
    g.sync.wait_ge(T.sem["dyx"], 16)
    g.scalar.wait_ge(T.sem["dyq"], 16)
